import numpy as np, ml_dtypes
CORES = [36,164,52,180,100,228,116,244]
N = 8
BF = ml_dtypes.bfloat16
def gentries(a):
    return np.ascontiguousarray(a.reshape(8, 16, -1).transpose(0, 2, 1)).reshape(8, -1)
def gtable(e):
    e = np.asarray(e); return np.ascontiguousarray(e.reshape(8, -1, 16).transpose(0, 2, 1)).reshape(128, -1).astype(np.int32)
V, C, L, R = 1024, 3584, 128, 3
F, MX, TOP = 16 * N, 31248 * N, 2 ** 22 - 1
def parents(rng):
    p = np.zeros((8, V), np.int64); o = rng.permutation(8)
    for g in range(8):
        m = (V >> 4, V >> 3, V >> 2, V >> 1)[int(o[g]) % 4]; pool = rng.permutation(V)[:m]
        p[g] = pool[rng.integers(0, m, V)]; p[g, pool[0]] = pool[0]
    return p
def parts(rng):
    x = rng.integers(-31, 32, (8, F, V)); k = rng.integers(-63, 64, (8, F, C))
    b = np.where(rng.random((8, C)) < 0.2, rng.integers(-MX, MX + 1, (8, C)), rng.integers(-4096, 4097, (8, C)))
    w = np.where(rng.random((8, C)) < 0.25, 1000 * rng.integers(0, 4, (8, C)), rng.integers(0, TOP + 1, (8, C)))
    d = rng.integers(0, C, (8, 16, V)); one = rng.random((8, 1, V)) < 0.15
    return x, k, b, w, np.where(one, d[:, :1], d), parents(rng)
def pack(x, k, b, w, d, p):
    def deal(a): return np.ascontiguousarray(a.reshape(8, N, 16, -1).transpose(1, 0, 2, 3)).reshape(N, 128, -1).astype(np.float32).astype(BF)
    def same(a): return np.stack([np.ascontiguousarray(a).astype(np.int32)] * N)
    return {"xv": deal(x), "kc": deal(k), "bt": same(b), "co": same(w), "cd": same(d.reshape(128, V)), "pa": same(gtable(p))}
def sides(x, k, b, g, c, plus, minus):
    k[g, 0, c] = 63; b[g, c] = 0
    for s, v in ((1, plus), (-1, minus)):
        a = x[g][:, v]; r = np.add.reduce(k[g, 1:, c][:, None] * a[1:], axis=0)
        a = np.where(r * s < 0, -a, a); a[0] = s * np.maximum(np.abs(a[0]), 1); x[g][:, v] = a
def setup_inputs(rng):
    return pack(*parts(rng))
def setup_inputs_corners(rng):
    x, k, b, w, d, p = parts(rng); v = np.arange(V)
    b[:, 0] = MX; b[:, C - 1] = -MX; w[:, 0] = 0; w[:, C - 1] = 0
    u = rng.integers(0, 5, (8, 1, V)); dead = (C - 1) * rng.integers(0, 2, (8, 16, V)); n = np.arange(16)[None, :, None]
    d = np.where(((u == 0) & (n < 15)) | ((u == 1) & (n > 0)) | ((u == 2) & (n >= 0)), dead, d)
    d[:, :, 0] = rng.integers(1, C - 1, (8, 16)); d[:, :, V - 1] = rng.integers(1, C - 1, (8, 16))
    t = L * np.arange(R); edge = np.unique(np.maximum(np.concatenate([t - 1, t, t + L - 1, t + L]), 0))
    shapes = [np.where(rng.random(V) < 0.5, v, p[0]), (v + L) % V, np.maximum(v - 1, 0), np.full(V, V - 1), np.where(v == V - 1, v, 0), edge[rng.integers(0, len(edge), V)], V - 1 - v, (v + 1) % V]
    o = rng.permutation(8); cut = rng.integers(1, C - 1, 8)
    for g, a in zip(o, shapes): p[g] = a
    g, c = int(o[0]), int(cut[0]); m = np.arange(16); i = L * (R - 2) + m; s = V - 17 + m; e = R * L + m
    p[g] = np.where(np.isin(p[g], np.concatenate([i, s, e])), V - 1, p[g])
    p[g, L * (R - 1):L * R] = v[L * (R - 1):L * R]; p[g, i] = s; p[g, s] = e
    sides(x, k, b, g, c, np.concatenate([i, e]), s); d[g, 0, s] = c; w[g, c] = 0
    g, c = int(o[3]), int(cut[3]); sides(x, k, b, g, c, v[:V - 1], v[V - 1:]); d[g, 0, V - 1] = c; w[g, c] = 0
    g, c = int(o[6]), int(cut[6]); i = np.arange(R * L); sides(x, k, b, g, c, i, V - 1 - i); d[g, rng.integers(0, 16, R * L), V - 1 - i] = c
    for r in range(1, R, 2):
        q = L * r + int(rng.integers(0, L)); p[g, q] = q
    g, c = int(o[7]), int(cut[7]); q = L * np.arange(1, R); sides(x, k, b, g, c, np.concatenate([q - 1, q + 1]), q)
    d[g, 0, q] = c; d[g, 0, q - 1] = c; d[g, :, q - 2] = 0; w[g, c] = 0
    return pack(x, k, b, w, d, p)
def setup_inputs_crowd(rng):
    x, k, b, w, d, p = parts(rng); o = rng.permutation(8)
    for n in range(8):
        g = int(o[n]); big = V - 1 - n
        p[g, :R * L] = big; rest = rng.random(V - R * L) < 0.5; p[g, R * L:] = np.where(rest, big, p[g, R * L:])
        if n % 4 == 2: p[g, 1:R * L:2] = V - 10
        if n % 2 == 1:
            for t in range(R): p[g, L * t + (0, L - 1, int(rng.integers(1, L - 1)))[(n // 2 + t) % 3]] = V - 20 - t
        if n < 2: b[g, 0] = MX; d[g, :, big] = 0
        elif n < 4: d[g, :, big] = d[g, 0, big]
    return pack(x, k, b, w, d, p)
def setup_inputs_ends(rng):
    x, k, b, w, d, p = parts(rng); h = 2 * rng.integers(0, 2, (8, F, 1)) - 1; h0 = h[:, :, 0]
    def signs(n):
        u = rng.integers(0, 3, (8, 1, n)); z = 2 * rng.integers(0, 2, (8, F, n)) - 1
        return np.where(u == 0, h, np.where(u == 1, -h, z))
    a, q = signs(V), signs(C); q[:, :, C - 1] = h0; q[:, :, 0] = -h0
    q[:, :, [C - 3, C - 2]] = h; q[:, :, [1, 2]] = -h
    a[:, :, V - 1] = h0 * (1 - 2 * (np.arange(8)[:, None] & 1)); a[:, :, 0] = -a[:, :, V - 1]
    b = np.where(rng.random((8, C)) < 0.7, MX * (2 * rng.integers(0, 2, (8, C)) - 1), rng.integers(-6000, 6001, (8, C))); b[:, 0] = -MX; b[:, C - 1] = -MX
    b[:, 1] = -MX; b[:, 2] = 1 - MX; b[:, C - 3] = MX - 32; b[:, C - 2] = MX - 1
    share = np.where(np.arange(8) % 2 == 1, 0.92, 0.5)[:, None]; w = np.where(rng.random((8, C)) < share, TOP, 0)
    w = np.where(rng.random((8, C)) < 0.15, np.abs(w - rng.integers(0, 4, (8, C))), w); w[1::2, 0] = TOP; w[::2, 0] = 0; w[:, C - 1] = TOP
    d = np.where(rng.random(d.shape) < 0.7, (C - 1) * rng.integers(0, 2, d.shape), d)
    p = np.where(rng.random(p.shape) < 0.68, (V - 1) * rng.integers(0, 2, p.shape), p)
    p = np.where((p >= V - 1 - 4 * R) & (p < V - 1), V - 1, p)
    for t in range(R):
        i, s = L * t + L - 1, V - 2 - t; p[:, i] = s; a[:, :, i] = h0; a[:, :, s] = -h0
    x = 31 * a
    for t in range(R):
        for n, c in enumerate(([C - 2], [1, 2], [1, 2, C - 3, C - 2])):
            i, s, f = L * t + L - 2 - n, V - 2 - R - 3 * t - n, int(rng.integers(0, F)); p[:, i] = s
            x[:, :, i] = 31 * h0; x[:, f, i] = 30 * h0[:, f]; x[:, :, s] = 31 * h0
            d[:, :, s] = np.array(c)[rng.integers(0, len(c), (8, 16))]
    return pack(x, 63 * q, b, w, d, p)
def setup_inputs_spread(rng):
    x, k, b, w, d, p = parts(rng)
    x = np.rint(x * np.exp2(-rng.integers(0, 5, (8, 1, V)).astype(np.float64))) * (rng.random((8, 1, V)) > 0.0625)
    k = np.rint(k * np.exp2(-rng.integers(0, 6, (8, 1, C)).astype(np.float64)))
    b = np.clip((np.exp2(17 * rng.random((8, C)))).astype(np.int64) * (2 * rng.integers(0, 2, (8, C)) - 1), -MX, MX)
    w = np.exp2(22 * rng.random((8, C))).astype(np.int64) - 1
    d = np.minimum((C * rng.random(d.shape) ** 2).astype(np.int64), C - 1)
    for g in range(8): p[g] = rng.permutation(V)[np.minimum((V * rng.random(V) ** 3).astype(np.int64), V - 1)]
    return pack(x, k, b, w, d, p)
def setup_inputs_ties(rng):
    x, k, b, w, d, p = parts(rng); i = np.arange(R * L)
    x[::2] = rng.integers(-1, 2, (4, F, V)); k[::2] = rng.integers(-1, 2, (4, F, C)); b[::2] = rng.integers(-3, 4, (4, C))
    w = np.array([0, 1, TOP - 1, TOP])[rng.integers(0, 4, (8, C))]; w[1::4] = TOP - rng.integers(0, 2, (2, C)); w[2::4] = TOP - rng.integers(0, 2, (2, C))
    for g in (1, 3, 5, 7):
        s = p[g, i]; c = d[g][:, s]; own = np.where(rng.random(c.shape) < 0.5, i[None, :], s[None, :])
        z = np.einsum("fkl,fkl->kl", k[g][:, c], x[g][:, own])
        b[g, c] = np.clip(z + rng.integers(-1, 2, c.shape), -MX, MX)
    return pack(x, k, b, w, d, p)
def check_inputs(d):
    bad = []
    for k, lo, hi in (("xv", -31, 31), ("kc", -63, 63), ("bt", -MX, MX), ("co", 0, TOP), ("cd", 0, C - 1), ("pa", 0, V - 1)):
        a = np.asarray(d[k]).astype(np.float64)
        if not (np.min(a) >= lo and np.max(a) <= hi): bad.append("range of " + k)
        if k in ("xv", "kc") and not np.all(a == np.floor(a)): bad.append("whole numbers in " + k)
        if k not in ("xv", "kc") and not np.all(a == a[:1]): bad.append(k + " alike on all ranks")
    return bad
def reference(xv, kc, bt, co, cd, pa):
    x = np.ascontiguousarray(xv.astype(np.float32).reshape(N, 8, 16, V).transpose(1, 0, 2, 3)).reshape(8, F, V)
    k = np.ascontiguousarray(kc.astype(np.float32).reshape(N, 8, 16, C).transpose(1, 0, 2, 3)).reshape(8, F, C)
    b = bt[0].astype(np.int64); w = co[0].astype(np.int64); d = cd[0].astype(np.int64).reshape(8, 16, V); p = gentries(pa[0]).astype(np.int64)
    yc = np.full((8, R * L), -1, np.int64)
    for rnd in range(R):
        lane = np.arange(L * rnd, L * rnd + L); new = np.array(p)
        for g in range(8):
            s = p[g, lane]; c = d[g][:, s]; kp = k[g][:, c]
            si = np.einsum("fkl,fl->kl", kp, x[g][:, lane]) > b[g][c]; ss = np.einsum("fkl,fl->kl", kp, x[g][:, s]) > b[g][c]
            apart = si != ss
            first = np.zeros(L, bool); first[np.unique(s, return_index=True)[1]] = True
            act = first & ((s < lane[0]) | (s > lane[-1])) & np.any(apart, axis=0)
            best = np.argmin(np.where(apart, w[g][c], 2 ** 24), axis=0)
            a = np.nonzero(act)[0]; i = lane[a]; sa = s[a]; ca = c[best[a], a]; side = si[best[a], a]
            yc[g, i] = w[g][ca]
            who = np.full(V, -1, np.int64); who[sa] = np.arange(len(a))
            u = who[p[g]]; j = np.nonzero(u >= 0)[0]; u = u[j]; cj = ca[u]
            sj = np.einsum("fj,fj->j", k[g][:, cj], x[g][:, j]) > b[g][cj]
            m = (sj == side[u]) & (j != i[u]); new[g, j[m]] = i[u[m]]
            up = p[g, sa]; o = (np.einsum("fj,fj->j", k[g][:, ca], x[g][:, up]) > b[g][ca]) == side
            new[g, i[o]] = up[o]; new[g, sa[o]] = i[o]
        p = new
    return {"yp": np.stack([gtable(p)] * N).astype(np.float32), "yc": np.stack([gtable(yc)] * N).astype(np.float32)}

@@ -1,0 +1,681 @@
+from concourse.bass import DstId, RemoteDMATransfer
+from concourse.mybir import AluOpType, AxisListType, ActivationFunctionType
+
+NV, NC, NL, NR = 1024, 3584, 128, 3
+BLK = 32
+OFF = 32768.0
+BIG = 4096.0
+F32, BF, F16, I32, U16 = "float32", "bfloat16", "float16", "int32", "uint16"
+
+_S = {
+    "xs_": (NV, BF), "kcs": (NC, BF), "cds": (NV, I32), "pas": (64, I32), "tb": (NC, I32),
+    "pl0": (64, U16), "pl1": (64, U16), "pl2": (64, U16),
+    "ci": (16, I32), "cf": (16, F32), "cg": (16, F32), "iv": (NV, F32), "rb": (256, F32), "rg": (128, F32), "r8": (64, F32),
+    "lf": (64, F32), "lst": (80, U16),
+    "m1": (128, F32), "r1": (8, F32), "mr2": (128, F32), "pm": (128, F32), "mi": (256, F32), "r2": (8, F32), "bi": (8, F16),
+    "bd": (128, F32), "rep": (128, F32), "tri": (256, BF), "idb": (128, BF), "rs": (256, F32), "bigu": (128, BF), "mq": (16, F32),
+    "ma": (128, F32), "m3": (64, F32), "jt": (8, F32), "dump": (8, F32), "z9": (80, F16), "z2": (40, F32), "zi": (72, F32),
+    "zo": (48, F32),
+    "so": (24, U16), "sl": (24, F32), "cut": (128, U16), "xg": (128, BF), "xm": (2048, BF), "kg": (2048, BF),
+    "ev": (16 * BLK, F32), "sb1": (3 * 256, U16), "ld1": (3 * 256, U16), "f1": (256, F32), "x1": (128, F32), "y1": (64, F32),
+    "sd": (32, F32), "mq2": (64, F32), "v32": (32, F32), "t32": (32, F32), "ld2": (80, F32),
+    "cs": (256, F32), "ec": (256, F32), "goff": (16, U16), "cq": (16, F32), "gg": (256, F32), "tw": (32, F32),
+    "rw": (256, F32), "wo": (256, F32), "less": (256, F32), "scan": (256, F32), "sc": (16, F32), "si": (8, I32),
+    "pnl": (32, U16), "pc2": (16, F32), "e2": (128, F32), "bq": (16, F32), "q1": (64, F32), "qq": (64, F32),
+    "oh": (128, F32), "oht": (128, F32), "smi": (128, I32), "smj": (128, I32), "yh": (8, F32), "yh2": (16, F32), "up": (16, F32),
+    "gm": (128, F32), "li": (16, I32), "cl": (8, U16), "tg": (32, F32), "tgt": (8, U16), "kcc": (128, BF), "kt": (1152, BF),
+    "xpn": (256, BF), "pf": (256, F16), "sb3": (32, U16), "ld3": (256, U16), "f3": (128, F32), "x3": (64, F32), "y3": (32, F32),
+    "w3": (96, F32), "gm2": (128, F32), "gm3": (128, F32), "gv": (128, F32), "mr3": (128, F32), "wv": (128, F32), "src": (128, F32),
+    "it": (1152, F32), "ian": (128, F32), "pn": (128, F32), "ei": (64, F32), "pc": (8, F32), "vi": (32, I32), "sdf": (48, F32),
+    "el": (64, F32), "yw": (16, F32), "gy": (128, F32), "ycs": (24, F32),
+    "xp": (NV, BF), "xps": (128, BF), "pr": (1152, F16), "sb9": (3 * 72, U16), "ld9": (3 * 72, U16), "f9": (72, F32),
+    "ia": (NV, F32), "eo": (40, F32), "vo": (32, I32), "sdo": (48, F32), "x9": (64, F32), "w9": (96, F32), "po": (8, F32),
+    "g64": (64, F32), "pu": (128, U16), "pw": (64, F32),
+}
+PLACE = {}
+_n = 0
+for _k, (_w, _d) in _S.items():
+    if _d == F32 and _w <= 96 and _k not in ("ld2", "ycs"):
+        PLACE[_k] = _n
+        _n += (_w + 15) // 16 * 16
+SCRATCH = {k: ("sbuf", [128, n], d) for k, (n, d) in _S.items() if k not in PLACE}
+SCRATCH["small"] = ("sbuf", [128, _n], F32)
+BANKS = ["pa0", "pa1", "pb", "pc_", "pd", "pe", "pf_", "pg"]
+for _b in BANKS:
+    SCRATCH[_b] = ("psum", [128, 512], F32)
+SCRATCH["dp1"] = ("dram", [8, 128, 8], U16)
+SCRATCH["dp2"] = ("dram", [8, 128, 8], U16)
+SCRATCH["dp3"] = ("dram", [8, 128, 8], F32)
+SEMAPHORES = ["V", "S", "P", "G", "sent"] + ["d%d" % i for i in range(24)] + ["a%d" % i for i in range(20)]
+
+HOP = 4.0
+HOPD = 2.5
+DMAT = 2.0
+BIAS = 3.0
+
+
+def rank_program(g, core, T, topo):
+    me = T.rank_of(core)
+    if me is None:
+        return
+    n = len(T.cores)
+    A, AX, AF = AluOpType, AxisListType.X, ActivationFunctionType
+    sgn = 1.0 if me % 2 == 0 else -1.0
+    ops = []
+    hist = {}
+    after = {}
+
+    def last(eng):
+        return max(k for k in range(len(ops)) if ops[k]["eng"] == eng)
+
+    def b(name, c0=0, c1=None, step=1, p0=0, p1=128):
+        if c1 is None:
+            c1 = _S[name][0]
+        if name in PLACE:
+            return ("small", c0 + PLACE[name], c1 + PLACE[name], step, p0, p1)
+        return (name, c0, c1, step, p0, p1)
+
+    def ind(win, off):
+        return ("#", win, off)
+
+    def ap(x):
+        if x[0] == "#":
+            return ap(x[1]).indirect(ap(x[2]))
+        if x[3] == 1:
+            return T[x[0]][x[4]:x[5], x[1]:x[2]]
+        return T[x[0]][x[4]:x[5], x[1]:x[2]:x[3]]
+
+    def val(x):
+        return ap(x) if isinstance(x, tuple) else x
+
+    def width(x):
+        if x[0] == "#":
+            return 16 * (x[2][2] - x[2][1])
+        return (x[2] - x[1] + x[3] - 1) // x[3]
+
+    def add(eng, fn, reads, writes, cost, lat=0.07, kind="c", extra=None):
+        k = len(ops)
+        deps = {}
+        rl, wl = [], []
+        for x in reads:
+            if isinstance(x, tuple):
+                if x[0] == "#":
+                    rl += [x[1], x[2]]
+                else:
+                    rl.append(x)
+        for x in writes:
+            if x[0] == "#":
+                wl.append(x[1])
+                rl.append(x[2])
+            else:
+                wl.append(x)
+        for x, wr in [(x, False) for x in rl] + [(x, True) for x in wl]:
+            h = hist.setdefault(x[0], [])
+            for (j, c0, c1, w2) in h:
+                if j == k:
+                    continue
+                if x[0] in BANKS:
+                    if ops[j]["eng"] != eng or eng == "P" or ((wr or w2) and c0 < x[2] and x[1] < c1):
+                        deps[j] = True
+                elif (wr or w2) and c0 < x[2] and x[1] < c1:
+                    deps[j] = True
+            h.append((k, x[1], x[2], wr))
+        if extra is not None:
+            deps[extra] = True
+        ops.append({"eng": eng, "fn": fn, "deps": sorted(deps), "cost": cost, "lat": lat, "kind": kind, "tag": writes[0][:2] if writes else "",
+                    "ord": [after[eng]] if eng in after else []})
+        return k
+
+    def vcost(out, ins, two=False):
+        m = width(out)
+        c = 2.0 if two else 1.0
+        if out[0] == "#":
+            c = 3.0
+        for x in ins:
+            if isinstance(x, tuple) and x[0] == "#":
+                c = max(c, 1.6)
+        return 0.06 + max(m * c - 40, 0) * 0.001
+
+    def cp(out, x):
+        add("V", lambda: g.vector.tensor_copy(ap(out), ap(x)), [x], [out], vcost(out, [x]))
+
+    def tt(out, x, y, op):
+        two = x[0] not in BANKS and y[0] not in BANKS
+        add("V", lambda: g.vector.tensor_tensor(ap(out), ap(x), ap(y), op), [x, y], [out], vcost(out, [x], two))
+
+    def ts(out, x, s1, op0, s2=None, op1=None):
+        if op1 is None:
+            fn = lambda: g.vector.tensor_scalar(ap(out), ap(x), val(s1), None, op0)
+        else:
+            fn = lambda: g.vector.tensor_scalar(ap(out), ap(x), val(s1), val(s2), op0, op1)
+        add("V", fn, [x, s1, s2], [out], vcost(out, [x]))
+
+    def red(out, x, op, ab=False):
+        if ab:
+            fn = lambda: g.vector.tensor_reduce(ap(out), ap(x), AX, op, apply_absolute_value=True)
+        else:
+            fn = lambda: g.vector.tensor_reduce(ap(out), ap(x), AX, op)
+        add("V", fn, [x], [out], vcost(x, []))
+
+    def fill(out, c):
+        add("V", lambda: g.vector.memset(ap(out), c), [], [out], vcost(out, []) * (0.5 if SCRATCH[out[0]][2] == BF else 1.0))
+
+    def act(out, x, scale=None):
+        if scale is None:
+            fn = lambda: g.scalar.activation(ap(out), ap(x), AF.Copy)
+        else:
+            fn = lambda: g.scalar.activation(ap(out), ap(x), AF.Copy, scale=scale)
+        add("S", fn, [x], [out], vcost(out, [x]) + 0.02)
+
+    def mm(items):
+        def fn():
+            r = None
+            for (o, l, rr, st, sp) in items:
+                r = g.tensor.matmul(ap(o), ap(l), ap(rr), st, sp)
+            return r
+        cost = 0.03
+        for (o, l, rr, st, sp) in items:
+            cost += max(min(64, width(l)), width(rr)) * (4 if SCRATCH[l[0]][2] == F32 else 1) * 0.0006
+        add("P", fn, [x for it in items for x in it[1:3]], [it[0] for it in items], cost)
+
+    def iota(out, pat, base, cm):
+        if SCRATCH[out[0]][2] == I32:
+            fn = lambda: g.iota(ap(out), pat, base, cm)
+        else:
+            fn = lambda: g.iota(ap(out), pat, base, cm, allow_small_or_imprecise_dtypes=True)
+        add("G", fn, [], [out], 0.13 + width(out) * 0.002)
+
+    nd = [0]
+
+    def dma(eng, pairs, reads, writes, lat=DMAT):
+        sem = T.sem["d%d" % nd[0]]
+        nd[0] += 1
+        q = g.sync if eng == "Y" else g.scalar
+
+        def fn():
+            for (o, i) in pairs:
+                q.dma_start(o, i).then_inc(sem, 16)
+        k = add(eng, fn, reads, writes, 0.1 * len(pairs), lat, "d")
+        ops[k]["sem"] = (sem, 16 * len(pairs))
+
+    peers = [(me + i) % n for i in range(1, n)]
+    engs = topo.engines(core, T.cores[peers[0]])
+    for r in peers:
+        engs = [e for e in engs if e in topo.engines(core, T.cores[r])]
+    full = 0
+    for e in engs:
+        full += 1 << e
+    dst = {}
+    for r in peers:
+        rid, pid = topo.addr(T.cores[r], core)
+        dst[r] = DstId(rid=rid, pnc=pid)
+    na = [0]
+    sent = [0]
+
+    def hop(srcs, dsts, reads, lands, spread, lat):
+        sem = T.sem["a%d" % na[0]]
+        na[0] += 1
+        if spread:
+            tr = [RemoteDMATransfer(dst_ids=[dst[r]], dma_engine_mask=1 << engs[i], remote_sem=sem, src=srcs(r), dst=dsts)
+                  for i, r in enumerate(peers)]
+            cnt = n - 1
+            sent[0] += n - 1
+        else:
+            tr = [RemoteDMATransfer(dst_ids=[dst[r] for r in peers], dma_engine_mask=full, remote_sem=sem, srcs=[srcs],
+                                    dsts=[dsts for r in peers])]
+            cnt = (n - 1) * len(engs)
+            sent[0] += len(engs)
+        k = add("G", lambda: g.remote_dma_fused(tr, local_sem=T.sem.sent), reads, [], 0.8, 0.0, "r")
+        k2 = add("X", None, [], lands, 0.0, lat, "a", extra=k)
+        ops[k2]["sem"] = (sem, cnt)
+
+    def others(name, base, w):
+        return [b(name, base + r * w, base + (r + 1) * w) for r in peers]
+
+    def gather_sum(f, land, base, w, own, thr, x, y):
+        o = b(f, me * w, (me + 1) * w)
+        cp(o, own)
+        for (c0, c1, th) in thr:
+            oo = b(f, me * w + c0, me * w + c1)
+            tt(oo, oo, th, A.subtract if me % 2 == 0 else A.add)
+        return o
+
+    def finish_sum(f, land, base, w, x, y, out):
+        if me > 0:
+            cp(b(f, 0, me * w), b(land, base, base + me * w))
+        if me < n - 1:
+            cp(b(f, (me + 1) * w, n * w), b(land, base + (me + 1) * w, base + n * w))
+        tt(b(x[0], x[1], x[1] + 4 * w), b(f, 0, 4 * w), b(f, 4 * w, 8 * w), A.add)
+        tt(b(y[0], y[1], y[1] + 2 * w), b(x[0], x[1], x[1] + 2 * w), b(x[0], x[1] + 2 * w, x[1] + 4 * w), A.add)
+        tt(out, b(y[0], y[1], y[1] + w), b(y[0], y[1] + w, y[1] + 2 * w), A.is_gt)
+
+    dma("Y", [(T.pas[:, :], T.pa[:, :])], [], [b("pas")])
+    after["Y"] = last("Y")
+    dma("Y", [(T.cds[:, :], T.cd[:, :])], [], [b("cds")], 3.2)
+    after["Y"] = last("Y")
+    dma("S", [(T["xs_"][:, :], T.xv[:, :])], [], [b("xs_")], 3.2)
+    dma("Y", [(T.kcs[:, :], T.kc[:, :])], [], [b("kcs")], 5.8)
+    fill(b("tb"), 0)
+    dma("Y", [(T.tb[0:128:16, :], T.bt[:, :]), (T.tb[1:128:16, :], T.co[:, :])], [], [b("tb")], 3.5)
+    dma("Y", [(T.tb[16 * h + 4:16 * h + 6, :], T.tb[16 * me:16 * me + 2, :]) for h in range(8)], [b("tb")], [b("tb")], 2.5)
+
+    def col(i):
+        return b("cf", i, i + 1)
+
+    def cg(i):
+        return b("cg", i, i + 1)
+    iota(b("ci", 0, 1), [[0, 1]], 0, 1)
+    p_ = b("ci", 0, 1)
+    ts(b("ci", 1, 2), p_, 15, A.bitwise_and)
+    ts(b("ci", 2, 3), p_, 4, A.arith_shift_right)
+    ts(b("ci", 3, 4), p_, 7, A.bitwise_and)
+    ts(b("ci", 4, 5), p_, 3, A.arith_shift_right)
+    ts(b("ci", 5, 6), p_, 4, A.arith_shift_right, 1, A.bitwise_and)
+    ts(b("ci", 6, 7), p_, 4, A.arith_shift_right, BLK // 16 - 1, A.bitwise_and)
+    ts(b("ci", 7, 8), p_, 3, A.arith_shift_right, 1, A.bitwise_and)
+    ts(b("ci", 8, 9), p_, 1, A.bitwise_and)
+    ts(b("ci", 9, 10), p_, 1, A.arith_shift_right, 7, A.bitwise_and)
+    cp(b("cf", 0, 10), b("ci", 0, 10))
+    cP, cB, cG, cP7, cP3, cA2, cAn, cB3, cB0, cB1 = [col(i) for i in range(10)]
+    ts(cg(0), cB, 8.0, A.mult, cG, A.add)
+    ts(cg(1), cB0, 8.0, A.mult, cG, A.add)
+    ts(cg(2), cB, 16.0, A.mult, cG, A.add)
+    ts(cg(3), cAn, 16.0, A.mult)
+    ts(cg(4), cB, float(BLK), A.mult, cg(3), A.add)
+    ts(cg(5), cP, float(-16 * me), A.add)
+    ts(cg(6), cA2, -1.0, A.mult, 1.0, A.add)
+    ts(cg(7), cP, 0.0, A.is_equal)
+    ts(cg(8), cG, 9.0, A.mult, 8.0, A.add)
+    ts(cg(9), cG, 2.0, A.mult, -63.0, A.add)
+    ts(cg(10), cB, 16.0, A.mult, cg(9), A.add)
+    ts(cg(11), cg(2), 8.0, A.add)
+    ts(cg(12), cg(5), 9.0, A.mult, 8.0, A.add)
+    iota(b("iv", 0, 128), [[1, 128]], 0, 0)
+    iota(b("iv", 128, NV), [[1, NV - 128]], 128, 0)
+    iota(b("rb"), [[0, 16], [1, 16]], 0, 0)
+    iota(b("rg"), [[1, 8], [0, 16]], 0, 0)
+    iota(b("r8"), [[0, 8], [1, 8]], 0, 0)
+    iota(b("lf", 0, 8), [[256, 8]], 0, 0)
+    iota(b("lf", 16, 32), [[1, 8], [8, 2]], 0, 0)
+    iota(b("lf", 32, 36), [[2, 4]], 0, 0)
+    iota(b("lf", 40, 48), [[16, 8]], NV, 0)
+    iota(b("jt"), [[128, 8]], 0, 1)
+    xoA, xoB, sel = b("lst", 0, 8), b("lst", 8, 16), b("lst", 16, 32)
+    gl, gl2, l1, l2, ly, lq = b("lst", 32, 40), b("lst", 40, 48), b("lst", 48, 49), b("lst", 50, 51), b("lst", 52, 56), b("goff")
+    lq = b("pu", 112, 128)
+    ts(xoA, b("lf", 0, 8), cg(2), A.add)
+    ts(xoB, b("lf", 0, 8), cg(11), A.add)
+    ts(sel, b("lf", 16, 32), cg(4), A.add)
+    cp(gl, b("iv", 0, 8))
+    cp(gl2, b("iv", 0, 8))
+    fill(b("lst", 40 + me, 41 + me), 8)
+    gl4, gl5, l5 = b("lst", 56, 64), b("lst", 64, 72), b("lst", 72, 73)
+    ts(gl4, b("iv", 0, 8), 2.0, A.mult)
+    fill(b("lst", 56 + me, 57 + me), 16)
+    ts(gl5, gl4, 1.0, A.add)
+    ts(cg(13), cP7, float(me), A.is_equal, float(16 - 2 * me), A.mult)
+    ts(cg(14), cP7, 2.0, A.mult, 1.0, A.add)
+    ts(l5, cg(14), cg(13), A.add)
+    cp(l1, cP)
+    cp(l2, cg(0))
+    ts(ly, b("lf", 32, 36), cB3, A.add)
+    cp(lq, b("iv", 16, 32))
+    ts(b("dump"), b("lf", 40, 48), cB, A.add)
+    i128, rb128 = b("iv", 0, 128), b("rb", 0, 128)
+    ts(b("m1"), rb128, cg(1), A.is_equal)
+    ts(b("r1"), b("iv", 0, 8), cB1, A.is_equal)
+    ts(b("mr2"), rb128, 2.0, A.is_equal)
+    ts(b("pm"), i128, cg(0), A.is_equal)
+    ts(b("mi"), b("rb"), cB, A.is_equal)
+    ts(b("r2"), b("iv", 0, 8), cG, A.is_equal)
+    ts(b("bi"), b("iv", 0, 8), cG, A.is_equal)
+    ts(b("bd"), b("rg"), cG, A.is_equal)
+    ts(b("rep"), rb128, cg(5), A.is_equal)
+    ts(b("tri"), b("rb"), cB, A.is_lt, -0.5, A.mult)
+    ts(b("idb"), i128, cP, A.is_equal)
+    ts(b("mr3"), rb128, 3.0, A.is_equal, cg(7), A.mult)
+    for t in range(NR - 1):
+        ts(b("pnl", 16 * t + 8, 16 * t + 16), b("dump"), float(NL * (t + 1) - NV), A.add)
+    cp(b("pnl", 0, 8), b("pas", 8, 16))
+    ts(b("rs"), b("rb"), 0.5, A.is_gt)
+    ts(b("bigu"), i128, cP, A.is_ge, BIG, A.mult)
+    ts(b("mq"), b("iv", 0, 16), cP3, A.is_equal)
+    ts(b("ma"), b("rg"), cP7, A.is_equal)
+    ts(b("m3"), b("r8"), cG, A.is_equal)
+    ts(b("z9"), b("iv", 0, 80), cg(8), A.is_equal)
+    ts(b("z2", 0, 33), b("iv", 0, 33), cg(10), A.is_equal)
+    ts(b("zi"), b("iv", 0, 72), cg(11), A.is_equal)
+    ts(b("zo", 0, 44), b("iv", 0, 44), cg(12), A.is_equal)
+    m2, mb = b("mi", 0, 128), b("mi", 0, 16)
+    for h in range(2):
+        act(b("xm", NV * h, NV * h + NV), b("iv"), 0.0)
+    fill(b("ld2"), 0.0)
+    cp(b("so", 0, 8), b("pas", 0, 8))
+    cp(b("sl", 0, 8), b("pas", 0, 8))
+    cp(b("pl0"), b("pas"))
+    xv, kc = b("xs_"), b("kcs")
+    act(b("ia"), ind(b("iv"), b("pl0")))
+    mm([(b("pg", 0, 9), b("ia", 128 * y, 128 * y + 128), b("zo", 8 - y, 17 - y), y == 0, y == 7) for y in range(8)])
+    act(b("po"), b("pg", 0, 8))
+
+    nl = BLK // 16
+    nb = 128 // BLK
+    half = 8 * BLK
+    cp(ind(b("xm"), xoA), b("xs_", 0, NL))
+    late = []
+    for t in range(NR):
+        so, sl, pl = b("so", 8 * t, 8 * t + 8), b("sl", 8 * t, 8 * t + 8), b("pl%d" % t)
+        after.clear()
+        cp(b("cut"), ind(b("cds"), so))
+        act(b("xg"), ind(xv, so))
+        cp(ind(b("xm"), xoB), b("xg"))
+        for c in range(8):
+            o = b("kg", 256 * c, 256 * c + 256)
+            i = ind(kc, b("cut", 16 * c, 16 * c + 16))
+            (act if c % 2 == 0 else cp)(o, i)
+            after["SV"[c % 2]] = len(ops) - 1
+            its = []
+            for m in range(256 // BLK * c, 256 // BLK * (c + 1)):
+                q, blk = m // nb, m % nb
+                c0 = (q % 12) * BLK
+                its.append((b("pa%d" % (q // 12), c0, c0 + BLK, 1, blk * BLK, blk * BLK + BLK), b("kg", m * BLK, m * BLK + BLK),
+                            b("xm", m * BLK, m * BLK + BLK), True, True))
+            mm(its)
+        after["V"] = last("V")
+        cp(b("cs", 0, 128), b("cut"))
+        act(b("ev", 0, 12 * BLK), b("pa0", 0, 12 * BLK))
+        cp(b("ev", 12 * BLK, 16 * BLK), b("pa1", 0, 4 * BLK))
+        B1 = 256 * t
+        ts(b("sb1", B1, B1 + 256), ind(b("ev"), sel), sgn, A.mult, OFF, A.add)
+        hop(lambda r: T.sb1[:, B1 + 32 * r:B1 + 32 * r + 32], T.ld1[:, B1 + 32 * me:B1 + 32 * me + 32],
+            [b("sb1", B1, B1 + 256), b("ld2")] if t == 0 else [b("sb1", B1, B1 + 256)], others("ld1", B1, 32), True, HOP)
+        for q in "VSGP":
+            after[q] = last(q)
+        for k in late:
+            ops[k]["ord"].append(after["V"])
+        if t == 0:
+            iota(b("kt"), [[0, 1152]], 0, 0)
+            iota(b("it"), [[0, 1152]], -1, 0)
+
+        act(b("cs", 128, 256), ind(b("iv"), so))
+        mm([(b("pb", 0, 128), b("rep"), b("cs", 0, 128), True, True), (b("pb", 128, 256), b("rep"), b("cs", 128, 256), True, False),
+            (b("pb", 128, 256), b("idb"), b("bigu"), False, True), (b("pb", 256, 260), b("cs", 128, 256), b("zo", 8, 12), True, True)])
+        act(b("ec"), b("pb", 0, 256))
+        act(b("sc", 0, 1), b("pb", 256, 257))
+        cp(b("goff"), ind(b("ec", 0, 128), l1))
+        cp(b("cq"), ind(b("ec", 0, 128), l2))
+        cp(b("gg"), ind(b("tb"), b("goff")))
+        mm([(b("pc_", 0, 32), b("gg", 128 * h, 128 * h + 128), b("z2", 1 - h, 33 - h), h == 0, h == 1) for h in range(2)])
+        act(b("tw"), b("pc_", 0, 32))
+        gather_sum("f1", "ld1", B1, 32, b("sb1", B1 + 32 * me, B1 + 32 * me + 32),
+                   [(0, 16, b("tw", 0, 16)), (16, 32, b("tw", 0, 16))], None, None)
+        tt(b("rw"), ind(b("tw"), lq), b("mi"), A.mult)
+        act(b("wo"), ind(b("tw"), lq))
+        mm([(b("pc_", 0, 256), b("idb"), b("tri"), True, False), (b("pc_", 0, 256), b("bd"), b("rw"), False, True)])
+        tt(b("less"), b("pc_", 0, 256), b("wo"), A.is_lt)
+        add("V", lambda: g.vector.tensor_tensor_scan(ap(b("scan")), ap(b("rs")), ap(b("less")), 0.0, A.mult, A.add),
+            [b("rs"), b("less")], [b("scan")], 0.3)
+        scol = b("sc", 0, 1)
+        ts(b("e2"), b("ec", 128, 256), scol, A.is_equal)
+        red(b("sc", 1, 2), b("e2"), A.max)
+        cp(b("si", 0, 1), scol)
+        ts(b("si", 1, 2), b("si", 0, 1), 7, A.arith_shift_right)
+        ts(b("si", 2, 3), b("si", 0, 1), 127, A.bitwise_and)
+        cp(b("sc", 2, 4), b("si", 1, 3))
+        ts(b("sc", 4, 5), b("sc", 2, 3), float(t), A.is_equal, b("sc", 1, 2), A.max)
+        ts(b("bq"), b("mq"), b("sc", 4, 5), A.mult)
+        mm([(b("pb", 0, 16), b("ma"), b("bq"), True, True)])
+        ts(b("q1", 0, 16), b("pb", 0, 16), -1.0, A.mult, 1.0, A.add)
+        ts(b("q1", 16, 32), b("scan", 15, 256, 16), -8192.0, A.mult, 131072.0, A.add)
+        tt(b("q1", 32, 48), b("q1", 16, 32), b("cq"), A.add)
+        tt(b("q1", 48, 64), b("q1", 32, 48), b("q1", 0, 16), A.mult)
+        qe = b("q1", 48, 64)
+        for h, mc in ((0, cg(6)), (1, cA2)):
+            ts(b("qq", 32 * h, 32 * h + 16), qe, 4096.0, A.add, mc, A.mult)
+            ts(b("qq", 32 * h + 16, 32 * h + 32), qe, mc, A.mult)
+
+        finish_sum("f1", "ld1", B1, 32, ("x1", 0), ("y1", 0), b("sd"))
+        for h in range(2):
+            tt(b("mq2", 32 * h, 32 * h + 32), b("sd"), b("qq", 32 * h, 32 * h + 32), A.mult)
+        for h in range(2):
+            tt(b("v32", 16 * h, 16 * h + 16), b("mq2", 32 * h, 32 * h + 16), b("mq2", 32 * h + 16, 32 * h + 32), A.subtract)
+        add("V", lambda: g.vector.transpose(ap(b("t32")), ap(b("v32"))), [b("v32")], [b("t32")], 0.07)
+        B2, wd = (0, 16, 48)[t], (1, 2, 1)[t]
+        own = B2 + 8 * wd
+        if wd == 2:
+            cp(b("ld2", own + 1, own + 2), b("po", t + 1, t + 2))
+        red(b("ld2", own, own + 1), b("t32"), A.max, True)
+        after["V"] = last("V")
+        hop(T.ld2[:, own:own + wd], T.ld2[:, B2 + me * wd:B2 + me * wd + wd], [b("ld2", own, own + wd)], [b("ld2", B2, own)], False, HOP)
+        win, glv = b("ld2", B2, own + 8), (gl2 if wd == 1 else gl4)
+        if t < NR - 1:
+            cp(ind(b("xm"), xoA), b("xs_", NL * t + NL, NL * t + 2 * NL))
+
+        ts(b("oh"), i128, b("sc", 3, 4), A.is_equal)
+        ts(b("yh"), b("iv", 0, 8), b("sc", 2, 3), A.is_equal)
+        ts(b("yh2", 0, 8), b("yh"), -BIG, A.mult)
+        ts(b("yh2", 8, 16), b("yh"), b("jt", t, t + 1), A.mult)
+        cp(b("smi"), b("ec", 128, 256))
+        ts(b("smj"), b("smi"), 127, A.bitwise_and)
+        ts(b("oht"), b("smj"), cP, A.is_equal)
+        mm([(b("pb", 0, 8), b("oht"), b("po"), True, True)])
+        tt(b("up", 0, 8), b("pb", 0, 8), b("yh"), A.mult)
+        red(b("up", 8, 9), b("up", 0, 8), A.add)
+        tt(b("tg", 0, 8), sl, b("dump"), A.subtract)
+        if t == 0:
+            act(b("xp"), ind(xv, pl))
+            act(b("xps"), ind(b("xp"), so))
+        if t < NR - 1:
+            pn = b("pnl", 16 * t, 16 * t + 8)
+            nx = NL * (t + 1)
+            act(b("xpn", 0, NL), b("xs_", nx, nx + NL))
+            if wd == 1:
+                pc = b("pc")
+                act(b("pn"), ind(b("iv"), pn))
+                mm([(b("pe", 64, 72), b("pn"), b("zi", 8, 16), True, True)])
+                act(pc, b("pe", 64, 72))
+                tt(b("gm3"), ind(pc, gl), m2, A.mult)
+            else:
+                pc = b("pc2", 0, 8)
+                tt(b("gm3"), ind(win, gl5), m2, A.mult)
+                mm([(b("pe", 64, 72), b("gm3"), b("r2"), True, True)])
+                cp(pn, b("pe", 64, 72))
+            act(b("xpn", NL, 2 * NL), ind(xv, pn))
+            mm([(b("pf_", 0, 8), b("gm3"), b("r2"), True, False)])
+
+        tt(b("gm"), ind(win, glv), b("m1"), A.mult)
+        mm([(b("pd", 0, 8), b("gm"), b("r1"), True, True)])
+        cp(b("li", 0, 8), b("pd", 0, 8))
+        ts(b("tg", 8, 16), b("pd", 0, 8), 8000.0, A.is_gt)
+        ts(b("li", 8, 16), b("li", 0, 8), 4095, A.bitwise_and)
+        tt(b("tg", 16, 24), b("tg", 8, 16), b("tg", 0, 8), A.mult)
+        cp(b("cl"), b("li", 8, 16))
+        tt(b("tg", 24, 32), b("tg", 16, 24), b("dump"), A.add)
+        cp(b("tgt"), b("tg", 24, 32))
+        act(b("kcc"), ind(kc, b("cl")))
+        cp(ind(b("kt"), b("tgt")), b("kcc"))
+        if t > 0:
+            after["S"] = last("S")
+            for h in range(2):
+                act(b("xp", 512 * h, 512 * h + 512), ind(xv, b("pl%d" % t, 32 * h, 32 * h + 32)))
+            act(b("xps"), ind(b("xp"), so))
+        if t < NR - 1:
+            B3 = 128 * t
+            tt(b("pf"), ind(b("kt"), b("pnl", 16 * t, 16 * t + 16)), b("xpn"), A.mult)
+            mm([(b("pg", 8 * w, 8 * w + 8), b("pf", 128 * w, 128 * w + 128), b("bi"), True, True) for w in range(2)])
+            ts(b("sb3", 16 * t, 16 * t + 16), b("pg", 0, 16), sgn, A.mult, OFF, A.add)
+            hop(T.sb3[:, 16 * t:16 * t + 16], T.ld3[:, B3 + 16 * me:B3 + 16 * me + 16], [b("sb3", 16 * t, 16 * t + 16)],
+                others("ld3", B3, 16), False, HOP)
+            after["V"] = last("V")
+        B9 = 72 * t
+        for c in range(4):
+            tt(b("pr", 256 * c, 256 * c + 256), ind(b("kt"), b("pl%d" % t, 16 * c, 16 * c + 16)), b("xs_", 256 * c, 256 * c + 256), A.mult)
+            mm([(b("pc_", 0, 72), b("pr", 128 * y, 128 * y + 128), b("z9", 8 - y, 80 - y), y == 0, False) for y in (2 * c, 2 * c + 1)])
+        tt(b("pr", 1024, 1152), b("kcc"), b("xps"), A.mult)
+        mm([(b("pc_", 0, 72), b("pr", 1024, 1152), b("z9", 0, 72), False, True)])
+        ts(b("sb9", B9, B9 + 72), b("pc_", 0, 72), sgn, A.mult, OFF, A.add)
+        last_conv = last("V")
+        hop(lambda r: T.sb9[:, B9 + 9 * r:B9 + 9 * r + 9], T.ld9[:, B9 + 9 * me:B9 + 9 * me + 9], [b("sb9", B9, B9 + 72)],
+            others("ld9", B9, 9), True, HOP)
+
+        tt(b("gv"), ind(win, glv), b("mr2"), A.mult)
+        mm([(b("pd", 128, 256), b("mr3"), b("iv", NL * t, NL * t + NL), True, False), (b("pd", 128, 256), b("gv"), b("pm"), False, True)])
+        act(b("wv"), b("pd", 128, 256))
+        if t == NR - 1:
+            after["V"] = last_conv
+        tt(b("src"), ind(b("tb"), b("cl")), b("wv"), A.add)
+        cp(ind(b("it"), b("tgt")), b("src"))
+        if t < NR - 1:
+            act(b("ian"), ind(b("it"), pn))
+            mm([(b("pe", 0, 64), b("ian"), b("zi", 8, 72), True, False), (b("pe", 0, 64), b("it", nx, nx + NL), b("zi", 0, 64), False, True)])
+            act(b("ei"), b("pe", 0, 64))
+            gather_sum("f3", "ld3", B3, 16, b("sb3", 16 * t, 16 * t + 16), [(0, 16, b("ei", 0, 16))], None, None)
+            cp(b("vi", 0, 16), b("ei", 32, 48))
+            ts(b("vi", 16, 32), b("vi", 0, 16), 12, A.arith_shift_right, 1, A.bitwise_and)
+            ts(b("sdf", 0, 16), b("ei", 48, 64), NL * t - 0.5, A.is_lt, 2.0, A.mult)
+            tt(b("sdf", 16, 32), b("vi", 16, 32), b("sdf", 0, 16), A.add)
+            if wd == 2:
+                cp(b("pc2"), ind(win, l5))
+            for w in range(2):
+                tt(b("sdf", 32 + 8 * w, 40 + 8 * w), b("ei", 48 + 8 * w, 56 + 8 * w), pc, A.subtract)
+            finish_sum("f3", "ld3", B3, 16, ("x3", 0), ("y3", 0), b("w3", 0, 16))
+            tt(b("w3", 16, 32), b("w3", 0, 16), b("sdf", 16, 32), A.is_equal)
+            tt(b("w3", 32, 48), b("w3", 16, 32), b("sdf", 32, 48), A.mult)
+            tt(b("w3", 48, 56), b("w3", 32, 40), b("w3", 24, 32), A.mult)
+            tt(b("w3", 56, 64), b("w3", 32, 40), b("w3", 40, 48), A.add)
+            tt(b("w3", 64, 72), b("w3", 56, 64), b("w3", 48, 56), A.subtract)
+            tt(b("gm2"), ind(b("w3", 64, 72), gl), m2, A.mult)
+            mm([(b("pf_", 0, 8), b("gm2"), b("r2"), False, True)])
+            cp(b("so", 8 * t + 8, 8 * t + 16), b("pf_", 0, 8))
+            cp(b("sl", 8 * t + 8, 8 * t + 16), b("pf_", 0, 8))
+
+        mm([(b("pe", 128, 192), b("src"), b("zi", 8, 72), True, True)])
+        act(b("el"), b("pe", 128, 192))
+        ts(b("yw", 0, 8), b("el", 32, 40), 8000.0, A.is_gt)
+        ts(b("yw", 8, 16), b("el", 16, 24), 1.0, A.add)
+        tt(b("yw", 8, 16), b("yw", 8, 16), b("yw", 0, 8), A.mult)
+        tt(b("gy"), ind(b("yw", 8, 16), gl), m2, A.mult)
+        mm([(b("pe", 256, 264), b("gy"), b("r2"), True, True)])
+        ts(b("ycs", 8 * t, 8 * t + 8), b("pe", 256, 264), -1.0, A.add)
+        if t == NR - 1:
+            dma("Y", [(T.yc[:, :], T.ycs[:, :])], [b("ycs")], [])
+
+        mm([(b("pg", 64, 100), b("src"), b("zo", 0, 36), True, False)])
+        for c in range(4):
+            act(b("ia", 256 * c, 256 * c + 256), ind(b("it"), b("pl%d" % t, 16 * c, 16 * c + 16)))
+            mm([(b("pg", 64, 100), b("ia", 128 * y, 128 * y + 128), b("zo", 8 - y, 44 - y), False, y == 7) for y in (2 * c, 2 * c + 1)])
+        act(b("eo", 0, 36), b("pg", 64, 100))
+        gather_sum("f9", "ld9", B9, 9, b("sb9", B9 + 9 * me, B9 + 9 * me + 9), [(0, 9, b("eo", 0, 9))], None, None)
+        cp(b("vo", 0, 9), b("eo", 18, 27))
+        ts(b("vo", 16, 25), b("vo", 0, 9), 12, A.arith_shift_right, 1, A.bitwise_and)
+        ts(b("sdo", 0, 8), b("eo", 27, 35), NL * t - 0.5, A.is_lt, 2.0, A.mult)
+        ts(b("sdo", 8, 9), b("eo", 26, 27), 8000.0, A.is_lt, 2.0, A.mult)
+        ts(b("sdo", t, t + 1), b("eo", 27 + t, 28 + t), b("jt", t, t + 1), A.is_equal, b("sdo", t, t + 1), A.add)
+        ts(b("sdo", 0, 9), b("sdo", 0, 9), 2.0, A.mult)
+        tt(b("sdo", 16, 25), b("vo", 16, 25), b("sdo", 0, 9), A.add)
+        tt(b("sdo", 32, 40), b("eo", 27, 35), b("po"), A.subtract)
+        tt(b("sdo", 40, 41), b("up", 8, 9), scol, A.subtract)
+        k0 = len(ops)
+        finish_sum("f9", "ld9", B9, 9, ("x9", 0), ("x9", 40), b("w9", 0, 9))
+        tt(b("w9", 16, 25), b("w9", 0, 9), b("sdo", 16, 25), A.is_equal)
+        ts(b("w9", 48, 64), b("yh2"), b("w9", 24, 25), A.mult)
+        tt(b("w9", 32, 41), b("w9", 16, 25), b("sdo", 32, 41), A.mult)
+        mm([(b("pg", 128, 144), b("oh"), b("w9", 48, 64), True, True)])
+        tt(b("w9", 64, 72), b("w9", 32, 40), b("po"), A.add)
+        tt(b("w9", 64 + t, 65 + t), b("w9", 64 + t, 65 + t), b("w9", 40, 41), A.add)
+        tt(b("w9", 72, 80), b("w9", 64, 72), b("pg", 128, 136), A.add)
+        tt(b("po"), b("w9", 72, 80), b("pg", 136, 144), A.max)
+        tt(b("g64"), ind(b("po"), ly), b("m3"), A.mult)
+        mm([(b("pg", 192, 256, 1, 0, 16), mb, b("g64"), True, True)])
+        dn = "dp%d" % (t + 1)
+        lo = b("pu", 0, 64, 1, 0, 16) if t < NR - 1 else b("pw", 0, 64, 1, 0, 16)
+        act(lo, b("pg", 192, 256, 1, 0, 16)) if t == NR - 1 else cp(lo, b("pg", 192, 256, 1, 0, 16))
+        late = [k for k in range(k0, len(ops)) if ops[k]["eng"] == "V"]
+        dma("Y", [(T[dn][me], ap(lo))], [lo], [(dn, me, me + 1)])
+        hop(T[dn][me], T[dn][me], [(dn, me, me + 1)], [(dn, r, r + 1) for r in peers], False, HOPD)
+        ops[-1]["bias"] = BIAS if t < NR - 1 else 0.0
+        if t < NR - 1:
+            dma("Y", [(T["pl%d" % (t + 1)][:, :], T[dn][:])], [(dn, 0, 8)], [b("pl%d" % (t + 1))])
+        else:
+            dma("Y", [(T.yp[:, :], T[dn][:])], [(dn, 0, 8)], [])
+
+    m = len(ops)
+    succ = [[] for _ in range(m)]
+    for k in range(m):
+        for j in ops[k]["deps"]:
+            succ[j].append(k)
+    behind = [[] for _ in range(m)]
+    for k in range(m):
+        for j in ops[k]["ord"]:
+            behind[j].append(k)
+    left = [len(succ[k]) + len(behind[k]) for k in range(m)]
+    todo = [k for k in range(m) if left[k] == 0]
+    prio = [0.0] * m
+    while todo:
+        k = todo.pop()
+        prio[k] = max([ops[k]["lat"] + prio[j] for j in succ[k]] + [prio[j] for j in behind[k]] + [ops[k]["lat"]]) + ops[k]["cost"] + 1e-6 \
+            + ops[k].get("bias", 0.0)
+        for j in ops[k]["deps"] + ops[k]["ord"]:
+            left[j] -= 1
+            if left[j] == 0:
+                todo.append(j)
+    assert max(left) == 0
+    busy = {}
+    start, done = [0.0] * m, [0.0] * m
+    for k in sorted(range(m), key=lambda k: (-prio[k], k)):
+        o = ops[k]
+        s = max([done[j] for j in o["deps"]] + [start[j] + ops[j]["cost"] for j in o["ord"]] + [0.0])
+        if o["eng"] != "X":
+            sl_ = busy.setdefault(o["eng"], [])
+            for (u, w) in sl_:
+                if s + o["cost"] <= u:
+                    break
+                s = max(s, w)
+            sl_.append((s, s + o["cost"]))
+            sl_.sort()
+        start[k] = s
+        done[k] = s + o["cost"] + o["lat"]
+    order = sorted(range(m), key=lambda k: (start[k], -prio[k], k))
+    PLAN[me] = [(start[k], done[k], ops[k]["eng"], k, ops[k]["tag"]) for k in order]
+    PLAN["ops"] = (ops, order)
+    queue = {"V": g.vector, "S": g.scalar, "P": g.tensor, "G": g, "Y": g.sync}
+    count = {"V": 0, "S": 0, "P": 0, "G": 0}
+    for k in order:
+        o = ops[k]
+        if o["kind"] == "c" and any(not (o["eng"] == "P" and ops[j]["eng"] == "P") for j in succ[k]):
+            count[o["eng"]] += 1
+            o["sem"] = (T.sem[o["eng"]], count[o["eng"]])
+            o["key"] = o["eng"]
+        elif o["kind"] in "da":
+            o["key"] = k
+    seen = {}
+    for k in order:
+        o = ops[k]
+        e = o["eng"]
+        if e == "X":
+            continue
+        need = {}
+        for j in o["deps"]:
+            d = ops[j]
+            if d["kind"] == "r" or (e == "P" and d["eng"] == "P"):
+                continue
+            if d["sem"][1] > need.get(d["key"], (None, 0))[1]:
+                need[d["key"]] = d["sem"]
+        for key in need:
+            if need[key][1] > seen.get((e, key), 0):
+                queue[e].wait_ge(need[key][0], need[key][1])
+                seen[(e, key)] = need[key][1]
+        r = o["fn"]()
+        if o["kind"] == "c" and "sem" in o:
+            r.then_inc(o["sem"][0], 1)
+    for e in count:
+        if count[e] > max([seen.get((q, e), 0) for q in queue]):
+            g.wait_ge(T.sem[e], count[e])
+    g.wait_ge(T.sem.sent, sent[0])
+    for k in order:
+        o = ops[k]
+        if o["kind"] in "da" and not any((q, k) in seen for q in queue):
+            g.sync.wait_ge(o["sem"][0], o["sem"][1])
+
+
+PLAN = {}

@@ -46,17 +46,54 @@ for _b in BANKS:
 SCRATCH["dp1"] = ("dram", [8, 128, 8], U16)
 SCRATCH["dp2"] = ("dram", [8, 128, 8], U16)
 SCRATCH["dp3"] = ("dram", [8, 128, 8], F32)
-SEMAPHORES = ["V", "S", "P", "G", "sent"] + ["d%d" % i for i in range(24)] + ["a%d" % i for i in range(20)]
+SEMAPHORES = ["V", "S", "P", "G", "sent", "h0", "h1", "s0", "s1"] + ["d%d" % i for i in range(32)] + ["a%d" % i for i in range(20)]
 
-HOP = 4.0
-HOPD = 2.5
-DMAT = 2.0
+HOP = 3.1
+HOPD = 1.8
+DMAT = 1.6
 BIAS = 3.0
+HELP = 2.5
+VIA = ()
+TBV = 2304
+STAGE = False
+for _t in range(NR):
+    SCRATCH["dd%d" % _t] = ("dram", [8, 128, 1], F32)
+
+
+def bits(engines):
+    return sum(1 << e for e in engines)
+
+
+def helper_of(core, T, topo):
+    return [c for c in topo.cores_of(core) if T.rank_of(c) is None and topo.die(c) == topo.die(core)
+            and all(topo.may_write(c, d) for d in T.cores)][0]
+
+
+def helper_program(g, core, me, T, topo):
+    n = len(T.cores)
+    hc = T.cores[me]
+    peers = [(me + i) % n for i in range(1, n)]
+    engs = [e for e in topo.engines(core, T.cores[peers[0]]) if all(e in topo.engines(core, T.cores[r]) for r in peers)]
+    off = [e for e in topo.engines(hc, T.cores[peers[0]]) if all(e in topo.engines(hc, T.cores[r]) for r in peers)]
+    spare = [e for e in topo.engines(hc, core) if e not in off]
+    for t in VIA:
+        tr = []
+        for i, r in enumerate(peers):
+            rid, pid = topo.addr(T.cores[r], core)
+            tr.append(RemoteDMATransfer(dst_ids=[DstId(rid=rid, pnc=pid)], dma_engine_mask=1 << engs[i], remote_sem=T.sem["s%d" % t],
+                                        src=T.sb9[:, 72 * t + 9 * r:72 * t + 9 * r + 9], dst=T.ld9[:, 72 * t + 9 * me:72 * t + 9 * me + 9]))
+        g.wait_ge(T.sem["h%d" % t], len(spare))
+        g.remote_dma_fused(tr, local_sem=T.sem.sent)
+    if VIA:
+        g.wait_ge(T.sem.sent, len(VIA) * (n - 1))
 
 
 def rank_program(g, core, T, topo):
     me = T.rank_of(core)
     if me is None:
+        for r, c in enumerate(T.cores):
+            if core in topo.cores_of(c) and helper_of(c, T, topo) == core:
+                helper_program(g, core, r, T, topo)
         return
     n = len(T.cores)
     A, AX, AF = AluOpType, AxisListType.X, ActivationFunctionType
@@ -167,6 +204,10 @@ def rank_program(g, core, T, topo):
             fn = lambda: g.scalar.activation(ap(out), ap(x), AF.Copy, scale=scale)
         add("S", fn, [x], [out], vcost(out, [x]) + 0.02)
 
+    def lin(out, x, scale, bias):
+        add("S", lambda: g.scalar.activation(ap(out), ap(x), AF.Identity, bias=val(bias), scale=val(scale)), [x, scale, bias], [out],
+            vcost(out, [x]) + 0.02)
+
     def mm(items):
         def fn():
             r = None
@@ -216,10 +257,22 @@ def rank_program(g, core, T, topo):
         sem = T.sem["a%d" % na[0]]
         na[0] += 1
         if spread:
-            tr = [RemoteDMATransfer(dst_ids=[dst[r]], dma_engine_mask=1 << engs[i], remote_sem=sem, src=srcs(r), dst=dsts)
-                  for i, r in enumerate(peers)]
-            cnt = n - 1
-            sent[0] += n - 1
+            calls, i0, cnt = [], 0, 0
+            for many in (4, 2, 1):
+                per = len(engs) // many
+                calls.append([RemoteDMATransfer(dst_ids=[dst[peers[i0 + i]]], dma_engine_mask=bits(engs[i * per:(i + 1) * per]),
+                                                remote_sem=sem, src=srcs(peers[i0 + i]), dst=dsts) for i in range(many)])
+                i0 += many
+                cnt += many * per
+            sent[0] += cnt
+
+            def fn():
+                for tr_ in calls:
+                    g.remote_dma_fused(tr_, local_sem=T.sem.sent)
+            k = add("G", fn, reads, [], 0.8, 0.0, "r")
+            k2 = add("X", None, [], lands, 0.0, lat, "a", extra=k)
+            ops[k2]["sem"] = (sem, cnt)
+            return
         else:
             tr = [RemoteDMATransfer(dst_ids=[dst[r] for r in peers], dma_engine_mask=full, remote_sem=sem, srcs=[srcs],
                                     dsts=[dsts for r in peers])]
@@ -228,6 +281,17 @@ def rank_program(g, core, T, topo):
         k = add("G", lambda: g.remote_dma_fused(tr, local_sem=T.sem.sent), reads, [], 0.8, 0.0, "r")
         k2 = add("X", None, [], lands, 0.0, lat, "a", extra=k)
         ops[k2]["sem"] = (sem, cnt)
+
+    def by_helper(t, lat):
+        hc = helper_of(core, T, topo)
+        spare = [e for e in topo.engines(core, hc) if e not in engs]
+        rid, pid = topo.addr(hc, core)
+        piece = T.sb9[:, 72 * t:72 * t + 72]
+        sent[0] += len(spare)
+        k = add("G", lambda: g.remote_dma(piece, piece, T.sem["h%d" % t], T.sem.sent, pid, rid, bits(spare)),
+                [b("sb9", 72 * t, 72 * t + 72)], [], 0.8, 0.0, "r")
+        k2 = add("X", None, [], others("ld9", 72 * t, 9), 0.0, lat, "a", extra=k)
+        ops[k2]["sem"] = (T.sem["s%d" % t], n - 1)
 
     def others(name, base, w):
         return [b(name, base + r * w, base + (r + 1) * w) for r in peers]
@@ -254,8 +318,13 @@ def rank_program(g, core, T, topo):
     dma("Y", [(T.cds[:, :], T.cd[:, :])], [], [b("cds")], 3.2)
     after["Y"] = last("Y")
     dma("S", [(T["xs_"][:, :], T.xv[:, :])], [], [b("xs_")], 3.2)
-    dma("Y", [(T.kcs[:, :], T.kc[:, :])], [], [b("kcs")], 5.8)
-    fill(b("tb"), 0)
+    dma("Y", [(T.kcs[:, :], T.kc[:, :])], [], [b("kcs")], 4.8)
+    iota(b("ci", 0, 1), [[0, 1]], 0, 1)
+    after["G"] = last("G")
+    iota(b("lf", 0, 8), [[256, 8]], 0, 0)
+    after["G"] = last("G")
+    fill(b("tb", 0, TBV), 0)
+    iota(b("tb", TBV, NC), [[0, NC - TBV]], 0, 0)
     dma("Y", [(T.tb[0:128:16, :], T.bt[:, :]), (T.tb[1:128:16, :], T.co[:, :])], [], [b("tb")], 3.5)
     dma("Y", [(T.tb[16 * h + 4:16 * h + 6, :], T.tb[16 * me:16 * me + 2, :]) for h in range(8)], [b("tb")], [b("tb")], 2.5)
 
@@ -264,7 +333,6 @@ def rank_program(g, core, T, topo):
 
     def cg(i):
         return b("cg", i, i + 1)
-    iota(b("ci", 0, 1), [[0, 1]], 0, 1)
     p_ = b("ci", 0, 1)
     ts(b("ci", 1, 2), p_, 15, A.bitwise_and)
     ts(b("ci", 2, 3), p_, 4, A.arith_shift_right)
@@ -295,7 +363,6 @@ def rank_program(g, core, T, topo):
     iota(b("rb"), [[0, 16], [1, 16]], 0, 0)
     iota(b("rg"), [[1, 8], [0, 16]], 0, 0)
     iota(b("r8"), [[0, 8], [1, 8]], 0, 0)
-    iota(b("lf", 0, 8), [[256, 8]], 0, 0)
     iota(b("lf", 16, 32), [[1, 8], [8, 2]], 0, 0)
     iota(b("lf", 32, 36), [[2, 4]], 0, 0)
     iota(b("lf", 40, 48), [[16, 8]], NV, 0)
@@ -346,15 +413,18 @@ def rank_program(g, core, T, topo):
     ts(b("z2", 0, 33), b("iv", 0, 33), cg(10), A.is_equal)
     ts(b("zi"), b("iv", 0, 72), cg(11), A.is_equal)
     ts(b("zo", 0, 44), b("iv", 0, 44), cg(12), A.is_equal)
+    if STAGE:
+        tt(b("m1"), b("bd"), b("mr2"), A.mult)
     m2, mb = b("mi", 0, 128), b("mi", 0, 16)
-    for h in range(2):
-        act(b("xm", NV * h, NV * h + NV), b("iv"), 0.0)
+    fill(b("xm", 0, NV), 0.0)
+    act(b("xm", NV, 2 * NV), b("xs_"), 0.0)
     fill(b("ld2"), 0.0)
     cp(b("so", 0, 8), b("pas", 0, 8))
     cp(b("sl", 0, 8), b("pas", 0, 8))
     cp(b("pl0"), b("pas"))
     xv, kc = b("xs_"), b("kcs")
-    act(b("ia"), ind(b("iv"), b("pl0")))
+    for h in range(2):
+        act(b("ia", 512 * h, 512 * h + 512), ind(b("iv"), b("pl0", 32 * h, 32 * h + 32)))
     mm([(b("pg", 0, 9), b("ia", 128 * y, 128 * y + 128), b("zo", 8 - y, 17 - y), y == 0, y == 7) for y in range(8)])
     act(b("po"), b("pg", 0, 8))
 
@@ -383,6 +453,8 @@ def rank_program(g, core, T, topo):
             mm(its)
         after["V"] = last("V")
         cp(b("cs", 0, 128), b("cut"))
+        act(b("cs", 128, 256), ind(b("iv"), so))
+        after["S"] = last("S")
         act(b("ev", 0, 12 * BLK), b("pa0", 0, 12 * BLK))
         cp(b("ev", 12 * BLK, 16 * BLK), b("pa1", 0, 4 * BLK))
         B1 = 256 * t
@@ -397,21 +469,23 @@ def rank_program(g, core, T, topo):
             iota(b("kt"), [[0, 1152]], 0, 0)
             iota(b("it"), [[0, 1152]], -1, 0)
 
-        act(b("cs", 128, 256), ind(b("iv"), so))
-        mm([(b("pb", 0, 128), b("rep"), b("cs", 0, 128), True, True), (b("pb", 128, 256), b("rep"), b("cs", 128, 256), True, False),
-            (b("pb", 128, 256), b("idb"), b("bigu"), False, True), (b("pb", 256, 260), b("cs", 128, 256), b("zo", 8, 12), True, True)])
-        act(b("ec"), b("pb", 0, 256))
-        act(b("sc", 0, 1), b("pb", 256, 257))
+        mm([(b("pb", 0, 128), b("rep"), b("cs", 0, 128), True, True)])
+        act(b("ec", 0, 128), b("pb", 0, 128))
+        mm([(b("pd", 128, 256), b("rep"), b("cs", 128, 256), True, False), (b("pd", 128, 256), b("idb"), b("bigu"), False, True),
+            (b("pd", 256, 260), b("cs", 128, 256), b("zo", 8, 12), True, True)])
+        act(b("ec", 128, 256), b("pd", 128, 256))
+        act(b("sc", 0, 1), b("pd", 256, 257))
+        mm([(b("pc_", 0, 256), b("idb"), b("tri"), True, False)])
         cp(b("goff"), ind(b("ec", 0, 128), l1))
         cp(b("cq"), ind(b("ec", 0, 128), l2))
         cp(b("gg"), ind(b("tb"), b("goff")))
-        mm([(b("pc_", 0, 32), b("gg", 128 * h, 128 * h + 128), b("z2", 1 - h, 33 - h), h == 0, h == 1) for h in range(2)])
-        act(b("tw"), b("pc_", 0, 32))
+        mm([(b("pb", 128, 160), b("gg", 128 * h, 128 * h + 128), b("z2", 1 - h, 33 - h), h == 0, h == 1) for h in range(2)])
+        act(b("tw"), b("pb", 128, 160))
         gather_sum("f1", "ld1", B1, 32, b("sb1", B1 + 32 * me, B1 + 32 * me + 32),
                    [(0, 16, b("tw", 0, 16)), (16, 32, b("tw", 0, 16))], None, None)
         tt(b("rw"), ind(b("tw"), lq), b("mi"), A.mult)
         act(b("wo"), ind(b("tw"), lq))
-        mm([(b("pc_", 0, 256), b("idb"), b("tri"), True, False), (b("pc_", 0, 256), b("bd"), b("rw"), False, True)])
+        mm([(b("pc_", 0, 256), b("bd"), b("rw"), False, True)])
         tt(b("less"), b("pc_", 0, 256), b("wo"), A.is_lt)
         add("V", lambda: g.vector.tensor_tensor_scan(ap(b("scan")), ap(b("rs")), ap(b("less")), 0.0, A.mult, A.add),
             [b("rs"), b("less")], [b("scan")], 0.3)
@@ -423,16 +497,16 @@ def rank_program(g, core, T, topo):
         ts(b("si", 2, 3), b("si", 0, 1), 127, A.bitwise_and)
         cp(b("sc", 2, 4), b("si", 1, 3))
         ts(b("sc", 4, 5), b("sc", 2, 3), float(t), A.is_equal, b("sc", 1, 2), A.max)
-        ts(b("bq"), b("mq"), b("sc", 4, 5), A.mult)
+        lin(b("bq"), b("mq"), b("sc", 4, 5), 0.0)
         mm([(b("pb", 0, 16), b("ma"), b("bq"), True, True)])
-        ts(b("q1", 0, 16), b("pb", 0, 16), -1.0, A.mult, 1.0, A.add)
+        lin(b("q1", 0, 16), b("pb", 0, 16), -1.0, 1.0)
         ts(b("q1", 16, 32), b("scan", 15, 256, 16), -8192.0, A.mult, 131072.0, A.add)
         tt(b("q1", 32, 48), b("q1", 16, 32), b("cq"), A.add)
         tt(b("q1", 48, 64), b("q1", 32, 48), b("q1", 0, 16), A.mult)
         qe = b("q1", 48, 64)
         for h, mc in ((0, cg(6)), (1, cA2)):
             ts(b("qq", 32 * h, 32 * h + 16), qe, 4096.0, A.add, mc, A.mult)
-            ts(b("qq", 32 * h + 16, 32 * h + 32), qe, mc, A.mult)
+            lin(b("qq", 32 * h + 16, 32 * h + 32), qe, mc, 0.0)
 
         finish_sum("f1", "ld1", B1, 32, ("x1", 0), ("y1", 0), b("sd"))
         for h in range(2):
@@ -440,21 +514,31 @@ def rank_program(g, core, T, topo):
         for h in range(2):
             tt(b("v32", 16 * h, 16 * h + 16), b("mq2", 32 * h, 32 * h + 16), b("mq2", 32 * h + 16, 32 * h + 32), A.subtract)
         add("V", lambda: g.vector.transpose(ap(b("t32")), ap(b("v32"))), [b("v32")], [b("t32")], 0.07)
-        B2, wd = (0, 16, 48)[t], (1, 2, 1)[t]
+        B2, wd = (0, 16, 48)[t], (1, 1 if STAGE else 2, 1)[t]
         own = B2 + 8 * wd
         if wd == 2:
             cp(b("ld2", own + 1, own + 2), b("po", t + 1, t + 2))
         red(b("ld2", own, own + 1), b("t32"), A.max, True)
         after["V"] = last("V")
-        hop(T.ld2[:, own:own + wd], T.ld2[:, B2 + me * wd:B2 + me * wd + wd], [b("ld2", own, own + wd)], [b("ld2", B2, own)], False, HOP)
+        if STAGE:
+            dd = "dd%d" % t
+            for e in range(2):
+                dma("YS"[e], [(T[dd][me, 64 * e:64 * e + 64, :], T.ld2[e:128:2, own:own + 1])], [b("ld2", own, own + 1)],
+                    [(dd, 2 * me + e, 2 * me + e + 1)])
+            hop(T[dd][me], T[dd][me], [(dd, 2 * me, 2 * me + 2)], [(dd, 2 * r, 2 * r + 2) for r in peers], False, HOPD)
+            dma("Y", [(T.ld2[:, B2:B2 + 8], T[dd][:])], [(dd, 0, 16)], [b("ld2", B2, B2 + 8)])
+            if t == 1:
+                cp(b("pnl", 16, 24), b("pl1", 16, 24))
+        else:
+            hop(T.ld2[:, own:own + wd], T.ld2[:, B2 + me * wd:B2 + me * wd + wd], [b("ld2", own, own + wd)], [b("ld2", B2, own)], False, HOP)
         win, glv = b("ld2", B2, own + 8), (gl2 if wd == 1 else gl4)
         if t < NR - 1:
             cp(ind(b("xm"), xoA), b("xs_", NL * t + NL, NL * t + 2 * NL))
 
         ts(b("oh"), i128, b("sc", 3, 4), A.is_equal)
         ts(b("yh"), b("iv", 0, 8), b("sc", 2, 3), A.is_equal)
-        ts(b("yh2", 0, 8), b("yh"), -BIG, A.mult)
-        ts(b("yh2", 8, 16), b("yh"), b("jt", t, t + 1), A.mult)
+        lin(b("yh2", 0, 8), b("yh"), -BIG, 0.0)
+        lin(b("yh2", 8, 16), b("yh"), b("jt", t, t + 1), 0.0)
         cp(b("smi"), b("ec", 128, 256))
         ts(b("smj"), b("smi"), 127, A.bitwise_and)
         ts(b("oht"), b("smj"), cP, A.is_equal)
@@ -462,8 +546,11 @@ def rank_program(g, core, T, topo):
         tt(b("up", 0, 8), b("pb", 0, 8), b("yh"), A.mult)
         red(b("up", 8, 9), b("up", 0, 8), A.add)
         tt(b("tg", 0, 8), sl, b("dump"), A.subtract)
-        if t == 0:
-            act(b("xp"), ind(xv, pl))
+        if t == NR - 1:
+            act(b("pa0", 0, 512), b("xs_", 512, NV))
+        if t != 1 or STAGE:
+            for h in range(2):
+                act(b("xp", 512 * h, 512 * h + 512), ind(xv, b("pl%d" % t, 32 * h, 32 * h + 32)))
             act(b("xps"), ind(b("xp"), so))
         if t < NR - 1:
             pn = b("pnl", 16 * t, 16 * t + 8)
@@ -483,10 +570,14 @@ def rank_program(g, core, T, topo):
             act(b("xpn", NL, 2 * NL), ind(xv, pn))
             mm([(b("pf_", 0, 8), b("gm3"), b("r2"), True, False)])
 
-        tt(b("gm"), ind(win, glv), b("m1"), A.mult)
-        mm([(b("pd", 0, 8), b("gm"), b("r1"), True, True)])
-        cp(b("li", 0, 8), b("pd", 0, 8))
-        ts(b("tg", 8, 16), b("pd", 0, 8), 8000.0, A.is_gt)
+        if STAGE:
+            lv = b("ld2", B2, B2 + 8)
+        else:
+            lv = b("pd", 0, 8)
+            tt(b("gm"), ind(win, glv), b("m1"), A.mult)
+            mm([(lv, b("gm"), b("r1"), True, True)])
+        cp(b("li", 0, 8), lv)
+        ts(b("tg", 8, 16), lv, 8000.0, A.is_gt)
         ts(b("li", 8, 16), b("li", 0, 8), 4095, A.bitwise_and)
         tt(b("tg", 16, 24), b("tg", 8, 16), b("tg", 0, 8), A.mult)
         cp(b("cl"), b("li", 8, 16))
@@ -494,7 +585,17 @@ def rank_program(g, core, T, topo):
         cp(b("tgt"), b("tg", 24, 32))
         act(b("kcc"), ind(kc, b("cl")))
         cp(ind(b("kt"), b("tgt")), b("kcc"))
-        if t > 0:
+        if STAGE:
+            tt(b("gv"), ind(lv, gl), m2, A.mult)
+            pair = (b("m1"), b("gv"))
+        else:
+            tt(b("gv"), ind(win, glv), b("mr2"), A.mult)
+            pair = (b("gv"), b("pm"))
+        mm([(b("pa1", 128, 256), b("mr3"), b("iv", NL * t, NL * t + NL), True, False)])
+        mm([(b("pa1", 128, 256), pair[0], pair[1], False, True)])
+        after["S"] = last("S")
+        act(b("wv"), b("pa1", 128, 256))
+        if t == 1 and not STAGE:
             after["S"] = last("S")
             for h in range(2):
                 act(b("xp", 512 * h, 512 * h + 512), ind(xv, b("pl%d" % t, 32 * h, 32 * h + 32)))
@@ -509,18 +610,23 @@ def rank_program(g, core, T, topo):
             after["V"] = last("V")
         B9 = 72 * t
         for c in range(4):
-            tt(b("pr", 256 * c, 256 * c + 256), ind(b("kt"), b("pl%d" % t, 16 * c, 16 * c + 16)), b("xs_", 256 * c, 256 * c + 256), A.mult)
+            kj = ind(b("kt"), b("pl%d" % t, 16 * c, 16 * c + 16))
+            if c < 2 or t < NR - 1:
+                tt(b("pr", 256 * c, 256 * c + 256), kj, b("xs_", 256 * c, 256 * c + 256), A.mult)
+            else:
+                act(b("kg", 256 * c, 256 * c + 256), kj)
+                tt(b("pr", 256 * c, 256 * c + 256), b("kg", 256 * c, 256 * c + 256), b("pa0", 256 * c - 512, 256 * c - 256), A.mult)
             mm([(b("pc_", 0, 72), b("pr", 128 * y, 128 * y + 128), b("z9", 8 - y, 80 - y), y == 0, False) for y in (2 * c, 2 * c + 1)])
         tt(b("pr", 1024, 1152), b("kcc"), b("xps"), A.mult)
         mm([(b("pc_", 0, 72), b("pr", 1024, 1152), b("z9", 0, 72), False, True)])
         ts(b("sb9", B9, B9 + 72), b("pc_", 0, 72), sgn, A.mult, OFF, A.add)
         last_conv = last("V")
-        hop(lambda r: T.sb9[:, B9 + 9 * r:B9 + 9 * r + 9], T.ld9[:, B9 + 9 * me:B9 + 9 * me + 9], [b("sb9", B9, B9 + 72)],
-            others("ld9", B9, 9), True, HOP)
+        if t in VIA:
+            by_helper(t, HOP + HELP)
+        else:
+            hop(lambda r: T.sb9[:, B9 + 9 * r:B9 + 9 * r + 9], T.ld9[:, B9 + 9 * me:B9 + 9 * me + 9], [b("sb9", B9, B9 + 72)],
+                others("ld9", B9, 9), True, HOP)
 
-        tt(b("gv"), ind(win, glv), b("mr2"), A.mult)
-        mm([(b("pd", 128, 256), b("mr3"), b("iv", NL * t, NL * t + NL), True, False), (b("pd", 128, 256), b("gv"), b("pm"), False, True)])
-        act(b("wv"), b("pd", 128, 256))
         if t == NR - 1:
             after["V"] = last_conv
         tt(b("src"), ind(b("tb"), b("cl")), b("wv"), A.add)
@@ -547,24 +653,27 @@ def rank_program(g, core, T, topo):
             tt(b("gm2"), ind(b("w3", 64, 72), gl), m2, A.mult)
             mm([(b("pf_", 0, 8), b("gm2"), b("r2"), False, True)])
             cp(b("so", 8 * t + 8, 8 * t + 16), b("pf_", 0, 8))
-            cp(b("sl", 8 * t + 8, 8 * t + 16), b("pf_", 0, 8))
+            cp(b("sl", 8 * t + 8, 8 * t + 16), b("so", 8 * t + 8, 8 * t + 16))
 
+        k1 = len(ops)
         mm([(b("pe", 128, 192), b("src"), b("zi", 8, 72), True, True)])
         act(b("el"), b("pe", 128, 192))
         ts(b("yw", 0, 8), b("el", 32, 40), 8000.0, A.is_gt)
-        ts(b("yw", 8, 16), b("el", 16, 24), 1.0, A.add)
+        lin(b("yw", 8, 16), b("el", 16, 24), 1.0, 1.0)
         tt(b("yw", 8, 16), b("yw", 8, 16), b("yw", 0, 8), A.mult)
         tt(b("gy"), ind(b("yw", 8, 16), gl), m2, A.mult)
         mm([(b("pe", 256, 264), b("gy"), b("r2"), True, True)])
-        ts(b("ycs", 8 * t, 8 * t + 8), b("pe", 256, 264), -1.0, A.add)
+        lin(b("ycs", 8 * t, 8 * t + 8), b("pe", 256, 264), 1.0, -1.0)
         if t == NR - 1:
             dma("Y", [(T.yc[:, :], T.ycs[:, :])], [b("ycs")], [])
 
         mm([(b("pg", 64, 100), b("src"), b("zo", 0, 36), True, False)])
         for c in range(4):
-            act(b("ia", 256 * c, 256 * c + 256), ind(b("it"), b("pl%d" % t, 16 * c, 16 * c + 16)))
+            (cp if t == NR - 1 and c % 2 == 0 else act)(b("ia", 256 * c, 256 * c + 256), ind(b("it"), b("pl%d" % t, 16 * c, 16 * c + 16)))
             mm([(b("pg", 64, 100), b("ia", 128 * y, 128 * y + 128), b("zo", 8 - y, 44 - y), False, y == 7) for y in (2 * c, 2 * c + 1)])
         act(b("eo", 0, 36), b("pg", 64, 100))
+        ops[k1]["ord"].append(last("P"))
+        ops[k1 + 1]["ord"].append(last("S"))
         gather_sum("f9", "ld9", B9, 9, b("sb9", B9 + 9 * me, B9 + 9 * me + 9), [(0, 9, b("eo", 0, 9))], None, None)
         cp(b("vo", 0, 9), b("eo", 18, 27))
         ts(b("vo", 16, 25), b("vo", 0, 9), 12, A.arith_shift_right, 1, A.bitwise_and)
@@ -589,7 +698,7 @@ def rank_program(g, core, T, topo):
         mm([(b("pg", 192, 256, 1, 0, 16), mb, b("g64"), True, True)])
         dn = "dp%d" % (t + 1)
         lo = b("pu", 0, 64, 1, 0, 16) if t < NR - 1 else b("pw", 0, 64, 1, 0, 16)
-        act(lo, b("pg", 192, 256, 1, 0, 16)) if t == NR - 1 else cp(lo, b("pg", 192, 256, 1, 0, 16))
+        cp(lo, b("pg", 192, 256, 1, 0, 16))
         late = [k for k in range(k0, len(ops)) if ops[k]["eng"] == "V"]
         dma("Y", [(T[dn][me], ap(lo))], [lo], [(dn, me, me + 1)])
         hop(T[dn][me], T[dn][me], [(dn, me, me + 1)], [(dn, r, r + 1) for r in peers], False, HOPD)

@@ -8,34 +8,40 @@ BIG = 4096.0
 F32, BF, F16, I32, U16 = "float32", "bfloat16", "float16", "int32", "uint16"
 
 _S = {
-    "xs_": (NV, BF), "kcs": (NC, BF), "cds": (NV, I32), "pas": (64, I32), "tb": (NC, I32),
-    "pl0": (64, U16), "pl1": (64, U16), "pl2": (64, U16),
-    "ci": (16, I32), "cf": (16, F32), "cg": (16, F32), "iv": (NV, F32), "rb": (256, F32), "rg": (128, F32), "r8": (64, F32),
-    "lf": (64, F32), "lst": (80, U16),
-    "m1": (128, F32), "r1": (8, F32), "mr2": (128, F32), "pm": (128, F32), "mi": (256, F32), "r2": (8, F32), "bi": (8, F16),
-    "bd": (128, F32), "rep": (128, F32), "tri": (256, BF), "idb": (128, BF), "rs": (256, F32), "bigu": (128, BF), "mq": (16, F32),
-    "ma": (128, F32), "m3": (64, F32), "jt": (8, F32), "dump": (8, F32), "z9": (80, F16), "z2": (40, F32), "zi": (72, F32),
-    "zo": (48, F32),
-    "so": (24, U16), "sl": (24, F32), "cut": (128, U16), "xg": (128, BF), "xm": (2048, BF), "kg": (2048, BF),
-    "ev": (16 * BLK, F32), "sb1": (3 * 256, U16), "ld1": (3 * 256, U16), "f1": (256, F32), "x1": (128, F32), "y1": (64, F32),
-    "sd": (32, F32), "mq2": (64, F32), "v32": (32, F32), "t32": (32, F32), "ld2": (80, F32),
-    "cs": (256, F32), "ec": (256, F32), "goff": (16, U16), "cq": (16, F32), "gg": (256, F32), "tw": (32, F32),
-    "rw": (256, F32), "wo": (256, F32), "less": (256, F32), "scan": (256, F32), "sc": (16, F32), "si": (8, I32),
-    "pnl": (32, U16), "pc2": (16, F32), "e2": (128, F32), "bq": (16, F32), "q1": (64, F32), "qq": (64, F32),
-    "oh": (128, F32), "oht": (128, F32), "smi": (128, I32), "smj": (128, I32), "yh": (8, F32), "yh2": (16, F32), "up": (16, F32),
+    "xs_": (NV, BF), "kcs": (NC, BF), "cds": (NV, I32), "pas": (64, I32), "tb": (NC, I32), "cs": (128, F32), "ec": (128, F32),
+    "rep": (128, F32),
+    "pl0": (64, U16), "pl1": (72, U16), "pl2": (72, U16),
+    "ci": (16, I32), "cf": (16, F32), "cg": (16, F32), "iv": (384, F32), "rb": (128, F32), "r8": (80, F32),
+    "lf": (96, F32), "lst": (128, U16), "la": (16, F32),
+    "m1": (128, F32), "r1": (8, F32), "pm": (128, F32), "m2": (128, F32), "bi": (8, F16),
+    "pmt": (128, F16), "one": (128, F16), "idh": (128, F16), "bigu": (128, F16), "mz": (48, F16), "mzf": (48, F32),
+    "kk": (32, F32), "m3": (80, F32), "jt": (8, F32), "dump": (8, F32), "z9": (80, F16), "z2": (72, F32), "zi": (136, F32),
+    "mk": (8, F32), "m2h": (128, F16), "sg": (64, F32), "mr6": (128, F32), "dh": (128, F16), "gmo": (128, F32), "gvo": (128, F32),
+    "lio": (16, I32), "tgo": (32, F32), "wvo": (128, F32), "sro": (128, F32), "ito": (1152, F32), "iao": (128, F32), "kj": (NV, BF),
+    "so": (24, U16), "cut": (128, U16), "xg": (128, BF), "xm": (2048, BF), "kg": (2048, BF),
+    "ev": (16 * BLK, F32), "sb1": (3 * 256, U16), "ld1": (3 * 256, U16), "f1": (256, F32), "x1": (64, F32), "y1": (96, F32),
+    "sd": (32, F32), "mq": (64, F32), "v32": (32, F32), "t32": (32, F32), "ld2": (48, F32),
+    "sw": (40, U16), "sh": (8, F16), "dg": (128, F16), "goff": (16, U16), "cq": (32, F32), "gg": (256, F32),
+    "ct": (64, F32), "less": (256, F32), "scan": (256, F32), "rs": (256, F32), "cm": (16, F32), "rk": (32, F32),
+    "wo": (256, F32), "e3": (128, F32), "sc": (16, F32), "si": (8, I32), "rm": (32, F32), "rt": (32, F32),
+    "pnl": (32, U16), "pc": (16, F32), "e2": (128, F32), "qq": (64, F32), "paf": (16, F32),
+    "ohb": (48, F16), "oha": (64, F32), "oh2": (384, F16), "obt": (128, F16), "ux": (64, F32), "up": (16, F32), "uh": (8, F16),
+    "pz": (64, F32), "py": (64, F32),
     "gm": (128, F32), "li": (16, I32), "cl": (8, U16), "tg": (32, F32), "tgt": (8, U16), "kcc": (128, BF), "kt": (1152, BF),
     "xpn": (256, BF), "pf": (256, F16), "sb3": (32, U16), "ld3": (256, U16), "f3": (128, F32), "x3": (64, F32), "y3": (32, F32),
-    "w3": (96, F32), "gm2": (128, F32), "gm3": (128, F32), "gv": (128, F32), "mr3": (128, F32), "wv": (128, F32), "src": (128, F32),
-    "it": (1152, F32), "ian": (128, F32), "pn": (128, F32), "ei": (64, F32), "pc": (8, F32), "vi": (32, I32), "sdf": (48, F32),
-    "el": (64, F32), "yw": (16, F32), "gy": (128, F32), "ycs": (24, F32),
-    "xp": (NV, BF), "xps": (128, BF), "pr": (1152, F16), "sb9": (3 * 72, U16), "ld9": (3 * 72, U16), "f9": (72, F32),
-    "ia": (NV, F32), "eo": (40, F32), "vo": (32, I32), "sdo": (48, F32), "x9": (64, F32), "w9": (96, F32), "po": (8, F32),
-    "g64": (64, F32), "pu": (128, U16), "pw": (64, F32),
+    "b3": (16, F32), "d0": (24, F32), "d1": (24, F32), "w3": (32, F32), "ga": (64, F16), "gv": (128, F32),
+    "mr3": (128, F32), "wv": (128, F32), "src": (128, F32),
+    "it": (1152, F32), "ian": (128, F32), "ei": (64, F32), "vi": (32, I32), "sdf": (32, F32),
+    "el": (64, F32), "yw": (32, F32), "gy": (64, F32), "ycs": (24, F32),
+    "xp": (NV, BF), "xps": (128, BF), "pr": (1152, F16), "sb9": (3 * 72, U16), "ld9": (3 * 64, U16), "f9": (72, F32),
+    "eo": (64, F32), "vo": (32, I32), "sdo": (48, F32), "x9": (64, F32), "w9": (32, F32), "po": (16, F32),
+    "gd": (80, F32), "g72": (80, F16), "rh2": (128, F16), "sm": (64, F32), "pu": (72, U16), "pw": (64, F32), "ph": (64, F16),
+    "px": (64, F32),
 }
 PLACE = {}
 _n = 0
 for _k, (_w, _d) in _S.items():
-    if _d == F32 and _w <= 96 and _k not in ("ld2", "ycs"):
+    if _d == F32 and _w <= 96 and _k not in ("ld2", "ycs", "pw"):
         PLACE[_k] = _n
         _n += (_w + 15) // 16 * 16
 SCRATCH = {k: ("sbuf", [128, n], d) for k, (n, d) in _S.items() if k not in PLACE}
@@ -43,57 +49,27 @@ SCRATCH["small"] = ("sbuf", [128, _n], F32)
 BANKS = ["pa0", "pa1", "pb", "pc_", "pd", "pe", "pf_", "pg"]
 for _b in BANKS:
     SCRATCH[_b] = ("psum", [128, 512], F32)
-SCRATCH["dp1"] = ("dram", [8, 128, 8], U16)
-SCRATCH["dp2"] = ("dram", [8, 128, 8], U16)
+SCRATCH["dp1"] = ("dram", [8, 128, 9], U16)
+SCRATCH["dp2"] = ("dram", [8, 128, 9], U16)
 SCRATCH["dp3"] = ("dram", [8, 128, 8], F32)
-SEMAPHORES = ["V", "S", "P", "G", "sent", "h0", "h1", "s0", "s1"] + ["d%d" % i for i in range(32)] + ["a%d" % i for i in range(20)]
+SEMAPHORES = ["V", "S", "P", "G", "sent"] + ["d%d" % i for i in range(32)] + ["a%d" % i for i in range(32)]
 
-HOP = 3.1
-HOPD = 1.8
-DMAT = 1.6
-BIAS = 3.0
-HELP = 2.5
-VIA = ()
+CYC, GAT, SCA, PEC, LAT, SFIX = 0.00083, 1.56, 3.8, 0.0005, 0.2, 0.1
+HOP, HOPD, DMAT, CALL, FIRST, DISS = 1.4, 0.9, 1.5, 0.2, 1.2, 0.1
+KNOB = {"list": 0.0, "sums": 0.0, "tables": 0.0, "late": True, "behind": False, "own": 0.0, "rank": "V", "pre": False,
+        "give": 1.0, "steps": (1.2, 0.6, 0.6, 0.3)}
+DIRECT = (0, 0, 256)
 TBV = 2304
-STAGE = False
-for _t in range(NR):
-    SCRATCH["dd%d" % _t] = ("dram", [8, 128, 1], F32)
+KS, KV = (288, 288, 288, 288), (320, 288, 288)
 
 
 def bits(engines):
     return sum(1 << e for e in engines)
 
 
-def helper_of(core, T, topo):
-    return [c for c in topo.cores_of(core) if T.rank_of(c) is None and topo.die(c) == topo.die(core)
-            and all(topo.may_write(c, d) for d in T.cores)][0]
-
-
-def helper_program(g, core, me, T, topo):
-    n = len(T.cores)
-    hc = T.cores[me]
-    peers = [(me + i) % n for i in range(1, n)]
-    engs = [e for e in topo.engines(core, T.cores[peers[0]]) if all(e in topo.engines(core, T.cores[r]) for r in peers)]
-    off = [e for e in topo.engines(hc, T.cores[peers[0]]) if all(e in topo.engines(hc, T.cores[r]) for r in peers)]
-    spare = [e for e in topo.engines(hc, core) if e not in off]
-    for t in VIA:
-        tr = []
-        for i, r in enumerate(peers):
-            rid, pid = topo.addr(T.cores[r], core)
-            tr.append(RemoteDMATransfer(dst_ids=[DstId(rid=rid, pnc=pid)], dma_engine_mask=1 << engs[i], remote_sem=T.sem["s%d" % t],
-                                        src=T.sb9[:, 72 * t + 9 * r:72 * t + 9 * r + 9], dst=T.ld9[:, 72 * t + 9 * me:72 * t + 9 * me + 9]))
-        g.wait_ge(T.sem["h%d" % t], len(spare))
-        g.remote_dma_fused(tr, local_sem=T.sem.sent)
-    if VIA:
-        g.wait_ge(T.sem.sent, len(VIA) * (n - 1))
-
-
 def rank_program(g, core, T, topo):
     me = T.rank_of(core)
     if me is None:
-        for r, c in enumerate(T.cores):
-            if core in topo.cores_of(c) and helper_of(c, T, topo) == core:
-                helper_program(g, core, r, T, topo)
         return
     n = len(T.cores)
     A, AX, AF = AluOpType, AxisListType.X, ActivationFunctionType
@@ -111,6 +87,9 @@ def rank_program(g, core, T, topo):
         if name in PLACE:
             return ("small", c0 + PLACE[name], c1 + PLACE[name], step, p0, p1)
         return (name, c0, c1, step, p0, p1)
+
+    def top(x):
+        return x[:4] + (0, 16)
 
     def ind(win, off):
         return ("#", win, off)
@@ -130,8 +109,9 @@ def rank_program(g, core, T, topo):
             return 16 * (x[2][2] - x[2][1])
         return (x[2] - x[1] + x[3] - 1) // x[3]
 
-    def add(eng, fn, reads, writes, cost, lat=0.07, kind="c", extra=None):
+    def add(eng, fn, reads, writes, cost, lat=None, kind="c", extra=None):
         k = len(ops)
+        lat = LAT if lat is None else lat
         deps = {}
         rl, wl = [], []
         for x in reads:
@@ -160,53 +140,61 @@ def rank_program(g, core, T, topo):
         if extra is not None:
             deps[extra] = True
         ops.append({"eng": eng, "fn": fn, "deps": sorted(deps), "cost": cost, "lat": lat, "kind": kind, "tag": writes[0][:2] if writes else "",
-                    "ord": [after[eng]] if eng in after else []})
+                    "ord": [after[eng]] if eng in after else [], "bias": 0.0})
         return k
 
-    def vcost(out, ins, two=False):
+    def short(x):
+        return x[0] != "#" and SCRATCH[x[0]][2] in (BF, F16, U16)
+
+    def vcost(out, x, per=1.0, fix=0.05):
         m = width(out)
-        c = 2.0 if two else 1.0
         if out[0] == "#":
-            c = 3.0
-        for x in ins:
-            if isinstance(x, tuple) and x[0] == "#":
-                c = max(c, 1.6)
-        return 0.06 + max(m * c - 40, 0) * 0.001
+            return fix + m * SCA * CYC
+        if x[0] == "#":
+            return fix + m * max(GAT, per) * CYC
+        return max(m * per, 64) * CYC + (SFIX if fix > 0.05 else 0.0)
 
     def cp(out, x):
-        add("V", lambda: g.vector.tensor_copy(ap(out), ap(x)), [x], [out], vcost(out, [x]))
+        add("V", lambda: g.vector.tensor_copy(ap(out), ap(x)), [x], [out], vcost(out, x, 0.5 if short(out) and short(x) else 1.0))
 
     def tt(out, x, y, op):
         two = x[0] not in BANKS and y[0] not in BANKS
-        add("V", lambda: g.vector.tensor_tensor(ap(out), ap(x), ap(y), op), [x, y], [out], vcost(out, [x], two))
+        add("V", lambda: g.vector.tensor_tensor(ap(out), ap(x), ap(y), op), [x, y], [out], vcost(out, x, 2.0 if two else 1.0))
 
     def ts(out, x, s1, op0, s2=None, op1=None):
         if op1 is None:
             fn = lambda: g.vector.tensor_scalar(ap(out), ap(x), val(s1), None, op0)
         else:
             fn = lambda: g.vector.tensor_scalar(ap(out), ap(x), val(s1), val(s2), op0, op1)
-        add("V", fn, [x, s1, s2], [out], vcost(out, [x]))
+        add("V", fn, [x, s1, s2], [out], vcost(out, x, 0.5 if short(out) and short(x) else 1.0))
 
     def red(out, x, op, ab=False):
         if ab:
             fn = lambda: g.vector.tensor_reduce(ap(out), ap(x), AX, op, apply_absolute_value=True)
         else:
             fn = lambda: g.vector.tensor_reduce(ap(out), ap(x), AX, op)
-        add("V", fn, [x], [out], vcost(x, []))
+        add("V", fn, [x], [out], vcost(x, x))
+
+    def scan(out, d0, d1):
+        add("V", lambda: g.vector.tensor_tensor_scan(ap(out), ap(d0), ap(d1), 0.0, A.mult, A.add), [d0, d1], [out], vcost(out, d0))
+
+    def turn(out, x):
+        add("V", lambda: g.vector.transpose(ap(out), ap(x)), [x], [out], vcost(out, x))
 
     def fill(out, c):
-        add("V", lambda: g.vector.memset(ap(out), c), [], [out], vcost(out, []) * (0.5 if SCRATCH[out[0]][2] == BF else 1.0))
+        add("V", lambda: g.vector.memset(ap(out), c), [], [out], vcost(out, out, 0.5 if short(out) else 1.0))
 
     def act(out, x, scale=None):
         if scale is None:
             fn = lambda: g.scalar.activation(ap(out), ap(x), AF.Copy)
         else:
             fn = lambda: g.scalar.activation(ap(out), ap(x), AF.Copy, scale=scale)
-        add("S", fn, [x], [out], vcost(out, [x]) + 0.02)
+        add("S", fn, [x], [out], vcost(out, x, 1.0, 0.065))
 
-    def lin(out, x, scale, bias):
-        add("S", lambda: g.scalar.activation(ap(out), ap(x), AF.Identity, bias=val(bias), scale=val(scale)), [x, scale, bias], [out],
-            vcost(out, [x]) + 0.02)
+    def lin(out, x, scale, bias, func=None, total=None):
+        more = {} if total is None else {"accum_out": ap(total)}
+        add("S", lambda: g.scalar.activation(ap(out), ap(x), func or AF.Identity, bias=val(bias), scale=val(scale), **more),
+            [x, scale, bias], [out] + ([total] if more else []), vcost(out, x, 1.0, 0.065) + (0.02 if more else 0.0))
 
     def mm(items):
         def fn():
@@ -214,9 +202,9 @@ def rank_program(g, core, T, topo):
             for (o, l, rr, st, sp) in items:
                 r = g.tensor.matmul(ap(o), ap(l), ap(rr), st, sp)
             return r
-        cost = 0.03
+        cost = 0.0
         for (o, l, rr, st, sp) in items:
-            cost += max(min(64, width(l)), width(rr)) * (4 if SCRATCH[l[0]][2] == F32 else 1) * 0.0006
+            cost += max(min(64, width(l)), width(rr)) * (4 if SCRATCH[l[0]][2] == F32 else 1) * PEC
         add("P", fn, [x for it in items for x in it[1:3]], [it[0] for it in items], cost)
 
     def iota(out, pat, base, cm):
@@ -224,7 +212,7 @@ def rank_program(g, core, T, topo):
             fn = lambda: g.iota(ap(out), pat, base, cm)
         else:
             fn = lambda: g.iota(ap(out), pat, base, cm, allow_small_or_imprecise_dtypes=True)
-        add("G", fn, [], [out], 0.13 + width(out) * 0.002)
+        add("G", fn, [], [out], 0.13 + width(out) * 2 * CYC)
 
     nd = [0]
 
@@ -236,16 +224,13 @@ def rank_program(g, core, T, topo):
         def fn():
             for (o, i) in pairs:
                 q.dma_start(o, i).then_inc(sem, 16)
-        k = add(eng, fn, reads, writes, 0.1 * len(pairs), lat, "d")
+        k = add(eng, fn, reads, writes, DISS * len(pairs), lat, "d")
         ops[k]["sem"] = (sem, 16 * len(pairs))
 
     peers = [(me + i) % n for i in range(1, n)]
     engs = topo.engines(core, T.cores[peers[0]])
     for r in peers:
         engs = [e for e in engs if e in topo.engines(core, T.cores[r])]
-    full = 0
-    for e in engs:
-        full += 1 << e
     dst = {}
     for r in peers:
         rid, pid = topo.addr(T.cores[r], core)
@@ -253,80 +238,86 @@ def rank_program(g, core, T, topo):
     na = [0]
     sent = [0]
 
-    def hop(srcs, dsts, reads, lands, spread, lat):
+    def arrive(k, lands, lat, cnt):
         sem = T.sem["a%d" % na[0]]
         na[0] += 1
-        if spread:
-            calls, i0, cnt = [], 0, 0
-            for many in (4, 2, 1):
-                per = len(engs) // many
-                calls.append([RemoteDMATransfer(dst_ids=[dst[peers[i0 + i]]], dma_engine_mask=bits(engs[i * per:(i + 1) * per]),
-                                                remote_sem=sem, src=srcs(peers[i0 + i]), dst=dsts) for i in range(many)])
-                i0 += many
-                cnt += many * per
-            sent[0] += cnt
-
-            def fn():
-                for tr_ in calls:
-                    g.remote_dma_fused(tr_, local_sem=T.sem.sent)
-            k = add("G", fn, reads, [], 0.8, 0.0, "r")
-            k2 = add("X", None, [], lands, 0.0, lat, "a", extra=k)
-            ops[k2]["sem"] = (sem, cnt)
-            return
-        else:
-            tr = [RemoteDMATransfer(dst_ids=[dst[r] for r in peers], dma_engine_mask=full, remote_sem=sem, srcs=[srcs],
-                                    dsts=[dsts for r in peers])]
-            cnt = (n - 1) * len(engs)
-            sent[0] += len(engs)
-        k = add("G", lambda: g.remote_dma_fused(tr, local_sem=T.sem.sent), reads, [], 0.8, 0.0, "r")
         k2 = add("X", None, [], lands, 0.0, lat, "a", extra=k)
         ops[k2]["sem"] = (sem, cnt)
 
-    def by_helper(t, lat):
-        hc = helper_of(core, T, topo)
-        spare = [e for e in topo.engines(core, hc) if e not in engs]
-        rid, pid = topo.addr(hc, core)
-        piece = T.sb9[:, 72 * t:72 * t + 72]
-        sent[0] += len(spare)
-        k = add("G", lambda: g.remote_dma(piece, piece, T.sem["h%d" % t], T.sem.sent, pid, rid, bits(spare)),
-                [b("sb9", 72 * t, 72 * t + 72)], [], 0.8, 0.0, "r")
-        k2 = add("X", None, [], others("ld9", 72 * t, 9), 0.0, lat, "a", extra=k)
-        ops[k2]["sem"] = (T.sem["s%d" % t], n - 1)
+    def spread(src, land, w, early, more=()):
+        sems = [T.sem["a%d" % na[0]], T.sem["a%d" % (na[0] + (1 if early else 0))]]
+        calls, i0 = [], 0
+        for many in (4, 2, 1):
+            per = len(engs) // many
+            calls.append([RemoteDMATransfer(dst_ids=[dst[peers[i]]], dma_engine_mask=bits(engs[(i - i0) * per:(i - i0 + 1) * per]),
+                                            remote_sem=sems[min(i0, 1)], src=ap(src(i)),
+                                            dst=ap(b(land[0], land[1] + i * w, land[1] + (i + 1) * w))) for i in range(i0, i0 + many)])
+            i0 += many
+        sent[0] += 3 * len(engs)
+        k1 = add("G", lambda: g.remote_dma_fused(calls[0], local_sem=T.sem.sent), [src(i) for i in range(4)] + list(more), [], CALL, 0.0, "r")
 
-    def others(name, base, w):
-        return [b(name, base + r * w, base + (r + 1) * w) for r in peers]
+        def fn():
+            for tr_ in calls[1:]:
+                g.remote_dma_fused(tr_, local_sem=T.sem.sent)
+        k2 = add("G", fn, [src(i) for i in range(4, 7)], [], 2 * CALL, 0.0, "r")
+        ops[k2]["ord"].append(k1)
+        if early:
+            more = FIRST if more else 0.0
+            arrive(k1, [b(land[0], land[1], land[1] + 4 * w)], HOP - 0.2 + more, len(engs))
+            arrive(k2, [b(land[0], land[1] + 4 * w, land[1] + 7 * w)], HOP - 0.1 + more, 2 * len(engs))
+        else:
+            arrive(k2, [b(land[0], land[1], land[1] + 7 * w)], HOP - 0.1, 3 * len(engs))
 
-    def gather_sum(f, land, base, w, own, thr, x, y):
-        o = b(f, me * w, (me + 1) * w)
+    def to_all(src, dsts, reads, lands, lat):
+        tr = [RemoteDMATransfer(dst_ids=[dst[r] for r in peers], dma_engine_mask=bits(engs), remote_sem=T.sem["a%d" % na[0]],
+                                srcs=[src], dsts=dsts)]
+        sent[0] += len(engs)
+        k = add("G", lambda: g.remote_dma_fused(tr, local_sem=T.sem.sent), reads, [], CALL, 0.0, "r")
+        arrive(k, lands, lat + 0.4, (n - 1) * len(engs))
+
+    def own_slot(f, w, own, thr):
+        o = b(f, 7 * w, 8 * w)
         cp(o, own)
-        for (c0, c1, th) in thr:
-            oo = b(f, me * w + c0, me * w + c1)
-            tt(oo, oo, th, A.subtract if me % 2 == 0 else A.add)
-        return o
+        tt(o, o, thr, A.subtract if me % 2 == 0 else A.add)
+
+    def compare(out, y, w):
+        ev_, od_ = b(y[0], y[1], y[1] + w), b(y[0], y[1] + w, y[1] + 2 * w)
+        if me % 2 == 0:
+            tt(out, od_, ev_, A.is_gt)
+        else:
+            tt(out, ev_, od_, A.is_gt)
 
     def finish_sum(f, land, base, w, x, y, out):
-        if me > 0:
-            cp(b(f, 0, me * w), b(land, base, base + me * w))
-        if me < n - 1:
-            cp(b(f, (me + 1) * w, n * w), b(land, base + (me + 1) * w, base + n * w))
+        cp(b(f, 0, 7 * w), b(land, base, base + 7 * w))
         tt(b(x[0], x[1], x[1] + 4 * w), b(f, 0, 4 * w), b(f, 4 * w, 8 * w), A.add)
         tt(b(y[0], y[1], y[1] + 2 * w), b(x[0], x[1], x[1] + 2 * w), b(x[0], x[1] + 2 * w, x[1] + 4 * w), A.add)
-        tt(out, b(y[0], y[1], y[1] + w), b(y[0], y[1] + w, y[1] + 2 * w), A.is_gt)
+        compare(out, y, w)
+
+    def to_list(bank, c0, rhs, mask):
+        mm([(b(bank, c0, c0 + 8, 1, 32 * (gr // 2), 32 * (gr // 2) + 32), b(mask, 16 - 16 * (gr % 2), 48 - 16 * (gr % 2)),
+             b(rhs, 8 * gr, 8 * gr + 8), gr % 2 == 0, gr % 2 == 1) for gr in range(8)])
 
     dma("Y", [(T.pas[:, :], T.pa[:, :])], [], [b("pas")])
     after["Y"] = last("Y")
-    dma("Y", [(T.cds[:, :], T.cd[:, :])], [], [b("cds")], 3.2)
+    dma("S", [(T["xs_"][:, :], T.xv[:, :])], [], [b("xs_")], 1.8)
+    after["S"] = last("S")
+    dma("Y", [(T.cds[:, :], T.cd[:, :])], [], [b("cds")], 2.6)
     after["Y"] = last("Y")
-    dma("S", [(T["xs_"][:, :], T.xv[:, :])], [], [b("xs_")], 3.2)
-    dma("Y", [(T.kcs[:, :], T.kc[:, :])], [], [b("kcs")], 4.8)
+    dma("Y", [(T.kcs[:, :], T.kc[:, :])], [], [b("kcs")], 4.2)
+    after["Y"] = last("Y")
     iota(b("ci", 0, 1), [[0, 1]], 0, 1)
     after["G"] = last("G")
     iota(b("lf", 0, 8), [[256, 8]], 0, 0)
     after["G"] = last("G")
     fill(b("tb", 0, TBV), 0)
     iota(b("tb", TBV, NC), [[0, NC - TBV]], 0, 0)
-    dma("Y", [(T.tb[0:128:16, :], T.bt[:, :]), (T.tb[1:128:16, :], T.co[:, :])], [], [b("tb")], 3.5)
-    dma("Y", [(T.tb[16 * h + 4:16 * h + 6, :], T.tb[16 * me:16 * me + 2, :]) for h in range(8)], [b("tb")], [b("tb")], 2.5)
+    rows = [(T.tb[8 * i + 4:8 * i + 5, :], (T.bt, T.co)[i % 2][me:me + 1, :]) for i in range(8)]
+    rows += [(T.tb[0:128:16, :], T.bt[:, :]), (T.tb[1:128:16, :], T.co[:, :])]
+    dma("Y", rows[:7], [b("tb")], [("tb4", 0, 1)])
+    after["Y"] = last("Y")
+    dma("S", rows[7:], [b("tb")], [("tb4", 1, 2)], 2.0)
+    tables_s = last("S")
+    dma("Y", [(T.tb[68:128:8, :], T.tb[4:64:8, :])], [("tb4", 0, 2)], [b("tb")])
 
     def col(i):
         return b("cf", i, i + 1)
@@ -337,245 +328,299 @@ def rank_program(g, core, T, topo):
     ts(b("ci", 1, 2), p_, 15, A.bitwise_and)
     ts(b("ci", 2, 3), p_, 4, A.arith_shift_right)
     ts(b("ci", 3, 4), p_, 7, A.bitwise_and)
-    ts(b("ci", 4, 5), p_, 3, A.arith_shift_right)
-    ts(b("ci", 5, 6), p_, 4, A.arith_shift_right, 1, A.bitwise_and)
-    ts(b("ci", 6, 7), p_, 4, A.arith_shift_right, BLK // 16 - 1, A.bitwise_and)
-    ts(b("ci", 7, 8), p_, 3, A.arith_shift_right, 1, A.bitwise_and)
-    ts(b("ci", 8, 9), p_, 1, A.bitwise_and)
-    ts(b("ci", 9, 10), p_, 1, A.arith_shift_right, 7, A.bitwise_and)
-    cp(b("cf", 0, 10), b("ci", 0, 10))
-    cP, cB, cG, cP7, cP3, cA2, cAn, cB3, cB0, cB1 = [col(i) for i in range(10)]
-    ts(cg(0), cB, 8.0, A.mult, cG, A.add)
-    ts(cg(1), cB0, 8.0, A.mult, cG, A.add)
+    ts(b("ci", 4, 5), p_, 4, A.arith_shift_right, 1, A.bitwise_and)
+    ts(b("ci", 5, 6), p_, 3, A.arith_shift_right, 1, A.bitwise_and)
+    ts(b("ci", 6, 7), p_, 1, A.bitwise_and)
+    ts(b("ci", 7, 8), p_, 1, A.arith_shift_right, 7, A.bitwise_and)
+    ts(b("ci", 8, 9), p_, 3, A.arith_shift_right)
+    cp(b("cf", 0, 9), b("ci", 0, 9))
+    cP, cB, cG, cP7, cA, cB3, cB0, cB1, cP3 = [col(i) for i in range(9)]
+    lin(cg(0), cB, 8.0, cG)
+    lin(cg(1), cB0, 8.0, cG)
     ts(cg(2), cB, 16.0, A.mult, cG, A.add)
-    ts(cg(3), cAn, 16.0, A.mult)
-    ts(cg(4), cB, float(BLK), A.mult, cg(3), A.add)
-    ts(cg(5), cP, float(-16 * me), A.add)
-    ts(cg(6), cA2, -1.0, A.mult, 1.0, A.add)
+    lin(cg(3), cA, 16.0, 0.0)
+    lin(cg(4), cB, float(BLK), cg(3))
     ts(cg(7), cP, 0.0, A.is_equal)
-    ts(cg(8), cG, 9.0, A.mult, 8.0, A.add)
-    ts(cg(9), cG, 2.0, A.mult, -63.0, A.add)
-    ts(cg(10), cB, 16.0, A.mult, cg(9), A.add)
+    lin(cg(8), cG, 9.0, 8.0)
+    lin(cg(9), cG, 2.0, 1.0)
     ts(cg(11), cg(2), 8.0, A.add)
-    ts(cg(12), cg(5), 9.0, A.mult, 8.0, A.add)
-    iota(b("iv", 0, 128), [[1, 128]], 0, 0)
-    iota(b("iv", 128, NV), [[1, NV - 128]], 128, 0)
-    iota(b("rb"), [[0, 16], [1, 16]], 0, 0)
-    iota(b("rg"), [[1, 8], [0, 16]], 0, 0)
-    iota(b("r8"), [[0, 8], [1, 8]], 0, 0)
-    iota(b("lf", 16, 32), [[1, 8], [8, 2]], 0, 0)
-    iota(b("lf", 32, 36), [[2, 4]], 0, 0)
+    iota(b("iv"), [[1, 384]], 0, 0)
+    iota(b("rb"), [[0, 8], [1, 16]], 0, 0)
+    iota(b("r8"), [[0, 10], [1, 8]], 0, 0)
+    iota(b("kk"), [[0, 2], [1, 8], [8, 2]], 0, 0)
+    iota(b("lf", 32, 37), [[2, 5]], 0, 0)
     iota(b("lf", 40, 48), [[16, 8]], NV, 0)
     iota(b("jt"), [[128, 8]], 0, 1)
     xoA, xoB, sel = b("lst", 0, 8), b("lst", 8, 16), b("lst", 16, 32)
-    gl, gl2, l1, l2, ly, lq = b("lst", 32, 40), b("lst", 40, 48), b("lst", 48, 49), b("lst", 50, 51), b("lst", 52, 56), b("goff")
-    lq = b("pu", 112, 128)
+    gl2, ly, lcm, lov = b("lst", 40, 48), b("lst", 56, 61), b("lst", 62, 63), b("lst", 48, 49)
+    lso, lpa, lyc, ldup, lpo = b("lst", 64, 68), b("lst", 68, 72), b("lst", 72, 76), b("lst", 76, 80), b("lst", 80, 81)
+    lv2, lA, lB = b("lst", 82, 90), b("lst", 96, 112), b("lst", 112, 128)
     ts(xoA, b("lf", 0, 8), cg(2), A.add)
     ts(xoB, b("lf", 0, 8), cg(11), A.add)
-    ts(sel, b("lf", 16, 32), cg(4), A.add)
-    cp(gl, b("iv", 0, 8))
-    cp(gl2, b("iv", 0, 8))
-    fill(b("lst", 40 + me, 41 + me), 8)
-    gl4, gl5, l5 = b("lst", 56, 64), b("lst", 64, 72), b("lst", 72, 73)
-    ts(gl4, b("iv", 0, 8), 2.0, A.mult)
-    fill(b("lst", 56 + me, 57 + me), 16)
-    ts(gl5, gl4, 1.0, A.add)
-    ts(cg(13), cP7, float(me), A.is_equal, float(16 - 2 * me), A.mult)
-    ts(cg(14), cP7, 2.0, A.mult, 1.0, A.add)
-    ts(l5, cg(14), cg(13), A.add)
+    ts(sel, b("kk", 2 * me + 2, 2 * me + 18), cg(4), A.add)
+    i8 = b("iv", 0, 8)
+    ts(b("la", 0, 8), i8, float(me), A.is_equal, float(8 - me), A.mult)
+    tt(b("la", 0, 8), b("la", 0, 8), i8, A.add)
+    cp(gl2, b("la", 0, 8))
+    ts(cg(6), cB, 2.0, A.is_equal)
+    ts(b("lf", 64, 72), b("la", 0, 8), -12.0, A.add, cg(6), A.mult)
+    ts(lv2, b("lf", 64, 72), 12.0, A.add)
+    ts(cg(10), cP7, cG, A.is_equal)
+    lin(b("la", 8, 12), b("lf", 32, 36), 1.0, cB3)
+    lin(b("lf", 80, 84), b("la", 8, 12), 3.0, -22.0)
+    ts(lso, b("lf", 80, 84), cg(10), A.mult, 24.0, A.add)
+    lin(b("lf", 84, 88), b("la", 8, 12), 1.0, -8.0)
+    ts(lyc, b("lf", 84, 88), cg(10), A.mult, 8.0, A.add)
+    lin(cg(12), cP7, 1.0, -8.0)
+    ts(b("lf", 88, 92), b("la", 8, 12), cG, A.is_equal, cg(12), A.mult)
+    ts(lpa, b("lf", 88, 92), 8.0, A.add)
+    cp(b("lst", 56, 60), b("la", 8, 12))
+    fill(b("lst", 60, 61), 8)
+    ts(b("la", 12, 16), b("iv", 0, 4), 1.5, A.is_gt, 16.0, A.mult)
+    ts(ldup, b("la", 12, 16), cB, A.add)
+    l1, l2 = b("lst", 32, 33), b("lst", 34, 36)
     cp(l1, cP)
-    cp(l2, cg(0))
-    ts(ly, b("lf", 32, 36), cB3, A.add)
-    cp(lq, b("iv", 16, 32))
-    ts(b("dump"), b("lf", 40, 48), cB, A.add)
+    ts(l2, b("iv", 0, 2), 0.0, A.mult, cg(0), A.add)
+    lin(cg(5), cP, 1.0, float(-16 * me))
+    ts(b("rep"), b("rb"), cg(5), A.is_equal)
+    ts(lpo, cP7, 8.0, A.mult, cG, A.add)
+    ts(lov, cG, 8.0, A.mult, cP7, A.add)
+    lin(b("dump"), b("lf", 40, 48), 1.0, cB)
     i128, rb128 = b("iv", 0, 128), b("rb", 0, 128)
     ts(b("m1"), rb128, cg(1), A.is_equal)
-    ts(b("r1"), b("iv", 0, 8), cB1, A.is_equal)
-    ts(b("mr2"), rb128, 2.0, A.is_equal)
+    ts(b("r1"), i8, cB1, A.is_equal)
     ts(b("pm"), i128, cg(0), A.is_equal)
-    ts(b("mi"), b("rb"), cB, A.is_equal)
-    ts(b("r2"), b("iv", 0, 8), cG, A.is_equal)
-    ts(b("bi"), b("iv", 0, 8), cG, A.is_equal)
-    ts(b("bd"), b("rg"), cG, A.is_equal)
-    ts(b("rep"), rb128, cg(5), A.is_equal)
-    ts(b("tri"), b("rb"), cB, A.is_lt, -0.5, A.mult)
-    ts(b("idb"), i128, cP, A.is_equal)
+    ts(b("m2"), rb128, cB, A.is_equal)
+    ts(b("bi"), i8, cG, A.is_equal)
+    ts(b("idh"), i128, cP, A.is_equal)
+    fill(b("one"), 1.0)
     ts(b("mr3"), rb128, 3.0, A.is_equal, cg(7), A.mult)
+    lin(b("mr3", 7, 128, 16), b("iv", 0, 8), 0.0, cg(7))
+    ts(b("mr6"), rb128, 6.0, A.is_equal)
+    cp(b("m2h"), b("m2"))
     for t in range(NR - 1):
         ts(b("pnl", 16 * t + 8, 16 * t + 16), b("dump"), float(NL * (t + 1) - NV), A.add)
-    cp(b("pnl", 0, 8), b("pas", 8, 16))
-    ts(b("rs"), b("rb"), 0.5, A.is_gt)
-    ts(b("bigu"), i128, cP, A.is_ge, BIG, A.mult)
-    ts(b("mq"), b("iv", 0, 16), cP3, A.is_equal)
-    ts(b("ma"), b("rg"), cP7, A.is_equal)
+    ts(b("bigu"), i128, cg(0), A.is_ge, BIG, A.mult)
     ts(b("m3"), b("r8"), cG, A.is_equal)
     ts(b("z9"), b("iv", 0, 80), cg(8), A.is_equal)
-    ts(b("z2", 0, 33), b("iv", 0, 33), cg(10), A.is_equal)
-    ts(b("zi"), b("iv", 0, 72), cg(11), A.is_equal)
-    ts(b("zo", 0, 44), b("iv", 0, 44), cg(12), A.is_equal)
-    if STAGE:
-        tt(b("m1"), b("bd"), b("mr2"), A.mult)
-    m2, mb = b("mi", 0, 128), b("mi", 0, 16)
+    ts(b("zi"), b("iv", 0, 136), cg(11), A.is_equal)
+    ts(b("mzf"), b("iv", 0, 48), -16.0, A.add, cB, A.is_equal)
+    cp(b("mz"), b("mzf"))
+    lin(b("sg", 1, 2), cP7, 16.0, cP3)
+    ts(b("pmt"), i128, b("sg", 1, 2), A.is_equal)
+    lin(b("sg", 2, 3), cB, 4.0, -16.0)
+    lin(b("sg", 3, 4), b("sg", 2, 3), 1.0, cg(9))
+    ts(b("sg", 4, 5), cP7, 4.0, A.is_equal)
+    ts(b("z2", 0, 65), b("iv", 0, 65), b("sg", 3, 4), A.is_equal, b("sg", 4, 5), A.mult)
+    act(b("e2", 0, 49), b("z2", 0, 49))
+    tt(b("z2", 16, 65), b("z2", 16, 65), b("e2", 0, 49), A.add)
+    ts(b("mk", 0, 2), b("iv", 0, 2), cA, A.not_equal, 1000.0, A.mult)
+    ts(b("mk", 2, 4), b("mk", 0, 2), 4223.5, A.add)
+    ts(b("lf", 48, 64), b("iv", 0, 16), cB, A.is_gt, 32.0, A.mult)
+    ts(b("sg", 6, 7), cB, cg(3), A.add)
+    ts(lA, b("lf", 48, 64), b("sg", 6, 7), A.add)
+    ts(lB, b("iv", 0, 16), cg(3), A.add)
+    iota(b("rs"), [[0, 16], [1, 16]], 0, 0)
+    lin(b("rs"), b("rs"), 1.0, 0.0, AF.Sign)
+    mb = b("mz", 16, 32)
     fill(b("xm", 0, NV), 0.0)
     act(b("xm", NV, 2 * NV), b("xs_"), 0.0)
-    fill(b("ld2"), 0.0)
+    for c in range(0, 1152, 288):
+        for name in ("kt", "it", "ito"):
+            lin(b(name, c, c + 288), b("xs_", 0, 288), 0.0, -1.0)
+            ops[-1]["ord"].append(tables_s)
+    for name in ("ld2", "d0", "w3", "yw", "w9", "sdo", "paf"):
+        fill(b(name), 0.0)
     cp(b("so", 0, 8), b("pas", 0, 8))
-    cp(b("sl", 0, 8), b("pas", 0, 8))
+    tt(b("tg", 0, 8), b("pas", 0, 8), b("dump"), A.subtract)
     cp(b("pl0"), b("pas"))
     xv, kc = b("xs_"), b("kcs")
-    for h in range(2):
-        act(b("ia", 512 * h, 512 * h + 512), ind(b("iv"), b("pl0", 32 * h, 32 * h + 32)))
-    mm([(b("pg", 0, 9), b("ia", 128 * y, 128 * y + 128), b("zo", 8 - y, 17 - y), y == 0, y == 7) for y in range(8)])
-    act(b("po"), b("pg", 0, 8))
 
-    nl = BLK // 16
+    def own_parents():
+        mm([(b("pg", 256, 320), top(b("m2h")), top(b("ph")), True, True)])
+        act(b("px"), b("pg", 256, 320))
+        act(b("po"), ind(b("px"), lpo))
+        cp(b("sw", 24, 40), ind(b("px"), lov))
+
+    def swap_tables(t, scol):
+        cp(b("si", 0, 1), scol)
+        ts(b("si", 1, 2), b("si", 0, 1), 4, A.arith_shift_right)
+        ts(b("si", 2, 3), b("si", 0, 1), 15, A.bitwise_and)
+        cp(b("sc", 8, 10), b("si", 1, 3))
+        ts(b("ohb", 16 * t, 16 * t + 16), b("iv", 0, 16), b("sc", 9, 10), A.is_equal)
+        ts(b("oha"), b("iv", 0, 64), b("sc", 8, 9), A.is_equal)
+        mm([(top(b("pg", 320, 448)), b("ohb", 16 * t, 16 * t + 16), b("idh"), True, True)])
+        cp(top(b("obt")), top(b("pg", 320, 448)))
+        ts(b("oh2", 128 * t, 128 * t + 64), b("oha"), -2048.0, A.mult)
+        ts(b("oh2", 128 * t + 64, 128 * t + 128), b("oha"), b("jt", t, t + 1), A.mult)
+
+    def grandparents(t, scol):
+        mm([(b("pg", 448, 512), top(b("obt")), top(b("ph")), True, True)])
+        tt(b("ux"), b("pg", 448, 512), b("oha"), A.mult)
+        red(b("up", 0, 1), b("ux"), A.add)
+        if t > 0:
+            ts(b("uh"), b("bi"), b("up", 0, 1), A.mult)
+            mm([(top(b("pg", 192, 200)), mb, b("uh"), True, True)])
+            cp(top(b("pu", 64, 72)), top(b("pg", 192, 200)))
+        ts(b("sdo", 40, 41), b("up", 0, 1), scol, A.subtract)
+    cp(b("rh2", 0, 64), b("pas"))
+    mm([(top(b("pg", 0, 64)), b("idh", 16 * me, 16 * me + 16), b("rh2", 0, 64), True, True)])
+    cp(top(b("ph")), top(b("pg", 0, 64)))
+    own_parents()
+    swap_tables(0, b("po", 0, 1))
+    grandparents(0, b("po", 0, 1))
+
     nb = 128 // BLK
-    half = 8 * BLK
     cp(ind(b("xm"), xoA), b("xs_", 0, NL))
-    late = []
+    late, lists = [], []
     for t in range(NR):
-        so, sl, pl = b("so", 8 * t, 8 * t + 8), b("sl", 8 * t, 8 * t + 8), b("pl%d" % t)
-        after.clear()
+        so = b("so", 8 * t, 8 * t + 8)
+        scol = b("po", 0, 1) if t == 0 else b("w3", 3 * me + 2, 3 * me + 3)
+        after.pop("V", None)
+        after.pop("S", None)
         cp(b("cut"), ind(b("cds"), so))
         act(b("xg"), ind(xv, so))
-        cp(ind(b("xm"), xoB), b("xg"))
-        for c in range(8):
-            o = b("kg", 256 * c, 256 * c + 256)
-            i = ind(kc, b("cut", 16 * c, 16 * c + 16))
-            (act if c % 2 == 0 else cp)(o, i)
-            after["SV"[c % 2]] = len(ops) - 1
-            its = []
-            for m in range(256 // BLK * c, 256 // BLK * (c + 1)):
-                q, blk = m // nb, m % nb
-                c0 = (q % 12) * BLK
-                its.append((b("pa%d" % (q // 12), c0, c0 + BLK, 1, blk * BLK, blk * BLK + BLK), b("kg", m * BLK, m * BLK + BLK),
-                            b("xm", m * BLK, m * BLK + BLK), True, True))
-            mm(its)
-        after["V"] = last("V")
-        cp(b("cs", 0, 128), b("cut"))
-        act(b("cs", 128, 256), ind(b("iv"), so))
-        after["S"] = last("S")
-        act(b("ev", 0, 12 * BLK), b("pa0", 0, 12 * BLK))
-        cp(b("ev", 12 * BLK, 16 * BLK), b("pa1", 0, 4 * BLK))
-        B1 = 256 * t
-        ts(b("sb1", B1, B1 + 256), ind(b("ev"), sel), sgn, A.mult, OFF, A.add)
-        hop(lambda r: T.sb1[:, B1 + 32 * r:B1 + 32 * r + 32], T.ld1[:, B1 + 32 * me:B1 + 32 * me + 32],
-            [b("sb1", B1, B1 + 256), b("ld2")] if t == 0 else [b("sb1", B1, B1 + 256)], others("ld1", B1, 32), True, HOP)
-        for q in "VSGP":
-            after[q] = last(q)
-        for k in late:
-            ops[k]["ord"].append(after["V"])
         if t == 0:
-            iota(b("kt"), [[0, 1152]], 0, 0)
-            iota(b("it"), [[0, 1152]], -1, 0)
+            ops[tables_s]["ord"].append(last("S"))
+            after["S"] = tables_s
+        cp(ind(b("xm"), xoB), b("xg"))
+        c0, pieces = 0, []
+        for i in range(len(KS)):
+            pieces += [("S", KS[i])] + ([("V", KV[i])] if i < len(KV) else [])
+        for (e, w) in pieces:
+            (act if e == "S" else cp)(b("kg", c0, c0 + w), ind(kc, b("cut", c0 // 16, (c0 + w) // 16)))
+            after[e] = len(ops) - 1
+            its = []
+            for m in range(c0 // BLK, (c0 + w) // BLK):
+                q, blk = m // nb, m % nb
+                its.append((b("pa%d" % (q // 8), (q % 8) * BLK, (q % 8 + 1) * BLK, 1, blk * BLK, blk * BLK + BLK),
+                            b("kg", m * BLK, m * BLK + BLK), b("xm", m * BLK, m * BLK + BLK), True, True))
+            mm(its)
+            c0 += w
+        act(b("ev", 0, 256), b("pa0", 0, 256))
+        cp(b("ev", 256, 512), b("pa1", 0, 256))
+        B1 = 256 * t
+        for h in range(2):
+            ts(b("sb1", B1 + 128 * h, B1 + 128 * h + 128), ind(b("ev"), b("lst", 16 + 8 * h, 24 + 8 * h)), sgn, A.mult, OFF, A.add)
+            after["V"] = last("V")
+        spread(lambda i: b("sb1", B1 + 32 * i, B1 + 32 * i + 32), ("ld1", B1), 32, True, [b("ld2")] if t == 0 else [])
+        lanes_end = last("V")
+        for k in late:
+            ops[k]["ord"].append(lanes_end)
+        after.pop("V", None)
+        after.pop("S", None)
 
-        mm([(b("pb", 0, 128), b("rep"), b("cs", 0, 128), True, True)])
-        act(b("ec", 0, 128), b("pb", 0, 128))
-        mm([(b("pd", 128, 256), b("rep"), b("cs", 128, 256), True, False), (b("pd", 128, 256), b("idb"), b("bigu"), False, True),
-            (b("pd", 256, 260), b("cs", 128, 256), b("zo", 8, 12), True, True)])
-        act(b("ec", 128, 256), b("pd", 128, 256))
-        act(b("sc", 0, 1), b("pd", 256, 257))
-        mm([(b("pc_", 0, 256), b("idb"), b("tri"), True, False)])
-        cp(b("goff"), ind(b("ec", 0, 128), l1))
-        cp(b("cq"), ind(b("ec", 0, 128), l2))
+        cp(b("cs"), b("cut"))
+        mm([(b("pb", 384, 512), b("rep"), b("cs"), True, True)])
+        act(b("ec"), b("pb", 384, 512))
+        cp(b("goff"), ind(b("ec"), l1))
+        after["V"] = lanes_end
         cp(b("gg"), ind(b("tb"), b("goff")))
-        mm([(b("pb", 128, 160), b("gg", 128 * h, 128 * h + 128), b("z2", 1 - h, 33 - h), h == 0, h == 1) for h in range(2)])
-        act(b("tw"), b("pb", 128, 160))
-        gather_sum("f1", "ld1", B1, 32, b("sb1", B1 + 32 * me, B1 + 32 * me + 32),
-                   [(0, 16, b("tw", 0, 16)), (16, 32, b("tw", 0, 16))], None, None)
-        tt(b("rw"), ind(b("tw"), lq), b("mi"), A.mult)
-        act(b("wo"), ind(b("tw"), lq))
-        mm([(b("pc_", 0, 256), b("bd"), b("rw"), False, True)])
-        tt(b("less"), b("pc_", 0, 256), b("wo"), A.is_lt)
-        add("V", lambda: g.vector.tensor_tensor_scan(ap(b("scan")), ap(b("rs")), ap(b("less")), 0.0, A.mult, A.add),
-            [b("rs"), b("less")], [b("scan")], 0.3)
-        scol = b("sc", 0, 1)
-        ts(b("e2"), b("ec", 128, 256), scol, A.is_equal)
-        red(b("sc", 1, 2), b("e2"), A.max)
-        cp(b("si", 0, 1), scol)
-        ts(b("si", 1, 2), b("si", 0, 1), 7, A.arith_shift_right)
-        ts(b("si", 2, 3), b("si", 0, 1), 127, A.bitwise_and)
-        cp(b("sc", 2, 4), b("si", 1, 3))
-        ts(b("sc", 4, 5), b("sc", 2, 3), float(t), A.is_equal, b("sc", 1, 2), A.max)
-        lin(b("bq"), b("mq"), b("sc", 4, 5), 0.0)
-        mm([(b("pb", 0, 16), b("ma"), b("bq"), True, True)])
-        lin(b("q1", 0, 16), b("pb", 0, 16), -1.0, 1.0)
-        ts(b("q1", 16, 32), b("scan", 15, 256, 16), -8192.0, A.mult, 131072.0, A.add)
-        tt(b("q1", 32, 48), b("q1", 16, 32), b("cq"), A.add)
-        tt(b("q1", 48, 64), b("q1", 32, 48), b("q1", 0, 16), A.mult)
-        qe = b("q1", 48, 64)
-        for h, mc in ((0, cg(6)), (1, cA2)):
-            ts(b("qq", 32 * h, 32 * h + 16), qe, 4096.0, A.add, mc, A.mult)
-            lin(b("qq", 32 * h + 16, 32 * h + 32), qe, mc, 0.0)
+        mm([(b("pb", 0, 64), b("gg", 128 * h, 128 * h + 128), b("z2", 1 - h, 65 - h), h == 0, h == 1) for h in range(2)])
+        turn(b("ct", 0, 32), b("pb", 32, 64))
+        own_slot("f1", 32, b("sb1", B1 + 224, B1 + 256), b("pb", 0, 32))
+        ts(b("ct", 32, 64), b("ct", 0, 32), -0.5, A.add)
+        act(b("wo"), ind(b("ct", 0, 32), lB))
+        tt(b("less"), ind(b("ct"), lA), b("wo"), A.is_lt)
+        scan(b("scan"), b("rs"), b("less"))
+        key, base = b("scan", 15, 256, 16), -16.0
+        cp(b("sh", 0, 1), scol)
+        ts(b("dg"), b("idh"), scol, A.mult)
+        mm([(b("pd", 0, 128), b("one"), b("dg"), True, False), (b("pd", 0, 128), b("idh"), b("bigu"), False, True),
+            (b("pd", 128, 129), b("pmt"), b("sh", 0, 1), True, True)])
+        s2 = b("sc", 0, 1)
+        act(s2, b("pd", 128, 129))
+        lin(b("e2"), b("pd", 0, 128), -1.0, s2, AF.Sign)
+        lin(b("e3"), b("e2"), 1.0, 0.0, AF.Square, b("sc", 1, 2))
+        lin(b("sc", 2, 3), s2, 1.0, -(NL * t + 63.5), AF.Square)
+        ts(b("sc", 3, 4), b("sc", 2, 3), 4096.0, A.min, b("sc", 1, 2), A.add)
+        ts(b("sc", 4, 6), b("mk", 2, 4), b("sc", 3, 4), A.is_lt, -8192.0, A.mult)
+        act(b("cq"), ind(b("ec"), l2))
+        for a in range(2):
+            ts(b("rm", 16 * a, 16 * a + 16), key, base, A.add, b("sc", 4 + a, 5 + a), A.mult)
+        turn(b("rt"), b("rm"))
+        tt(b("qq", 32, 64), b("rt"), b("cq"), A.add)
+        ts(b("qq", 0, 32), b("qq", 32, 64), 4096.0, A.add)
+        ops[-1]["bias"] = KNOB["tables"]
+        ts(b("dh"), b("m2h"), scol, A.mult)
+        mm([(b("pb", 72, 80), b("dh"), b("bi"), True, True)])
+        tt(b("tgo", 0, 8), b("pb", 72, 80), b("dump"), A.subtract)
 
-        finish_sum("f1", "ld1", B1, 32, ("x1", 0), ("y1", 0), b("sd"))
-        for h in range(2):
-            tt(b("mq2", 32 * h, 32 * h + 32), b("sd"), b("qq", 32 * h, 32 * h + 32), A.mult)
-        for h in range(2):
-            tt(b("v32", 16 * h, 16 * h + 16), b("mq2", 32 * h, 32 * h + 16), b("mq2", 32 * h + 16, 32 * h + 32), A.subtract)
-        add("V", lambda: g.vector.transpose(ap(b("t32")), ap(b("v32"))), [b("v32")], [b("t32")], 0.07)
-        B2, wd = (0, 16, 48)[t], (1, 1 if STAGE else 2, 1)[t]
-        own = B2 + 8 * wd
-        if wd == 2:
-            cp(b("ld2", own + 1, own + 2), b("po", t + 1, t + 2))
+        cp(b("f1", 0, 128), b("ld1", B1, B1 + 128))
+        tt(b("x1"), b("f1", 0, 64), b("f1", 64, 128), A.add)
+        tt(b("y1", 64, 96), b("x1", 32, 64), b("x1", 0, 32), A.subtract)
+        tt(b("f1", 224, 256), b("f1", 224, 256), b("y1", 64, 96), A.add)
+        cp(b("f1", 128, 224), b("ld1", B1 + 128, B1 + 224))
+        tt(b("y1", 0, 64), b("f1", 128, 192), b("f1", 192, 256), A.add)
+        compare(b("sd"), ("y1", 0), 32)
+        tt(b("mq"), ind(b("sd"), ldup), b("qq"), A.mult)
+        tt(b("v32"), b("mq", 0, 32), b("mq", 32, 64), A.subtract)
+        turn(b("t32"), b("v32"))
+        B2 = 16 * t
+        own = B2 + 8
         red(b("ld2", own, own + 1), b("t32"), A.max, True)
         after["V"] = last("V")
-        if STAGE:
-            dd = "dd%d" % t
-            for e in range(2):
-                dma("YS"[e], [(T[dd][me, 64 * e:64 * e + 64, :], T.ld2[e:128:2, own:own + 1])], [b("ld2", own, own + 1)],
-                    [(dd, 2 * me + e, 2 * me + e + 1)])
-            hop(T[dd][me], T[dd][me], [(dd, 2 * me, 2 * me + 2)], [(dd, 2 * r, 2 * r + 2) for r in peers], False, HOPD)
-            dma("Y", [(T.ld2[:, B2:B2 + 8], T[dd][:])], [(dd, 0, 16)], [b("ld2", B2, B2 + 8)])
-            if t == 1:
-                cp(b("pnl", 16, 24), b("pl1", 16, 24))
-        else:
-            hop(T.ld2[:, own:own + wd], T.ld2[:, B2 + me * wd:B2 + me * wd + wd], [b("ld2", own, own + wd)], [b("ld2", B2, own)], False, HOP)
-        win, glv = b("ld2", B2, own + 8), (gl2 if wd == 1 else gl4)
+        to_all(T.ld2[:, own:own + 1], [T.ld2[:, B2 + me:B2 + me + 1] for r in peers], [b("ld2", own, own + 1)], [b("ld2", B2, own)], HOP)
+        for k in lists:
+            ops[k]["ord"].append(last("G"))
+        win = b("ld2", B2, own + 8)
         if t < NR - 1:
             cp(ind(b("xm"), xoA), b("xs_", NL * t + NL, NL * t + 2 * NL))
 
-        ts(b("oh"), i128, b("sc", 3, 4), A.is_equal)
-        ts(b("yh"), b("iv", 0, 8), b("sc", 2, 3), A.is_equal)
-        lin(b("yh2", 0, 8), b("yh"), -BIG, 0.0)
-        lin(b("yh2", 8, 16), b("yh"), b("jt", t, t + 1), 0.0)
-        cp(b("smi"), b("ec", 128, 256))
-        ts(b("smj"), b("smi"), 127, A.bitwise_and)
-        ts(b("oht"), b("smj"), cP, A.is_equal)
-        mm([(b("pb", 0, 8), b("oht"), b("po"), True, True)])
-        tt(b("up", 0, 8), b("pb", 0, 8), b("yh"), A.mult)
-        red(b("up", 8, 9), b("up", 0, 8), A.add)
-        tt(b("tg", 0, 8), sl, b("dump"), A.subtract)
-        if t == NR - 1:
-            act(b("pa0", 0, 512), b("xs_", 512, NV))
-        if t != 1 or STAGE:
-            for h in range(2):
-                act(b("xp", 512 * h, 512 * h + 512), ind(xv, b("pl%d" % t, 32 * h, 32 * h + 32)))
+        mm([(top(b("pf_", 0, 64)), top(b("idh", 0, 16)), top(b("ph")), True, False)])
+        dec = b("ld2", own, own + 1)
+        ts(b("gmo"), b("m1"), dec, A.mult)
+        lin(b("gvo"), b("mr6"), dec, 0.0)
+        mm([(b("pb", 64, 72), b("gmo"), b("r1"), True, True)])
+        cp(b("lio", 0, 8), b("pb", 64, 72))
+        ts(b("tgo", 8, 16), b("pb", 64, 72), 8000.0, A.is_gt)
+        ts(b("lio", 8, 16), b("lio", 0, 8), 4095, A.bitwise_and)
+        tt(b("tgo", 16, 24), b("tgo", 8, 16), b("tgo", 0, 8), A.mult)
+        cp(b("sw", 8, 16), b("lio", 8, 16))
+        tt(b("tgo", 24, 32), b("tgo", 16, 24), b("dump"), A.add)
+        cp(b("sw", 16, 24), b("tgo", 24, 32))
+        mm([(b("pb", 256, 384), b("mr3"), b("iv", NL * t, NL * t + NL), True, False), (b("pb", 256, 384), b("gvo"), b("pm"), False, True)])
+        act(b("wvo"), b("pb", 256, 384))
+        tt(b("sro"), ind(b("tb"), b("sw", 8, 16)), b("wvo"), A.add)
+        cp(ind(b("ito"), b("sw", 16, 24)), b("sro"))
+        act(b("iao"), ind(b("ito"), b("sw", 24, 32)))
+        mm([(b("pg", 64, 128), b("iao"), b("zi", 72, 136), True, False), (b("pg", 64, 128), b("sro"), b("zi", 64, 128), False, True)])
+        act(b("eo"), b("pg", 64, 128))
+        cp(b("vo", 0, 9), b("eo", 32, 41))
+        ts(b("vo", 16, 25), b("vo", 0, 9), 12, A.arith_shift_right, 1, A.bitwise_and)
+        ts(b("sdo", 0, 8), b("eo", 48, 56), NL * t - 0.5, A.is_lt, 4.0, A.mult)
+        ts(b("sdo", 8, 9), b("eo", 40, 41), 8000.0, A.is_lt, 4.0, A.mult)
+        ts(b("sdo", 9, 10), b("eo", 48 + t, 49 + t), b("jt", t, t + 1), A.is_equal, 2.0, A.mult)
+        tt(b("sdo", 16, 25), b("vo", 16, 25), b("sdo", 0, 9), A.add)
+        lin(b("sdo", 16 + t, 17 + t), b("sdo", 16 + t, 17 + t), 1.0, b("sdo", 9, 10))
+        tt(b("sdo", 32, 40), b("eo", 48, 56), b("po", 0, 8), A.subtract)
+        tt(b("gd"), ind(b("sdo", 32, 48), ly), b("m3"), A.mult)
+        ops[-1]["bias"] = KNOB["own"]
+
+        for c in range(DIRECT[t], NV, 256):
+            act(b("pa0", c - 512, c - 256) if c >= 512 else b("pd", c - DIRECT[t], c - DIRECT[t] + 256), b("xs_", c, c + 256))
+        if t == 0:
+            for h in range(4):
+                act(b("xp", 256 * h, 256 * h + 256), ind(xv, b("pl0", 16 * h, 16 * h + 16)))
             act(b("xps"), ind(b("xp"), so))
+        else:
+            act(b("xps"), ind(xv, b("pl%d" % t, 64, 72)))
         if t < NR - 1:
             pn = b("pnl", 16 * t, 16 * t + 8)
             nx = NL * (t + 1)
+            pc = b("pc", 0, 8)
             act(b("xpn", 0, NL), b("xs_", nx, nx + NL))
-            if wd == 1:
-                pc = b("pc")
-                act(b("pn"), ind(b("iv"), pn))
-                mm([(b("pe", 64, 72), b("pn"), b("zi", 8, 16), True, True)])
-                act(pc, b("pe", 64, 72))
-                tt(b("gm3"), ind(pc, gl), m2, A.mult)
-            else:
-                pc = b("pc2", 0, 8)
-                tt(b("gm3"), ind(win, gl5), m2, A.mult)
-                mm([(b("pe", 64, 72), b("gm3"), b("r2"), True, True)])
-                cp(pn, b("pe", 64, 72))
+            cp(pn, b("pl%d" % t, 8 * t + 8, 8 * t + 16))
             act(b("xpn", NL, 2 * NL), ind(xv, pn))
-            mm([(b("pf_", 0, 8), b("gm3"), b("r2"), True, False)])
+            cp(b("paf", 0, 8), pn)
+            act(b("pz"), ind(b("paf"), lpa))
+            mm([(b("pe", 64, 128), b("m2"), b("pz"), True, True)])
+            act(b("py"), b("pe", 64, 128))
+            act(b("pc"), ind(b("py"), lpo))
 
-        if STAGE:
-            lv = b("ld2", B2, B2 + 8)
-        else:
-            lv = b("pd", 0, 8)
-            tt(b("gm"), ind(win, glv), b("m1"), A.mult)
-            mm([(lv, b("gm"), b("r1"), True, True)])
+        lv = b("pa1", 0, 8)
+        tt(b("gm"), ind(win, gl2), b("m1"), A.mult)
+        mm([(lv, b("gm"), b("r1"), True, True)])
         cp(b("li", 0, 8), lv)
         ts(b("tg", 8, 16), lv, 8000.0, A.is_gt)
         ts(b("li", 8, 16), b("li", 0, 8), 4095, A.bitwise_and)
@@ -585,126 +630,109 @@ def rank_program(g, core, T, topo):
         cp(b("tgt"), b("tg", 24, 32))
         act(b("kcc"), ind(kc, b("cl")))
         cp(ind(b("kt"), b("tgt")), b("kcc"))
-        if STAGE:
-            tt(b("gv"), ind(lv, gl), m2, A.mult)
-            pair = (b("m1"), b("gv"))
-        else:
-            tt(b("gv"), ind(win, glv), b("mr2"), A.mult)
-            pair = (b("gv"), b("pm"))
-        mm([(b("pa1", 128, 256), b("mr3"), b("iv", NL * t, NL * t + NL), True, False)])
-        mm([(b("pa1", 128, 256), pair[0], pair[1], False, True)])
-        after["S"] = last("S")
-        act(b("wv"), b("pa1", 128, 256))
-        if t == 1 and not STAGE:
-            after["S"] = last("S")
-            for h in range(2):
-                act(b("xp", 512 * h, 512 * h + 512), ind(xv, b("pl%d" % t, 32 * h, 32 * h + 32)))
-            act(b("xps"), ind(b("xp"), so))
+        act(b("gv"), ind(win, lv2))
+        mm([(b("pb", 128, 256), b("mr3"), b("iv", NL * t, NL * t + NL), True, False)])
+        mm([(b("pb", 128, 256), b("gv"), b("pm"), False, True)])
+        act(b("wv"), b("pb", 128, 256))
         if t < NR - 1:
             B3 = 128 * t
             tt(b("pf"), ind(b("kt"), b("pnl", 16 * t, 16 * t + 16)), b("xpn"), A.mult)
-            mm([(b("pg", 8 * w, 8 * w + 8), b("pf", 128 * w, 128 * w + 128), b("bi"), True, True) for w in range(2)])
-            ts(b("sb3", 16 * t, 16 * t + 16), b("pg", 0, 16), sgn, A.mult, OFF, A.add)
-            hop(T.sb3[:, 16 * t:16 * t + 16], T.ld3[:, B3 + 16 * me:B3 + 16 * me + 16], [b("sb3", 16 * t, 16 * t + 16)],
-                others("ld3", B3, 16), False, HOP)
+            mm([(b("pa1", 16 + 8 * w, 24 + 8 * w), b("pf", 128 * w, 128 * w + 128), b("bi"), True, True) for w in range(2)])
+            ts(b("sb3", 16 * t, 16 * t + 16), b("pa1", 16, 32), sgn, A.mult, OFF, A.add)
+            to_all(T.sb3[:, 16 * t:16 * t + 16], [T.ld3[:, B3 + 16 * i:B3 + 16 * i + 16] for i in range(n - 1)],
+                   [b("sb3", 16 * t, 16 * t + 16)], [b("ld3", B3, B3 + 112)], HOP)
             after["V"] = last("V")
         B9 = 72 * t
-        for c in range(4):
+        first = [True]
+
+        def sums(ys):
+            mm([(b("pc_", 0, 72), b("pr", 128 * y, 128 * y + 128), b("z9", 8 - y, 80 - y), first[0] and y == ys[0], y == 7) for y in ys])
+            first[0] = False
+        for c in (0, 4, 1, 2, 3):
+            if c == 4:
+                tt(b("pr", 1024, 1152), b("kcc"), b("xps"), A.mult)
+                sums([8])
+                continue
             kj = ind(b("kt"), b("pl%d" % t, 16 * c, 16 * c + 16))
-            if c < 2 or t < NR - 1:
+            if 256 * c < DIRECT[t]:
                 tt(b("pr", 256 * c, 256 * c + 256), kj, b("xs_", 256 * c, 256 * c + 256), A.mult)
             else:
-                act(b("kg", 256 * c, 256 * c + 256), kj)
-                tt(b("pr", 256 * c, 256 * c + 256), b("kg", 256 * c, 256 * c + 256), b("pa0", 256 * c - 512, 256 * c - 256), A.mult)
-            mm([(b("pc_", 0, 72), b("pr", 128 * y, 128 * y + 128), b("z9", 8 - y, 80 - y), y == 0, False) for y in (2 * c, 2 * c + 1)])
-        tt(b("pr", 1024, 1152), b("kcc"), b("xps"), A.mult)
-        mm([(b("pc_", 0, 72), b("pr", 1024, 1152), b("z9", 0, 72), False, True)])
+                act(b("kj", 256 * c, 256 * c + 256), kj)
+                tt(b("pr", 256 * c, 256 * c + 256), b("kj", 256 * c, 256 * c + 256),
+                   b("pa0", 256 * c - 512, 256 * c - 256) if c > 1 else b("pd", 256 * c - DIRECT[t], 256 * c + 256 - DIRECT[t]), A.mult)
+            sums([2 * c, 2 * c + 1])
         ts(b("sb9", B9, B9 + 72), b("pc_", 0, 72), sgn, A.mult, OFF, A.add)
         last_conv = last("V")
-        if t in VIA:
-            by_helper(t, HOP + HELP)
-        else:
-            hop(lambda r: T.sb9[:, B9 + 9 * r:B9 + 9 * r + 9], T.ld9[:, B9 + 9 * me:B9 + 9 * me + 9], [b("sb9", B9, B9 + 72)],
-                others("ld9", B9, 9), True, HOP)
+        spread(lambda i: b("sb9", B9 + 9 * peers[i], B9 + 9 * peers[i] + 9), ("ld9", 64 * t), 9, False)
+        ops[-1]["bias"] = KNOB["sums"] if t < NR - 1 else 0.0
 
         if t == NR - 1:
             after["V"] = last_conv
         tt(b("src"), ind(b("tb"), b("cl")), b("wv"), A.add)
-        cp(ind(b("it"), b("tgt")), b("src"))
         if t < NR - 1:
+            cp(ind(b("it"), b("tgt")), b("src"))
             act(b("ian"), ind(b("it"), pn))
             mm([(b("pe", 0, 64), b("ian"), b("zi", 8, 72), True, False), (b("pe", 0, 64), b("it", nx, nx + NL), b("zi", 0, 64), False, True)])
             act(b("ei"), b("pe", 0, 64))
-            gather_sum("f3", "ld3", B3, 16, b("sb3", 16 * t, 16 * t + 16), [(0, 16, b("ei", 0, 16))], None, None)
+            own_slot("f3", 16, b("sb3", 16 * t, 16 * t + 16), b("ei", 0, 16))
             cp(b("vi", 0, 16), b("ei", 32, 48))
             ts(b("vi", 16, 32), b("vi", 0, 16), 12, A.arith_shift_right, 1, A.bitwise_and)
             ts(b("sdf", 0, 16), b("ei", 48, 64), NL * t - 0.5, A.is_lt, 2.0, A.mult)
             tt(b("sdf", 16, 32), b("vi", 16, 32), b("sdf", 0, 16), A.add)
-            if wd == 2:
-                cp(b("pc2"), ind(win, l5))
+            tt(b("d1", 0, 24, 3), pc, b("ei", 48, 56), A.subtract)
+            tt(b("d1", 1, 24, 3), b("ei", 48, 56), b("ei", 56, 64), A.subtract)
+            act(b("d1", 2, 24, 3), b("ei", 56, 64))
+            if KNOB["pre"]:
+                after["V"] = last_conv
+            finish_sum("f3", "ld3", B3, 16, ("x3", 0), ("y3", 0), b("b3"))
             for w in range(2):
-                tt(b("sdf", 32 + 8 * w, 40 + 8 * w), b("ei", 48 + 8 * w, 56 + 8 * w), pc, A.subtract)
-            finish_sum("f3", "ld3", B3, 16, ("x3", 0), ("y3", 0), b("w3", 0, 16))
-            tt(b("w3", 16, 32), b("w3", 0, 16), b("sdf", 16, 32), A.is_equal)
-            tt(b("w3", 32, 48), b("w3", 16, 32), b("sdf", 32, 48), A.mult)
-            tt(b("w3", 48, 56), b("w3", 32, 40), b("w3", 24, 32), A.mult)
-            tt(b("w3", 56, 64), b("w3", 32, 40), b("w3", 40, 48), A.add)
-            tt(b("w3", 64, 72), b("w3", 56, 64), b("w3", 48, 56), A.subtract)
-            tt(b("gm2"), ind(b("w3", 64, 72), gl), m2, A.mult)
-            mm([(b("pf_", 0, 8), b("gm2"), b("r2"), False, True)])
-            cp(b("so", 8 * t + 8, 8 * t + 16), b("pf_", 0, 8))
-            cp(b("sl", 8 * t + 8, 8 * t + 16), b("so", 8 * t + 8, 8 * t + 16))
+                tt(b("d0", 1 + w, 24, 3), b("b3", 8 * w, 8 * w + 8), b("sdf", 16 + 8 * w, 24 + 8 * w), A.not_equal)
+            scan(b("w3", 0, 24), b("d0"), b("d1"))
+            cp(b("ga"), ind(b("w3"), lso))
+            to_list("pa1", 32, "ga", "mz")
+            cp(b("so", 8 * t + 8, 8 * t + 16), b("pa1", 32, 40))
+            tt(b("tg", 0, 8), b("pa1", 32, 40), b("dump"), A.subtract)
+            swap_tables(t + 1, b("w3", 3 * me + 2, 3 * me + 3))
 
         k1 = len(ops)
         mm([(b("pe", 128, 192), b("src"), b("zi", 8, 72), True, True)])
         act(b("el"), b("pe", 128, 192))
-        ts(b("yw", 0, 8), b("el", 32, 40), 8000.0, A.is_gt)
-        lin(b("yw", 8, 16), b("el", 16, 24), 1.0, 1.0)
-        tt(b("yw", 8, 16), b("yw", 8, 16), b("yw", 0, 8), A.mult)
-        tt(b("gy"), ind(b("yw", 8, 16), gl), m2, A.mult)
-        mm([(b("pe", 256, 264), b("gy"), b("r2"), True, True)])
+        ts(b("yw", 16, 24), b("el", 32, 40), 8000.0, A.is_gt)
+        lin(b("yw", 24, 32), b("el", 16, 24), 1.0, 1.0)
+        tt(b("yw", 0, 8), b("yw", 24, 32), b("yw", 16, 24), A.mult)
+        act(b("gy"), ind(b("yw", 0, 16), lyc))
+        to_list("pe", 256, "gy", "mzf")
         lin(b("ycs", 8 * t, 8 * t + 8), b("pe", 256, 264), 1.0, -1.0)
-        if t == NR - 1:
-            dma("Y", [(T.yc[:, :], T.ycs[:, :])], [b("ycs")], [])
 
-        mm([(b("pg", 64, 100), b("src"), b("zo", 0, 36), True, False)])
-        for c in range(4):
-            (cp if t == NR - 1 and c % 2 == 0 else act)(b("ia", 256 * c, 256 * c + 256), ind(b("it"), b("pl%d" % t, 16 * c, 16 * c + 16)))
-            mm([(b("pg", 64, 100), b("ia", 128 * y, 128 * y + 128), b("zo", 8 - y, 44 - y), False, y == 7) for y in (2 * c, 2 * c + 1)])
-        act(b("eo", 0, 36), b("pg", 64, 100))
-        ops[k1]["ord"].append(last("P"))
-        ops[k1 + 1]["ord"].append(last("S"))
-        gather_sum("f9", "ld9", B9, 9, b("sb9", B9 + 9 * me, B9 + 9 * me + 9), [(0, 9, b("eo", 0, 9))], None, None)
-        cp(b("vo", 0, 9), b("eo", 18, 27))
-        ts(b("vo", 16, 25), b("vo", 0, 9), 12, A.arith_shift_right, 1, A.bitwise_and)
-        ts(b("sdo", 0, 8), b("eo", 27, 35), NL * t - 0.5, A.is_lt, 2.0, A.mult)
-        ts(b("sdo", 8, 9), b("eo", 26, 27), 8000.0, A.is_lt, 2.0, A.mult)
-        ts(b("sdo", t, t + 1), b("eo", 27 + t, 28 + t), b("jt", t, t + 1), A.is_equal, b("sdo", t, t + 1), A.add)
-        ts(b("sdo", 0, 9), b("sdo", 0, 9), 2.0, A.mult)
-        tt(b("sdo", 16, 25), b("vo", 16, 25), b("sdo", 0, 9), A.add)
-        tt(b("sdo", 32, 40), b("eo", 27, 35), b("po"), A.subtract)
-        tt(b("sdo", 40, 41), b("up", 8, 9), scol, A.subtract)
-        k0 = len(ops)
-        finish_sum("f9", "ld9", B9, 9, ("x9", 0), ("x9", 40), b("w9", 0, 9))
+        own_slot("f9", 9, b("sb9", B9 + 9 * me, B9 + 9 * me + 9), b("eo", 0, 9))
+        finish_sum("f9", "ld9", 64 * t, 9, ("x9", 0), ("x9", 40), b("w9", 0, 9))
         tt(b("w9", 16, 25), b("w9", 0, 9), b("sdo", 16, 25), A.is_equal)
-        ts(b("w9", 48, 64), b("yh2"), b("w9", 24, 25), A.mult)
-        tt(b("w9", 32, 41), b("w9", 16, 25), b("sdo", 32, 41), A.mult)
-        mm([(b("pg", 128, 144), b("oh"), b("w9", 48, 64), True, True)])
-        tt(b("w9", 64, 72), b("w9", 32, 40), b("po"), A.add)
-        tt(b("w9", 64 + t, 65 + t), b("w9", 64 + t, 65 + t), b("w9", 40, 41), A.add)
-        tt(b("w9", 72, 80), b("w9", 64, 72), b("pg", 128, 136), A.add)
-        tt(b("po"), b("w9", 72, 80), b("pg", 136, 144), A.max)
-        tt(b("g64"), ind(b("po"), ly), b("m3"), A.mult)
-        mm([(b("pg", 192, 256, 1, 0, 16), mb, b("g64"), True, True)])
+        ts(b("rh2"), b("oh2", 128 * t, 128 * t + 128), b("w9", 24, 25), A.mult)
+        tt(b("g72"), ind(b("w9", 16, 32), ly), b("gd"), A.mult)
+        mm([(top(b("pg", 128, 192)), b("ohb", 16 * t, 16 * t + 16), b("rh2", 64, 128), True, True),
+            (top(b("pf_", 0, 64)), b("ohb", 16 * t, 16 * t + 16), b("rh2", 0, 64), False, False)])
+        act(top(b("sm")), top(b("pg", 128, 192)))
+        if t == NR - 1:
+            after["S"] = last("S")
+            dma("S", [(T.yc[:, :], T.ycs[:, :])], [b("ycs")], [])
+        mm([(top(b("pf_", 8 * t, 8 * t + 8)), mb, b("g72", 64, 72), False, False),
+            (top(b("pf_", 0, 64)), mb, b("g72", 0, 64), False, True)])
+        tt(top(b("pw")), top(b("pf_", 0, 64)), top(b("sm")), A.max)
         dn = "dp%d" % (t + 1)
-        lo = b("pu", 0, 64, 1, 0, 16) if t < NR - 1 else b("pw", 0, 64, 1, 0, 16)
-        cp(lo, b("pg", 192, 256, 1, 0, 16))
-        late = [k for k in range(k0, len(ops)) if ops[k]["eng"] == "V"]
-        dma("Y", [(T[dn][me], ap(lo))], [lo], [(dn, me, me + 1)])
-        hop(T[dn][me], T[dn][me], [(dn, me, me + 1)], [(dn, r, r + 1) for r in peers], False, HOPD)
-        ops[-1]["bias"] = BIAS if t < NR - 1 else 0.0
+        lo = top(b("pw"))
         if t < NR - 1:
-            dma("Y", [(T["pl%d" % (t + 1)][:, :], T[dn][:])], [(dn, 0, 8)], [b("pl%d" % (t + 1))])
+            lo = top(b("pu"))
+            cp(top(b("ph")), top(b("pw")))
+            cp(top(b("pu", 0, 64)), top(b("pw")))
+            grandparents(t + 1, b("w3", 3 * me + 2, 3 * me + 3))
+            own_parents()
+            late = [k for k in range(k1, len(ops)) if ops[k]["eng"] == "V" and KNOB["late"]]
+        dma("Y", [(T[dn][me], ap(lo))], [lo], [(dn, me, me + 1)])
+        to_all(T[dn][me], [T[dn][me] for r in peers], [(dn, me, me + 1)], [(dn, r, r + 1) for r in peers], HOPD)
+        ops[-1]["bias"] = KNOB["list"] if t < NR - 1 else 0.0
+        lists = [last("G")] if KNOB["behind"] else []
+        if t < NR - 1:
+            dma("Y", [(T["pl%d" % (t + 1)][:, :], T[dn][:])], [(dn, 0, 8)], [b("pl%d" % (t + 1))], DMAT + 0.3)
         else:
             dma("Y", [(T.yp[:, :], T[dn][:])], [(dn, 0, 8)], [])
 
@@ -720,33 +748,60 @@ def rank_program(g, core, T, topo):
     left = [len(succ[k]) + len(behind[k]) for k in range(m)]
     todo = [k for k in range(m) if left[k] == 0]
     prio = [0.0] * m
+
+    def lag(j, k):
+        return 0.0 if ops[j]["eng"] == "P" and ops[k]["eng"] == "P" else ops[j]["lat"]
     while todo:
         k = todo.pop()
-        prio[k] = max([ops[k]["lat"] + prio[j] for j in succ[k]] + [prio[j] for j in behind[k]] + [ops[k]["lat"]]) + ops[k]["cost"] + 1e-6 \
-            + ops[k].get("bias", 0.0)
+        prio[k] = max([lag(k, j) + prio[j] for j in succ[k]] + [prio[j] for j in behind[k]] + [ops[k]["lat"]]) + ops[k]["cost"] + 1e-6 \
+            + ops[k]["bias"]
         for j in ops[k]["deps"] + ops[k]["ord"]:
             left[j] -= 1
             if left[j] == 0:
                 todo.append(j)
     assert max(left) == 0
-    busy = {}
-    start, done = [0.0] * m, [0.0] * m
-    for k in sorted(range(m), key=lambda k: (-prio[k], k)):
-        o = ops[k]
-        s = max([done[j] for j in o["deps"]] + [start[j] + ops[j]["cost"] for j in o["ord"]] + [0.0])
-        if o["eng"] != "X":
-            sl_ = busy.setdefault(o["eng"], [])
-            for (u, w) in sl_:
-                if s + o["cost"] <= u:
-                    break
-                s = max(s, w)
-            sl_.append((s, s + o["cost"]))
-            sl_.sort()
-        start[k] = s
-        done[k] = s + o["cost"] + o["lat"]
+    rank = sorted(range(m), key=lambda k: (-prio[k], k))
+    wait = [[(j, ops[j]["cost"] + lag(j, k)) for j in ops[k]["deps"]] + [(j, ops[j]["cost"]) for j in ops[k]["ord"]] for k in range(m)]
+
+    def lay(more):
+        busy = {e: [] for e in "VSPGY"}
+        start = [0.0] * m
+        for k in rank:
+            s, c = 0.0, ops[k]["cost"]
+            for (j, d) in wait[k]:
+                if start[j] + d > s:
+                    s = start[j] + d
+            if ops[k]["eng"] == "X":
+                s += more.get(k, 0.0)
+            else:
+                sl_ = busy[ops[k]["eng"]]
+                lo, hi = 0, len(sl_)
+                while lo < hi:
+                    mid = (lo + hi) // 2
+                    if sl_[mid][1] <= s:
+                        lo = mid + 1
+                    else:
+                        hi = mid
+                while lo < len(sl_) and s + c > sl_[lo][0]:
+                    s = max(s, sl_[lo][1])
+                    lo += 1
+                sl_.insert(lo, (s, s + c))
+            start[k] = s
+        return start
+    shape = tuple((o["eng"], tuple(o["deps"]), tuple(o["ord"]), round(o["cost"], 4)) for o in ops)
+    if shape not in LAID:
+        more = {}
+        start = lay(more)
+        bound = max(start) + KNOB["give"]
+        for step in KNOB["steps"]:
+            for k in sorted((k for k in range(m) if ops[k]["eng"] == "X"), key=lambda k: start[k]):
+                more[k] = more.get(k, 0.0) + step
+                if max(lay(more)) > bound:
+                    more[k] -= step
+        LAID[shape] = lay(more)
+    start = LAID[shape]
     order = sorted(range(m), key=lambda k: (start[k], -prio[k], k))
-    PLAN[me] = [(start[k], done[k], ops[k]["eng"], k, ops[k]["tag"]) for k in order]
-    PLAN["ops"] = (ops, order)
+    PLAN[me] = (ops, order, start)
     queue = {"V": g.vector, "S": g.scalar, "P": g.tensor, "G": g, "Y": g.sync}
     count = {"V": 0, "S": 0, "P": 0, "G": 0}
     for k in order:
@@ -787,4 +842,4 @@ def rank_program(g, core, T, topo):
             g.sync.wait_ge(o["sem"][0], o["sem"][1])
 
 
-PLAN = {}
+PLAN, LAID = {}, {}

@@ -5,62 +5,67 @@ NV, NC, NL, NR = 1024, 3584, 128, 3
 BLK = 32
 OFF = 32768.0
 BIG = 4096.0
+TOP = 2.0 ** 22
+FAR = 2 ** 24 - 1
 F32, BF, F16, I32, U16 = "float32", "bfloat16", "float16", "int32", "uint16"
 
 _S = {
-    "xs_": (NV, BF), "kcs": (NC, BF), "cds": (NV, I32), "pas": (64, I32), "tb": (NC, I32), "cs": (128, F32), "ec": (128, F32),
-    "rep": (128, F32),
-    "pl0": (64, U16), "pl1": (72, U16), "pl2": (72, U16),
-    "ci": (16, I32), "cf": (16, F32), "cg": (16, F32), "iv": (384, F32), "rb": (128, F32), "r8": (80, F32),
-    "lf": (96, F32), "lst": (128, U16), "la": (16, F32),
-    "m1": (128, F32), "r1": (8, F32), "pm": (128, F32), "m2": (128, F32), "bi": (8, F16),
-    "pmt": (128, F16), "one": (128, F16), "idh": (128, F16), "bigu": (128, F16), "mz": (48, F16), "mzf": (48, F32),
-    "kk": (32, F32), "m3": (80, F32), "jt": (8, F32), "dump": (8, F32), "z9": (80, F16), "z2": (72, F32), "zi": (136, F32),
-    "mk": (8, F32), "m2h": (128, F16), "sg": (64, F32), "mr6": (128, F32), "dh": (128, F16), "gmo": (128, F32), "gvo": (128, F32),
-    "lio": (16, I32), "tgo": (32, F32), "wvo": (128, F32), "sro": (128, F32), "ito": (1152, F32), "iao": (128, F32), "kj": (NV, BF),
-    "so": (24, U16), "cut": (128, U16), "xg": (128, BF), "xm": (2048, BF), "kg": (2048, BF),
-    "ev": (16 * BLK, F32), "sb1": (3 * 256, U16), "ld1": (3 * 256, U16), "f1": (256, F32), "x1": (64, F32), "y1": (96, F32),
-    "sd": (32, F32), "mq": (64, F32), "v32": (32, F32), "t32": (32, F32), "ld2": (48, F32),
-    "sw": (40, U16), "sh": (8, F16), "dg": (128, F16), "goff": (16, U16), "cq": (32, F32), "gg": (256, F32),
-    "ct": (64, F32), "less": (256, F32), "scan": (256, F32), "rs": (256, F32), "cm": (16, F32), "rk": (32, F32),
-    "wo": (256, F32), "e3": (128, F32), "sc": (16, F32), "si": (8, I32), "rm": (32, F32), "rt": (32, F32),
-    "pnl": (32, U16), "pc": (16, F32), "e2": (128, F32), "qq": (64, F32), "paf": (16, F32),
-    "ohb": (48, F16), "oha": (64, F32), "oh2": (384, F16), "obt": (128, F16), "ux": (64, F32), "up": (16, F32), "uh": (8, F16),
-    "pz": (64, F32), "py": (64, F32),
-    "gm": (128, F32), "li": (16, I32), "cl": (8, U16), "tg": (32, F32), "tgt": (8, U16), "kcc": (128, BF), "kt": (1152, BF),
-    "xpn": (256, BF), "pf": (256, F16), "sb3": (32, U16), "ld3": (256, U16), "f3": (128, F32), "x3": (64, F32), "y3": (32, F32),
-    "b3": (16, F32), "d0": (24, F32), "d1": (24, F32), "w3": (32, F32), "ga": (64, F16), "gv": (128, F32),
-    "mr3": (128, F32), "wv": (128, F32), "src": (128, F32),
-    "it": (1152, F32), "ian": (128, F32), "ei": (64, F32), "vi": (32, I32), "sdf": (32, F32),
-    "el": (64, F32), "yw": (32, F32), "gy": (64, F32), "ycs": (24, F32),
-    "xp": (NV, BF), "xps": (128, BF), "pr": (1152, F16), "sb9": (3 * 72, U16), "ld9": (3 * 64, U16), "f9": (72, F32),
-    "eo": (64, F32), "vo": (32, I32), "sdo": (48, F32), "x9": (64, F32), "w9": (32, F32), "po": (16, F32),
-    "gd": (80, F32), "g72": (80, F16), "rh2": (128, F16), "sm": (64, F32), "pu": (72, U16), "pw": (64, F32), "ph": (64, F16),
-    "px": (64, F32),
+    "xs_": (NV, BF), "kcs": (NC, BF), "cds": (NV, I32), "cs": (128, F32), "ec": (128, F32), "rep": (128, F32), "pas": (64, I32), "pin": (8, I32), "tb": (NC, I32),
+    "pl0": (64, U16), "pl1": (64, U16), "pl2": (64, U16),
+    "ci": (16, I32), "cf": (16, F32), "cg": (32, F32), "iv": (144, F32), "rb": (128, F32), "tm": (128, F32),
+    "lf": (96, F32), "lst": (128, U16), "la": (16, F32), "ws": (3, F32), "lrow": (384, F32), "wb": (16, F32),
+    "m1": (128, F32), "r1": (16, F32), "m2": (128, F32), "bi": (8, F16), "b7": (8, F16), "m4": (128, F32),
+    "pmt": (128, F16), "one": (128, F16), "idh": (128, F16), "bigu": (128, F16), "mz": (48, F16),
+    "jt": (8, F32), "lnl": (8, F32), "z9": (80, F16), "z2": (72, F32), "zi": (136, F32),
+    "m2h": (128, F16), "dh": (128, F16), "gmo": (128, F32),
+    "lio": (32, I32), "tgo": (32, F32), "wvo": (128, F32), "sro": (128, F32), "ito": (1152, F32), "iao": (NV, F32), "zo": (4, F32), "kj": (1152, BF),
+    "so": (24, U16), "cut": (128, U16), "xg": (128, BF), "xm": (2048, BF), "kg": (2064, BF),
+    "sb1": (3 * 256, U16), "ld1": (3 * 256, U16), "f1": (256, F32), "x1": (96, F32), "x1s": (96, F32), "x1d": (96, F32), "y1": (64, F32),
+    "sd": (32, F32), "td": (32, F32), "v64": (64, F32), "t64": (72, F32), "dd": (32, F32), "ld2": (144, F32),
+    "sw": (40, U16), "su": (4, U16), "sh": (8, F16), "dg": (128, F16), "goff": (16, U16), "cq": (32, F32), "gg": (256, F32),
+    "ct": (32, F32), "cc": (64, F32), "qc": (32, F32), "sc": (16, F32), "si": (8, I32),
+    "pnl": (32, U16), "pc": (16, F32), "e2": (128, F32), "e3": (128, F32), "qq": (32, F32), "paf": (16, F32),
+    "ux": (8, F32), "up": (16, F32), "pz": (64, F32), "py": (64, F32),
+    "gm": (128, F32), "li": (32, I32), "cl": (16, U16), "ck": (8, U16), "tg": (32, F32), "tgt": (8, U16), "kcc": (128, BF), "kt": (1152, BF),
+    "xpn": (128, BF), "pf": (256, F16), "sb3": (32, U16), "ld3": (256, U16), "f3": (128, F32), "x3": (64, F32), "y3": (32, F32),
+    "b3": (16, F32), "d0": (24, F32), "d1": (24, F32), "w3": (32, F32), "ga": (64, F16), "wv": (128, F32), "src": (128, F32),
+    "it": (1152, F32), "ian": (128, F32), "ei": (64, F32), "sdf": (16, F32), "ycr": (384, F32),
+    "xps": (128, BF), "gpl": (8, U16), "pr": (1296, F16), "sb9": (3 * 72, U16), "ld9": (3 * 64, U16), "f9": (72, F32),
+    "eo": (64, F32), "sdo": (32, F32), "x9": (64, F32), "w9": (32, F32), "po": (16, F32),
+    "gd": (128, F32), "g72": (128, F16), "rh2": (24, F16), "rh0": (24, F16), "sa": (48, F32), "sm": (16, F32), "pu": (56, U16), "pw": (16, F32), "ph": (16, F16),
+    "mx": (128, F32), "ox": (128, F16), "lt": (136, F16), "ohm": (384, F16), "oht": (128, F16), "ohu": (24, F32), "rhc": (72, F32),
 }
 PLACE = {}
 _n = 0
 for _k, (_w, _d) in _S.items():
-    if _d == F32 and _w <= 96 and _k not in ("ld2", "ycs", "pw"):
+    if _d == F32 and _w <= 96 and _k != "pw":
         PLACE[_k] = _n
         _n += (_w + 15) // 16 * 16
 SCRATCH = {k: ("sbuf", [128, n], d) for k, (n, d) in _S.items() if k not in PLACE}
 SCRATCH["small"] = ("sbuf", [128, _n], F32)
-BANKS = ["pa0", "pa1", "pb", "pc_", "pd", "pe", "pf_", "pg"]
+BANKS = ["pa0", "px0", "px1", "pb", "pc_", "pe", "pf_", "pg"]
 for _b in BANKS:
     SCRATCH[_b] = ("psum", [128, 512], F32)
-SCRATCH["dp1"] = ("dram", [8, 128, 9], U16)
-SCRATCH["dp2"] = ("dram", [8, 128, 9], U16)
+for _t in range(NR):
+    SCRATCH["dg%d" % _t] = ("dram", [8, 128, 1], U16)
+SCRATCH["dp1"] = ("dram", [8, 128, 8], U16)
+SCRATCH["dp2"] = ("dram", [8, 128, 8], U16)
 SCRATCH["dp3"] = ("dram", [8, 128, 8], F32)
-SEMAPHORES = ["V", "S", "P", "G", "sent"] + ["d%d" % i for i in range(32)] + ["a%d" % i for i in range(32)]
+SEMAPHORES = ["V", "S", "P", "G", "sent"] + ["d%d" % i for i in range(32)] + ["a%d" % i for i in range(32)] + ["h%d" % i for i in range(8)]
+RELAYED = ("sb9",)
 
-CYC, GAT, SCA, PEC, LAT, SFIX = 0.00083, 1.56, 3.8, 0.0005, 0.2, 0.1
-HOP, HOPD, DMAT, CALL, FIRST, DISS = 1.4, 0.9, 1.5, 0.2, 1.2, 0.1
-KNOB = {"list": 0.0, "sums": 0.0, "tables": 0.0, "late": True, "behind": False, "own": 0.0, "rank": "V", "pre": False,
-        "give": 1.0, "steps": (1.2, 0.6, 0.6, 0.3)}
-DIRECT = (0, 0, 256)
+CYC, GAT, SCA, PEC, LAT, SLAT, SFIX = 0.0009, 1.56, 3.8, 0.00054, 0.175, 0.05, 0.1
+HOPD, START = 1.9, 0.55
+HOP, DMAT, CALL, FIRST, DISS = 1.4, 2.0, 0.28, 1.5, 0.12
+KNOB = {"give": 0.1, "steps": (0.3,), "loads": (2.9, 4.3, 6.9, 4.0), "passes": 4, "reach": 40, "list": 0.5, "open": 0.3, "late": 1, "kcc": 1, "direct": 0, "two": ("f1", "f3", "f9"), "sweeps": 1, "long": 0.2, "listed": 1, "summed": 1,
+        "cases": ((1.0, 1.0, 0.007, 0.0, 0.55), (0.95, 0.97, 0.003, 0.0, 0.4), (1.4, 1.0, 0.008, 0.0, 0.55), (1.02, 1.0, 0.035, 0.1, 0.85),
+                  (1.1, 1.1, 0.02, 0.4, 0.9), (1.0, 1.0, 0.04, 0.2, 0.7))}
+ON_SCALAR = ["rhc", "up", "first", "dh", "dg", "sh", "sdo", "cc"]
 TBV = 2304
-KS, KV = (288, 288, 288, 288), (320, 288, 288)
+PIECES = [[("V", 128), ("S", 192), ("V", 256), ("S", 256), ("V", 320), ("S", 320), ("V", 320), ("S", 256)],
+          [("S", 384), ("V", 192), ("S", 256), ("V", 256), ("S", 256), ("V", 256), ("S", 192), ("V", 256)]]
+BLOCKS = [[("S", 0, 1), ("S", 2, 4), ("S", 4, 6), ("S", 6, 8)], [("S", 0, 2), ("S", 3, 4), ("S", 4, 6), ("S", 6, 8)],
+          [("V", 0, 2), ("S", 4, 6), ("V", 2, 3), ("S", 6, 8), ("S", 3, 4)]]
 
 
 def bits(engines):
@@ -68,9 +73,16 @@ def bits(engines):
 
 
 def rank_program(g, core, T, topo):
+    def helpers(c):
+        return [x for x in topo.cores_of(c) if x not in T.cores and topo.die(x) == topo.die(c)][:2]
     me = T.rank_of(core)
     if me is None:
-        return
+        mine = [r for r, c in enumerate(T.cores) if core in helpers(c)]
+        if not mine:
+            return
+        me = mine[0]
+    home = T.cores[me]
+    aids = helpers(home)
     n = len(T.cores)
     A, AX, AF = AluOpType, AxisListType.X, ActivationFunctionType
     sgn = 1.0 if me % 2 == 0 else -1.0
@@ -87,9 +99,6 @@ def rank_program(g, core, T, topo):
         if name in PLACE:
             return ("small", c0 + PLACE[name], c1 + PLACE[name], step, p0, p1)
         return (name, c0, c1, step, p0, p1)
-
-    def top(x):
-        return x[:4] + (0, 16)
 
     def ind(win, off):
         return ("#", win, off)
@@ -111,15 +120,12 @@ def rank_program(g, core, T, topo):
 
     def add(eng, fn, reads, writes, cost, lat=None, kind="c", extra=None):
         k = len(ops)
-        lat = LAT if lat is None else lat
-        deps = {}
+        lat = LAT + (SLAT if eng == "S" else 0.0) if lat is None else lat
+        deps, ords = {}, {}
         rl, wl = [], []
         for x in reads:
             if isinstance(x, tuple):
-                if x[0] == "#":
-                    rl += [x[1], x[2]]
-                else:
-                    rl.append(x)
+                rl += [x[1], x[2]] if x[0] == "#" else [x]
         for x in writes:
             if x[0] == "#":
                 wl.append(x[1])
@@ -128,19 +134,22 @@ def rank_program(g, core, T, topo):
                 wl.append(x)
         for x, wr in [(x, False) for x in rl] + [(x, True) for x in wl]:
             h = hist.setdefault(x[0], [])
-            for (j, c0, c1, w2) in h:
+            st = x[3] if len(x) > 3 else 1
+            for (j, c0, c1, s2, w2) in h:
                 if j == k:
                     continue
-                if x[0] in BANKS:
-                    if ops[j]["eng"] != eng or eng == "P" or ((wr or w2) and c0 < x[2] and x[1] < c1):
-                        deps[j] = True
-                elif (wr or w2) and c0 < x[2] and x[1] < c1:
+                meet = (wr or w2) and c0 < x[2] and x[1] < c1 and not (s2 == st and (c0 - x[1]) % st)
+                if x[0] in BANKS and (ops[j]["eng"] != eng or eng == "P"):
                     deps[j] = True
-            h.append((k, x[1], x[2], wr))
+                elif meet:
+                    deps[j] = True
+            h.append((k, x[1], x[2], st, wr))
         if extra is not None:
             deps[extra] = True
+        if eng in after:
+            ords[after[eng]] = True
         ops.append({"eng": eng, "fn": fn, "deps": sorted(deps), "cost": cost, "lat": lat, "kind": kind, "tag": writes[0][:2] if writes else "",
-                    "ord": [after[eng]] if eng in after else [], "bias": 0.0})
+                    "ord": sorted(j for j in ords if j not in deps)})
         return k
 
     def short(x):
@@ -169,14 +178,11 @@ def rank_program(g, core, T, topo):
         add("V", fn, [x, s1, s2], [out], vcost(out, x, 0.5 if short(out) and short(x) else 1.0))
 
     def red(out, x, op, ab=False):
-        if ab:
-            fn = lambda: g.vector.tensor_reduce(ap(out), ap(x), AX, op, apply_absolute_value=True)
-        else:
-            fn = lambda: g.vector.tensor_reduce(ap(out), ap(x), AX, op)
-        add("V", fn, [x], [out], vcost(x, x))
+        more = {"apply_absolute_value": True} if ab else {}
+        add("V", lambda: g.vector.tensor_reduce(ap(out), ap(x), AX, op, **more), [x], [out], vcost(x, x))
 
-    def scan(out, d0, d1):
-        add("V", lambda: g.vector.tensor_tensor_scan(ap(out), ap(d0), ap(d1), 0.0, A.mult, A.add), [d0, d1], [out], vcost(out, d0))
+    def scan(out, d0, d1, init=0.0, op0=A.mult, op1=A.add):
+        add("V", lambda: g.vector.tensor_tensor_scan(ap(out), ap(d0), ap(d1), val(init), op0, op1), [d0, d1, init], [out], vcost(out, d0))
 
     def turn(out, x):
         add("V", lambda: g.vector.transpose(ap(out), ap(x)), [x], [out], vcost(out, x))
@@ -184,17 +190,16 @@ def rank_program(g, core, T, topo):
     def fill(out, c):
         add("V", lambda: g.vector.memset(ap(out), c), [], [out], vcost(out, out, 0.5 if short(out) else 1.0))
 
-    def act(out, x, scale=None):
-        if scale is None:
-            fn = lambda: g.scalar.activation(ap(out), ap(x), AF.Copy)
-        else:
-            fn = lambda: g.scalar.activation(ap(out), ap(x), AF.Copy, scale=scale)
-        add("S", fn, [x], [out], vcost(out, x, 1.0, 0.065))
-
-    def lin(out, x, scale, bias, func=None, total=None):
+    def lin(out, x, scale=1.0, bias=0.0, func=AF.Identity, total=None):
         more = {} if total is None else {"accum_out": ap(total)}
-        add("S", lambda: g.scalar.activation(ap(out), ap(x), func or AF.Identity, bias=val(bias), scale=val(scale), **more),
+        add("S", lambda: g.scalar.activation(ap(out), ap(x), func, bias=val(bias), scale=val(scale), **more),
             [x, scale, bias], [out] + ([total] if more else []), vcost(out, x, 1.0, 0.065) + (0.02 if more else 0.0))
+
+    def aff(tag, out, x, scale=1.0, bias=0.0):
+        if tag in ON_SCALAR:
+            lin(out, x, scale, bias)
+        else:
+            ts(out, x, scale, A.mult, bias, A.add)
 
     def mm(items):
         def fn():
@@ -228,31 +233,53 @@ def rank_program(g, core, T, topo):
         ops[k]["sem"] = (sem, 16 * len(pairs))
 
     peers = [(me + i) % n for i in range(1, n)]
-    engs = topo.engines(core, T.cores[peers[0]])
+    engs = topo.engines(home, T.cores[peers[0]])
     for r in peers:
-        engs = [e for e in engs if e in topo.engines(core, T.cores[r])]
-    dst = {}
-    for r in peers:
-        rid, pid = topo.addr(T.cores[r], core)
-        dst[r] = DstId(rid=rid, pnc=pid)
+        engs = [e for e in engs if all(e in topo.engines(c, T.cores[r]) for c in [home] + aids)]
+    near = [e for e in topo.engines(home, aids[0]) if e in topo.engines(home, aids[1])]
+    spare = [e for e in near if e not in engs]
+
+    def address(to, by):
+        rid, pid = topo.addr(to, by)
+        return DstId(rid=rid, pnc=pid)
+    dst = {r: address(T.cores[r], home) for r in peers}
+    far = [{r: address(T.cores[r], c) for r in peers} for c in aids]
     na = [0]
     sent = [0]
+    relays = []
+
+    def hand_on(src, mid, calls, use, rows):
+        sem = T.sem["h%d" % len(relays)]
+        per = len(use) // len(calls)
+        relays.append((sem, per, calls))
+        srcs = src if isinstance(src, list) else [src]
+        tr = [RemoteDMATransfer(dst_ids=[address(aids[h], home)], dma_engine_mask=bits(use[h * per:h * per + per]), remote_sem=sem,
+                                srcs=[ap(x) for x in srcs], dsts=[mid], alu_op=2 * (len(srcs) - 1)) for h in range(len(calls))]
+        sent[0] += len(use)
+        k = add("G", lambda: g.remote_dma_fused(tr, local_sem=T.sem.sent), srcs, [], CALL, 0.0, "r")
+        ops[k]["rows"], ops[k]["on"] = (128 // per, 32), (len(calls),) + rows
+        ops[k]["ord"] += [j for j in range(k) if "on" in ops[j]]
+        return k
 
     def arrive(k, lands, lat, cnt):
         sem = T.sem["a%d" % na[0]]
         na[0] += 1
         k2 = add("X", None, [], lands, 0.0, lat, "a", extra=k)
-        ops[k2]["sem"] = (sem, cnt)
+        ops[k2]["sem"], ops[k2]["by"] = (sem, cnt), k
 
-    def spread(src, land, w, early, more=()):
+    def spread(src, land, w, early, more=(), via=None):
         sems = [T.sem["a%d" % na[0]], T.sem["a%d" % (na[0] + (1 if early else 0))]]
         calls, i0 = [], 0
         for many in (4, 2, 1):
             per = len(engs) // many
-            calls.append([RemoteDMATransfer(dst_ids=[dst[peers[i]]], dma_engine_mask=bits(engs[(i - i0) * per:(i - i0 + 1) * per]),
+            calls.append([RemoteDMATransfer(dst_ids=[(far[min(i0, 1)] if via else dst)[peers[i]]], dma_engine_mask=bits(engs[(i - i0) * per:(i - i0 + 1) * per]),
                                             remote_sem=sems[min(i0, 1)], src=ap(src(i)),
                                             dst=ap(b(land[0], land[1] + i * w, land[1] + (i + 1) * w))) for i in range(i0, i0 + many)])
             i0 += many
+        if via:
+            k = hand_on(via, ap(via), [calls[:1], calls[1:]], spare, (64, 2 * w))
+            arrive(k, [b(land[0], land[1], land[1] + 7 * w)], HOP + 1.0, 3 * len(engs))
+            return
         sent[0] += 3 * len(engs)
         k1 = add("G", lambda: g.remote_dma_fused(calls[0], local_sem=T.sem.sent), [src(i) for i in range(4)] + list(more), [], CALL, 0.0, "r")
 
@@ -261,22 +288,22 @@ def rank_program(g, core, T, topo):
                 g.remote_dma_fused(tr_, local_sem=T.sem.sent)
         k2 = add("G", fn, [src(i) for i in range(4, 7)], [], 2 * CALL, 0.0, "r")
         ops[k2]["ord"].append(k1)
+        ops[k1]["rows"], ops[k2]["rows"] = (64, 2 * w), (48, 2 * w)
         if early:
-            more = FIRST if more else 0.0
-            arrive(k1, [b(land[0], land[1], land[1] + 4 * w)], HOP - 0.2 + more, len(engs))
-            arrive(k2, [b(land[0], land[1] + 4 * w, land[1] + 7 * w)], HOP - 0.1 + more, 2 * len(engs))
+            arrive(k1, [b(land[0], land[1], land[1] + 4 * w)], HOP - 0.1, len(engs))
+            arrive(k2, [b(land[0], land[1] + 4 * w, land[1] + 7 * w)], HOP + 0.2, 2 * len(engs))
         else:
             arrive(k2, [b(land[0], land[1], land[1] + 7 * w)], HOP - 0.1, 3 * len(engs))
 
-    def to_all(src, dsts, reads, lands, lat):
-        tr = [RemoteDMATransfer(dst_ids=[dst[r] for r in peers], dma_engine_mask=bits(engs), remote_sem=T.sem["a%d" % na[0]],
+    def to_all(src, dsts, reads, lands, lat, rows=(112, 24), to=peers):
+        tr = [RemoteDMATransfer(dst_ids=[dst[r] for r in to], dma_engine_mask=bits(engs), remote_sem=T.sem["a%d" % na[0]],
                                 srcs=[src], dsts=dsts)]
         sent[0] += len(engs)
         k = add("G", lambda: g.remote_dma_fused(tr, local_sem=T.sem.sent), reads, [], CALL, 0.0, "r")
-        arrive(k, lands, lat + 0.4, (n - 1) * len(engs))
+        ops[k]["rows"] = rows
+        arrive(k, lands, lat, len(to) * len(engs))
 
-    def own_slot(f, w, own, thr):
-        o = b(f, 7 * w, 8 * w)
+    def own_slot(o, own, thr):
         cp(o, own)
         tt(o, o, thr, A.subtract if me % 2 == 0 else A.add)
 
@@ -287,40 +314,72 @@ def rank_program(g, core, T, topo):
         else:
             tt(out, ev_, od_, A.is_gt)
 
-    def finish_sum(f, land, base, w, x, y, out):
+    def one_step_sum(f, land, base, w, x, y, out):
         cp(b(f, 0, 7 * w), b(land, base, base + 7 * w))
-        tt(b(x[0], x[1], x[1] + 4 * w), b(f, 0, 4 * w), b(f, 4 * w, 8 * w), A.add)
-        tt(b(y[0], y[1], y[1] + 2 * w), b(x[0], x[1], x[1] + 2 * w), b(x[0], x[1] + 2 * w, x[1] + 4 * w), A.add)
-        compare(out, y, w)
+        tt(b(x, 0, 4 * w), b(f, 0, 4 * w), b(f, 4 * w, 8 * w), A.add)
+        tt(b(y, 0, 2 * w), b(x, 0, 2 * w), b(x, 2 * w, 4 * w), A.add)
+        compare(out, (y, 0), w)
 
-    def to_list(bank, c0, rhs, mask):
-        mm([(b(bank, c0, c0 + 8, 1, 32 * (gr // 2), 32 * (gr // 2) + 32), b(mask, 16 - 16 * (gr % 2), 48 - 16 * (gr % 2)),
-             b(rhs, 8 * gr, 8 * gr + 8), gr % 2 == 0, gr % 2 == 1) for gr in range(8)])
+    def to_lists(lo, dn, to, lands, lat, fold=None):
+        share = [peers[:4], peers[4:]] if dn == "dg0" else [peers]
+        on = [[[RemoteDMATransfer(dst_ids=[far[h][r] for r in to_], dma_engine_mask=bits(engs), remote_sem=T.sem["a%d" % na[0]],
+                                  srcs=[T[dn][me]], dsts=[T[dn][me] for r in to_])]] for h, to_ in enumerate(share)]
+        if dn == "dp3" and KNOB["direct"]:
+            to_all(ap(lo), [T[dn][me] for r in peers], [lo], [(dn, r, r + 1) for r in peers], HOP + 0.3, (112, 32))
+        else:
+            k = hand_on(fold or lo, T[dn][me], on, near if dn in ("dg0", "dp3") else spare, (7, 512))
+            arrive(k, [(dn, r, r + 1) for r in peers], lat, (n - 1) * len(engs))
+        dma("S" if dn == "dg0" else "Y", [(to[16 * me:16 * me + 16, :], ap(lo))], [lo], lands)
+        cuts = ((0, me), (me + 1, n)) if 0 < me < n - 1 else ((1, 4), (4, n)) if me == 0 else ((0, 4), (4, me))
+        rest = [(to[16 * r0:16 * r1, :], T[dn][r0:r1]) for (r0, r1) in cuts]
+        if lands:
+            dma("Y", rest, [(dn, 0, 8)], lands, DMAT + 0.2)
+        else:
+            for e, pair in zip("YS", rest):
+                dma(e, [pair], [(dn, 0, 8)], [])
 
-    dma("Y", [(T.pas[:, :], T.pa[:, :])], [], [b("pas")])
+    def two_step_sum(f, land, base, w, x, y, out):
+        if f not in KNOB["two"]:
+            cp(b(f, 7 * w, 8 * w), b(x, 2, 3 * w, 3))
+            return one_step_sum(f, land, base, w, "x1s", y, out)
+        cp(b(f, 0, 4 * w), b(land, base, base + 4 * w))
+        for h in range(2):
+            tt(b(x, h, 3 * w, 3), b(f, h * w, h * w + w), b(f, 2 * w + h * w, 3 * w + h * w), A.add)
+        scan(b("x1s", 0, 3 * w), b("x1d", 0, 3 * w), b(x, 0, 3 * w))
+        cp(b(f, 4 * w, 7 * w), b(land, base + 4 * w, base + 7 * w))
+        ops[-1]["ord"].append(len(ops) - 2)
+        tt(b(y, 0, w), b(f, 4 * w, 5 * w), b(f, 6 * w, 7 * w), A.add)
+        tt(b(y, w, 2 * w), b(f, 5 * w, 6 * w), b("x1s", 2, 3 * w, 3), A.add)
+        compare(out, (y, 0), w)
+
+    dma("Y", [(T.pas[:, :], T.pa[:, :])], [], [b("pas")], 2.0)
     after["Y"] = last("Y")
-    dma("S", [(T["xs_"][:, :], T.xv[:, :])], [], [b("xs_")], 1.8)
-    after["S"] = last("S")
-    dma("Y", [(T.cds[:, :], T.cd[:, :])], [], [b("cds")], 2.6)
+    dma("S", [(T["xs_"][:, :], T.xv[:, :])], [], [b("xs_")], KNOB["loads"][0])
+    dma("S", [(T.pin[:, :], T.pa[16 * me:16 * me + 16, :])], [], [b("pin")], 2.0)
+    dma("Y", [(T.cds[:, :], T.cd[:, :])], [], [b("cds")], KNOB["loads"][1])
     after["Y"] = last("Y")
-    dma("Y", [(T.kcs[:, :], T.kc[:, :])], [], [b("kcs")], 4.2)
+    dma("Y", [(T.kcs[:, :], T.kc[:, :])], [], [b("kcs")], KNOB["loads"][2])
     after["Y"] = last("Y")
     iota(b("ci", 0, 1), [[0, 1]], 0, 1)
-    after["G"] = last("G")
-    iota(b("lf", 0, 8), [[256, 8]], 0, 0)
-    after["G"] = last("G")
-    fill(b("tb", 0, TBV), 0)
-    iota(b("tb", TBV, NC), [[0, NC - TBV]], 0, 0)
-    rows = [(T.tb[8 * i + 4:8 * i + 5, :], (T.bt, T.co)[i % 2][me:me + 1, :]) for i in range(8)]
-    rows += [(T.tb[0:128:16, :], T.bt[:, :]), (T.tb[1:128:16, :], T.co[:, :])]
-    dma("Y", rows[:7], [b("tb")], [("tb4", 0, 1)])
-    after["Y"] = last("Y")
-    dma("S", rows[7:], [b("tb")], [("tb4", 1, 2)], 2.0)
-    tables_s = last("S")
-    dma("Y", [(T.tb[68:128:8, :], T.tb[4:64:8, :])], [("tb4", 0, 2)], [b("tb")])
+    fill(b("xm", 0, NV), 0.0)
+    lin(b("xm", NV, 2 * NV), b("xs_"), 0.0)
 
-    def col(i):
-        return b("cf", i, i + 1)
+    def lane_features(t, lat, behind=()):
+        dma("Y", [(T.xm[16 * r:16 * r + 16, 256 * ((r - me - 1) % n):256 * ((r - me - 1) % n) + NL],
+                   T.xv[16 * r:16 * r + 16, NL * t:NL * t + NL]) for r in range(n)], list(behind), [b("xm")], lat)
+    for c in range(0, TBV, 384):
+        fill(b("tb", c, c + 384), FAR)
+    iota(b("iv"), [[1, 144]], 0, 0)
+    iota(b("rb"), [[0, 8], [1, 16]], 0, 0)
+    iota(b("tm"), [[1, 16], [128, 8]], 0, 0)
+    iota(b("tb", TBV, NC), [[0, NC - TBV]], FAR, 0)
+    ops[-1]["ord"] += [k for k in range(len(ops) - 1) if ops[k]["eng"] == "G"]
+    rows = [(T.tb[8 * i + 4:8 * i + 5, :], (T.bt, T.co)[i % 2][me:me + 1, :]) for i in range(16)]
+    rows += [(T.tb[0:128:16, :], T.bt[:, :]), (T.tb[1:128:16, :], T.co[:, :])]
+    dma("Y", rows, [], [b("tb")], KNOB["loads"][3])
+    after.pop("Y")
+    for c in range(0, 1152, 288):
+        lin(b("kt", c, c + 288), b("xs_", 0, 288))
 
     def cg(i):
         return b("cg", i, i + 1)
@@ -333,475 +392,421 @@ def rank_program(g, core, T, topo):
     ts(b("ci", 6, 7), p_, 1, A.bitwise_and)
     ts(b("ci", 7, 8), p_, 1, A.arith_shift_right, 7, A.bitwise_and)
     ts(b("ci", 8, 9), p_, 3, A.arith_shift_right)
-    cp(b("cf", 0, 9), b("ci", 0, 9))
-    cP, cB, cG, cP7, cA, cB3, cB0, cB1, cP3 = [col(i) for i in range(9)]
+    ts(b("ci", 9, 10), p_, 3, A.bitwise_and)
+    cp(b("cf", 0, 10), b("ci", 0, 10))
+    cP, cB, cG, cP7, cA, cB3, cB0, cB1, cP3, cR3 = [b("cf", i, i + 1) for i in range(10)]
+    iota(b("jt"), [[128, 8]], 0, 1)
+    iota(b("mx"), [[1, 16], [0, 8]], 0, 0)
+    i2, i4, i8, i128, rb128 = b("iv", 0, 2), b("iv", 0, 4), b("iv", 0, 8), b("iv", 0, 128), b("rb")
+    xoA, xoB, lpm, lpq, lx = b("lst", 0, 8), b("lst", 8, 16), b("lst", 16, 18), b("lst", 18, 20), b("lst", 24, 32)
+    l8, gl2, lpi = b("lst", 32, 40), b("lst", 40, 48), b("lst", 48, 56)
+    lso, lpa, ldup, lpo = b("lst", 64, 68), b("lst", 68, 72), b("lst", 76, 80), b("lst", 80, 81)
     lin(cg(0), cB, 8.0, cG)
     lin(cg(1), cB0, 8.0, cG)
-    ts(cg(2), cB, 16.0, A.mult, cG, A.add)
-    lin(cg(3), cA, 16.0, 0.0)
-    lin(cg(4), cB, float(BLK), cg(3))
-    ts(cg(7), cP, 0.0, A.is_equal)
-    lin(cg(8), cG, 9.0, 8.0)
-    lin(cg(9), cG, 2.0, 1.0)
-    ts(cg(11), cg(2), 8.0, A.add)
-    iota(b("iv"), [[1, 384]], 0, 0)
-    iota(b("rb"), [[0, 8], [1, 16]], 0, 0)
-    iota(b("r8"), [[0, 10], [1, 8]], 0, 0)
-    iota(b("kk"), [[0, 2], [1, 8], [8, 2]], 0, 0)
-    iota(b("lf", 32, 37), [[2, 5]], 0, 0)
-    iota(b("lf", 40, 48), [[16, 8]], NV, 0)
-    iota(b("jt"), [[128, 8]], 0, 1)
-    xoA, xoB, sel = b("lst", 0, 8), b("lst", 8, 16), b("lst", 16, 32)
-    gl2, ly, lcm, lov = b("lst", 40, 48), b("lst", 56, 61), b("lst", 62, 63), b("lst", 48, 49)
-    lso, lpa, lyc, ldup, lpo = b("lst", 64, 68), b("lst", 68, 72), b("lst", 72, 76), b("lst", 76, 80), b("lst", 80, 81)
-    lv2, lA, lB = b("lst", 82, 90), b("lst", 96, 112), b("lst", 112, 128)
-    ts(xoA, b("lf", 0, 8), cg(2), A.add)
-    ts(xoB, b("lf", 0, 8), cg(11), A.add)
-    ts(sel, b("kk", 2 * me + 2, 2 * me + 18), cg(4), A.add)
-    i8 = b("iv", 0, 8)
-    ts(b("la", 0, 8), i8, float(me), A.is_equal, float(8 - me), A.mult)
+    ts(cg(4), cG, float(me) + 0.5, A.is_lt, 8.0, A.mult)
+    ts(cg(14), cG, cg(4), A.add, -me - 0.5, A.add)
+    lin(cg(2), cg(14), 256.0)
+    ts(b("lnl"), i8, 16.0, A.mult, cB, A.add)
+    ts(xoB, b("lnl"), cg(2), A.add)
+    ts(xoA, b("lnl"), cg(2), A.add, -128.0, A.add)
+    l1, l2 = b("lst", 20, 21), b("lst", 22, 24)
+    cp(l1, cP)
+    ts(l2, i2, 0.0, A.mult, cg(0), A.add)
+    lin(cg(25), cP, 1.0, float(-16 * me))
+    ts(b("rep"), rb128, cg(25), A.is_equal)
+    ts(b("zo"), i4, cg(25), A.is_equal)
+    add("V", lambda: g.vector.memset(ap(b("pg", 64, 128)), 0.0), [], [b("pg", 64, 128)], 64 * CYC)
+    ts(b("la", 0, 8), i8, float(me), A.is_equal, float(39 - me), A.mult)
     tt(b("la", 0, 8), b("la", 0, 8), i8, A.add)
     cp(gl2, b("la", 0, 8))
-    ts(cg(6), cB, 2.0, A.is_equal)
-    ts(b("lf", 64, 72), b("la", 0, 8), -12.0, A.add, cg(6), A.mult)
-    ts(lv2, b("lf", 64, 72), 12.0, A.add)
+    cp(l8, i8)
     ts(cg(10), cP7, cG, A.is_equal)
-    lin(b("la", 8, 12), b("lf", 32, 36), 1.0, cB3)
+    ts(b("la", 8, 12), i4, 2.0, A.mult, cB3, A.add)
     lin(b("lf", 80, 84), b("la", 8, 12), 3.0, -22.0)
     ts(lso, b("lf", 80, 84), cg(10), A.mult, 24.0, A.add)
-    lin(b("lf", 84, 88), b("la", 8, 12), 1.0, -8.0)
-    ts(lyc, b("lf", 84, 88), cg(10), A.mult, 8.0, A.add)
     lin(cg(12), cP7, 1.0, -8.0)
     ts(b("lf", 88, 92), b("la", 8, 12), cG, A.is_equal, cg(12), A.mult)
     ts(lpa, b("lf", 88, 92), 8.0, A.add)
-    cp(b("lst", 56, 60), b("la", 8, 12))
-    fill(b("lst", 60, 61), 8)
-    ts(b("la", 12, 16), b("iv", 0, 4), 1.5, A.is_gt, 16.0, A.mult)
-    ts(ldup, b("la", 12, 16), cB, A.add)
-    l1, l2 = b("lst", 32, 33), b("lst", 34, 36)
-    cp(l1, cP)
-    ts(l2, b("iv", 0, 2), 0.0, A.mult, cg(0), A.add)
-    lin(cg(5), cP, 1.0, float(-16 * me))
-    ts(b("rep"), b("rb"), cg(5), A.is_equal)
+    ts(b("la", 12, 14), i2, cA, A.not_equal, 16.0, A.mult)
+    for h in range(2):
+        ts(b("lst", 76 + 2 * h, 78 + 2 * h), b("la", 12, 14), cB, A.add)
+    ts(lx, i8, 0.0, A.mult, cP7, A.add)
+    lin(cg(5), cP7, 16.0, cB3)
+    ts(lpi, i8, 2.0, A.mult, cg(5), A.add)
     ts(lpo, cP7, 8.0, A.mult, cG, A.add)
-    ts(lov, cG, 8.0, A.mult, cP7, A.add)
-    lin(b("dump"), b("lf", 40, 48), 1.0, cB)
-    i128, rb128 = b("iv", 0, 128), b("rb", 0, 128)
     ts(b("m1"), rb128, cg(1), A.is_equal)
-    ts(b("r1"), i8, cB1, A.is_equal)
-    ts(b("pm"), i128, cg(0), A.is_equal)
+    ts(b("r1", 8, 16), i8, cB1, A.is_equal, 2048.0, A.mult)
+    ts(b("r1", 0, 8), i8, cB1, A.is_equal, -0.25, A.mult)
     ts(b("m2"), rb128, cB, A.is_equal)
+    ts(b("m2h"), rb128, cB, A.is_equal)
+    ts(b("m4"), rb128, cP3, A.is_equal)
     ts(b("bi"), i8, cG, A.is_equal)
+    ts(b("b7"), i8, cP7, A.is_equal)
     ts(b("idh"), i128, cP, A.is_equal)
     fill(b("one"), 1.0)
-    ts(b("mr3"), rb128, 3.0, A.is_equal, cg(7), A.mult)
-    lin(b("mr3", 7, 128, 16), b("iv", 0, 8), 0.0, cg(7))
-    ts(b("mr6"), rb128, 6.0, A.is_equal)
-    cp(b("m2h"), b("m2"))
-    for t in range(NR - 1):
-        ts(b("pnl", 16 * t + 8, 16 * t + 16), b("dump"), float(NL * (t + 1) - NV), A.add)
     ts(b("bigu"), i128, cg(0), A.is_ge, BIG, A.mult)
-    ts(b("m3"), b("r8"), cG, A.is_equal)
+    lin(cg(8), cG, 9.0, 8.0)
     ts(b("z9"), b("iv", 0, 80), cg(8), A.is_equal)
-    ts(b("zi"), b("iv", 0, 136), cg(11), A.is_equal)
-    ts(b("mzf"), b("iv", 0, 48), -16.0, A.add, cB, A.is_equal)
-    cp(b("mz"), b("mzf"))
-    lin(b("sg", 1, 2), cP7, 16.0, cP3)
-    ts(b("pmt"), i128, b("sg", 1, 2), A.is_equal)
-    lin(b("sg", 2, 3), cB, 4.0, -16.0)
-    lin(b("sg", 3, 4), b("sg", 2, 3), 1.0, cg(9))
-    ts(b("sg", 4, 5), cP7, 4.0, A.is_equal)
-    ts(b("z2", 0, 65), b("iv", 0, 65), b("sg", 3, 4), A.is_equal, b("sg", 4, 5), A.mult)
-    act(b("e2", 0, 49), b("z2", 0, 49))
+    lin(cg(13), cB, 16.0, cG)
+    ts(b("zi"), b("iv", 0, 136), -8.0, A.add, cg(13), A.is_equal)
+    ts(b("mz"), b("iv", 0, 48), -16.0, A.add, cB, A.is_equal)
+    ts(b("mx"), b("mx"), cB, A.is_equal)
+    lin(cg(15), cB, 8.0, float(NR - 1))
+    ts(b("lt"), b("iv", 0, 136), cg(15), A.is_equal)
+    lin(cg(16), cP7, 16.0, cP3)
+    ts(b("pmt"), i128, cg(16), A.is_equal)
+    lin(cg(9), cG, 2.0, -15.0)
+    lin(cg(17), cB, 4.0, cg(9))
+    ts(cg(18), cP7, 4.0, A.is_equal)
+    ts(b("z2", 0, 65), b("iv", 0, 65), cg(17), A.is_equal, cg(18), A.mult)
+    lin(b("e2", 0, 49), b("z2", 0, 49))
     tt(b("z2", 16, 65), b("z2", 16, 65), b("e2", 0, 49), A.add)
-    ts(b("mk", 0, 2), b("iv", 0, 2), cA, A.not_equal, 1000.0, A.mult)
-    ts(b("mk", 2, 4), b("mk", 0, 2), 4223.5, A.add)
-    ts(b("lf", 48, 64), b("iv", 0, 16), cB, A.is_gt, 32.0, A.mult)
-    ts(b("sg", 6, 7), cB, cg(3), A.add)
-    ts(lA, b("lf", 48, 64), b("sg", 6, 7), A.add)
-    ts(lB, b("iv", 0, 16), cg(3), A.add)
-    iota(b("rs"), [[0, 16], [1, 16]], 0, 0)
-    lin(b("rs"), b("rs"), 1.0, 0.0, AF.Sign)
-    mb = b("mz", 16, 32)
-    fill(b("xm", 0, NV), 0.0)
-    act(b("xm", NV, 2 * NV), b("xs_"), 0.0)
-    for c in range(0, 1152, 288):
-        for name in ("kt", "it", "ito"):
-            lin(b(name, c, c + 288), b("xs_", 0, 288), 0.0, -1.0)
-            ops[-1]["ord"].append(tables_s)
-    for name in ("ld2", "d0", "w3", "yw", "w9", "sdo", "paf"):
+    lin(cg(3), cA, 16.0, 15.0)
+    ts(cg(19), cg(3), cB1, A.subtract)
+    ts(lpq, i2, -8.0, A.mult, cg(19), A.add)
+    lin(cg(20), cB0, -32.0, 32.0)
+    ts(cg(21), cg(20), cg(19), A.add)
+    ts(lpm, i2, -8.0, A.mult, cg(21), A.add)
+    lin(cg(22), cg(0), -64.0, 2032.0 * 4)
+    ts(b("qc"), b("iv", 0, 32), 2.0, A.mult, cg(22), A.add)
+    lin(cg(23), cg(0), -4.0, -4096.0)
+    ts(b("wb", 0, 4), i4, cR3, A.is_equal)
+    ts(b("ws", 0, 1), cR3, 1.5, A.is_lt, float(FAR), A.mult)
+    ts(b("ws", 1, 2), b("ws", 0, 1), b("wb", 2, 3), A.add)
+    ts(cg(24), b("wb", 2, 3), 4.0, A.mult, b("wb", 1, 2), A.subtract)
+    ts(b("ws", 2, 3), b("wb", 0, 1), float(FAR), A.mult, cg(24), A.add)
+    ts(b("wb", 8, 12), i4, b("wb", 2, 3), A.mult, 8.0, A.mult)
+    for t in range(NR):
+        ts(b("lrow", NL * t, NL * t + NL), i128, float(NL * t), A.add, b("wb", 3, 4), A.mult)
+    for h in range(3):
+        fill(b("x1d", h, 96, 3), (0.0, -1.0, 1.0)[h])
+    fill(b("t64", 64, 72), 0.5)
+    fill(b("td", 16, 32), 0.0)
+    fill(b("kg", 2048, 2064), 0.0)
+    for name in ("ito", "it"):
+        for c in range(0, 1152, 288):
+            iota(b(name, c, c + 288), [[0, 288]], -1, 0)
+    for name in ("ld2", "d0", "w3", "x9", "sdo", "paf", "pw", "po"):
         fill(b(name), 0.0)
     cp(b("so", 0, 8), b("pas", 0, 8))
-    tt(b("tg", 0, 8), b("pas", 0, 8), b("dump"), A.subtract)
+    cp(b("tg", 0, 8), b("pas", 0, 8))
     cp(b("pl0"), b("pas"))
     xv, kc = b("xs_"), b("kcs")
+    for c in range(0, NV, 256):
+        lin(b("px%d" % (c // 512), c % 512, c % 512 + 256), b("xs_", c, c + 256))
 
-    def own_parents():
-        mm([(b("pg", 256, 320), top(b("m2h")), top(b("ph")), True, True)])
-        act(b("px"), b("pg", 256, 320))
-        act(b("po"), ind(b("px"), lpo))
-        cp(b("sw", 24, 40), ind(b("px"), lov))
+    def own_parents(t):
+        if t == NR - 1:
+            mm([(b("pe", 128, 136), b("pmt"), b("ph", 0, 8), True, True)])
+            cp(b("sw", 24, 32), b("pe", 128, 136))
+        tt(b("ox"), ind(b("pw"), l8), b("m4"), A.mult)
+        mm([(b("pe", 136, 144), b("ox"), b("b7"), True, True)])
+        lin(b("po", 0, 8), b("pe", 136, 144))
 
     def swap_tables(t, scol):
         cp(b("si", 0, 1), scol)
-        ts(b("si", 1, 2), b("si", 0, 1), 4, A.arith_shift_right)
-        ts(b("si", 2, 3), b("si", 0, 1), 15, A.bitwise_and)
+        ts(b("si", 1, 2), b("si", 0, 1), 128 * 7 + 15, A.bitwise_and)
+        ts(b("si", 2, 3), b("si", 0, 1), 16 * 7, A.bitwise_and)
         cp(b("sc", 8, 10), b("si", 1, 3))
-        ts(b("ohb", 16 * t, 16 * t + 16), b("iv", 0, 16), b("sc", 9, 10), A.is_equal)
-        ts(b("oha"), b("iv", 0, 64), b("sc", 8, 9), A.is_equal)
-        mm([(top(b("pg", 320, 448)), b("ohb", 16 * t, 16 * t + 16), b("idh"), True, True)])
-        cp(top(b("obt")), top(b("pg", 320, 448)))
-        ts(b("oh2", 128 * t, 128 * t + 64), b("oha"), -2048.0, A.mult)
-        ts(b("oh2", 128 * t + 64, 128 * t + 128), b("oha"), b("jt", t, t + 1), A.mult)
+        ts(b("ohm", 128 * t, 128 * t + 128), b("tm"), b("sc", 8, 9), A.is_equal)
+        ts(b("ohu", 8 * t, 8 * t + 8), b("iv", 0, 128, 16), b("sc", 9, 10), A.is_equal)
+        mm([(b("pb", 128, 256), b("ohm", 128 * t, 128 * t + 128), b("idh"), True, True)])
+        lin(b("oht"), b("pb", 128, 256))
+        aff("rhc", b("rhc", 24 * t, 24 * t + 8), b("ohu", 8 * t, 8 * t + 8), -2048.0)
+        aff("rhc", b("rhc", 24 * t + 8, 24 * t + 16), b("ohu", 8 * t, 8 * t + 8), b("jt", t, t + 1))
 
     def grandparents(t, scol):
-        mm([(b("pg", 448, 512), top(b("obt")), top(b("ph")), True, True)])
-        tt(b("ux"), b("pg", 448, 512), b("oha"), A.mult)
+        mm([(b("pg", 448, 456), b("oht"), b("ph", 0, 8), True, True)])
+        tt(b("ux"), b("pg", 448, 456), b("ohu", 8 * t, 8 * t + 8), A.mult)
         red(b("up", 0, 1), b("ux"), A.add)
-        if t > 0:
-            ts(b("uh"), b("bi"), b("up", 0, 1), A.mult)
-            mm([(top(b("pg", 192, 200)), mb, b("uh"), True, True)])
-            cp(top(b("pu", 64, 72)), top(b("pg", 192, 200)))
-        ts(b("sdo", 40, 41), b("up", 0, 1), scol, A.subtract)
-    cp(b("rh2", 0, 64), b("pas"))
-    mm([(top(b("pg", 0, 64)), b("idh", 16 * me, 16 * me + 16), b("rh2", 0, 64), True, True)])
-    cp(top(b("ph")), top(b("pg", 0, 64)))
-    own_parents()
+        cp(b("pu", 32 + 8 * t, 33 + 8 * t), b("up", 0, 1))
+        to_lists(b("pu", 32 + 8 * t, 33 + 8 * t), "dg%d" % t, T.gpl, [b("gpl")], HOPD)
+        aff("up", b("up", 1, 2), scol, -1.0, b("up", 0, 1))
+        aff("up", b("rhc", 24 * t + 16, 24 * t + 24), b("bi"), b("up", 1, 2))
+
+    def decode(bank, c0, li, tg, cut, state, tgt):
+        tt(b(tg, 8, 16), b(bank, c0, c0 + 8), b(tg, 0, 8), A.max)
+        cp(b(li, 0, 8), b(bank, c0 + 8, c0 + 16))
+        cp(tgt, b(tg, 8, 16))
+        ts(b(li, 8, 16), b(li, 0, 8), 4095, A.bitwise_and)
+        ts(b(li, 16, 24), b(li, 0, 8), 12, A.arith_shift_right, 2 ** 19 + 1, A.bitwise_and)
+        cp(cut, b(li, 8, 16))
+        ts(state, b(li, 16, 24), 2.0, A.min)
+    fill(b("ph", 8, 16), 0.0)
+    cp(b("ph", 0, 8), b("pin"))
+    cp(b("pw", 0, 8), b("pin"))
+    own_parents(0)
     swap_tables(0, b("po", 0, 1))
     grandparents(0, b("po", 0, 1))
+    opening = last("G")
+    ops[opening]["plus"] = FIRST + KNOB["open"]
+    ops[opening]["cost"] += ops[opening]["plus"]
 
     nb = 128 // BLK
     cp(ind(b("xm"), xoA), b("xs_", 0, NL))
-    late, lists = [], []
     for t in range(NR):
         so = b("so", 8 * t, 8 * t + 8)
         scol = b("po", 0, 1) if t == 0 else b("w3", 3 * me + 2, 3 * me + 3)
-        after.pop("V", None)
-        after.pop("S", None)
         cp(b("cut"), ind(b("cds"), so))
-        act(b("xg"), ind(xv, so))
-        if t == 0:
-            ops[tables_s]["ord"].append(last("S"))
-            after["S"] = tables_s
+        lin(b("xg"), ind(xv, so))
         cp(ind(b("xm"), xoB), b("xg"))
-        c0, pieces = 0, []
-        for i in range(len(KS)):
-            pieces += [("S", KS[i])] + ([("V", KV[i])] if i < len(KV) else [])
-        for (e, w) in pieces:
-            (act if e == "S" else cp)(b("kg", c0, c0 + w), ind(kc, b("cut", c0 // 16, (c0 + w) // 16)))
-            after[e] = len(ops) - 1
+        c0 = 0
+        for (e, w) in PIECES[min(t, 1)]:
+            (lin if e == "S" else cp)(b("kg", c0, c0 + w), ind(kc, b("cut", c0 // 16, (c0 + w) // 16)))
             its = []
             for m in range(c0 // BLK, (c0 + w) // BLK):
                 q, blk = m // nb, m % nb
-                its.append((b("pa%d" % (q // 8), (q % 8) * BLK, (q % 8 + 1) * BLK, 1, blk * BLK, blk * BLK + BLK),
-                            b("kg", m * BLK, m * BLK + BLK), b("xm", m * BLK, m * BLK + BLK), True, True))
+                its.append((b("pa0", q, 256, 16, blk * BLK, blk * BLK + BLK), b("kg", m * BLK, m * BLK + BLK),
+                            b("xm", 2 * m + 1, 2048, 128), True, True))
+                its.append((b("pa0", q, 256, 16, blk * BLK, blk * BLK + 16), b("kg", m * BLK, m * BLK + 16),
+                            b("xm", 2 * m, 2048, 128), True, True))
             mm(its)
             c0 += w
-        act(b("ev", 0, 256), b("pa0", 0, 256))
-        cp(b("ev", 256, 512), b("pa1", 0, 256))
         B1 = 256 * t
+        if t > 0 and KNOB["late"] == 1:
+            ops[late]["ord"].append(last("V"))
         for h in range(2):
-            ts(b("sb1", B1 + 128 * h, B1 + 128 * h + 128), ind(b("ev"), b("lst", 16 + 8 * h, 24 + 8 * h)), sgn, A.mult, OFF, A.add)
-            after["V"] = last("V")
+            ts(b("sb1", B1 + 128 * h, B1 + 128 * h + 128), b("pa0", 128 * h, 128 * h + 128), sgn, A.mult, OFF, A.add)
+        if t > 0 and KNOB["late"] == 2:
+            ops[late]["ord"].append(last("V"))
         spread(lambda i: b("sb1", B1 + 32 * i, B1 + 32 * i + 32), ("ld1", B1), 32, True, [b("ld2")] if t == 0 else [])
-        lanes_end = last("V")
-        for k in late:
-            ops[k]["ord"].append(lanes_end)
-        after.pop("V", None)
-        after.pop("S", None)
+        if t == 0:
+            ops[last("G") - 1]["ord"].append(opening)
+        if t < NR - 1:
+            lane_features(t + 1, 2.0, [b("ld1", B1, B1 + 224)])
 
         cp(b("cs"), b("cut"))
         mm([(b("pb", 384, 512), b("rep"), b("cs"), True, True)])
-        act(b("ec"), b("pb", 384, 512))
+        lin(b("ec"), b("pb", 384, 512))
         cp(b("goff"), ind(b("ec"), l1))
-        after["V"] = lanes_end
         cp(b("gg"), ind(b("tb"), b("goff")))
         mm([(b("pb", 0, 64), b("gg", 128 * h, 128 * h + 128), b("z2", 1 - h, 65 - h), h == 0, h == 1) for h in range(2)])
-        turn(b("ct", 0, 32), b("pb", 32, 64))
-        own_slot("f1", 32, b("sb1", B1 + 224, B1 + 256), b("pb", 0, 32))
-        ts(b("ct", 32, 64), b("ct", 0, 32), -0.5, A.add)
-        act(b("wo"), ind(b("ct", 0, 32), lB))
-        tt(b("less"), ind(b("ct"), lA), b("wo"), A.is_lt)
-        scan(b("scan"), b("rs"), b("less"))
-        key, base = b("scan", 15, 256, 16), -16.0
-        cp(b("sh", 0, 1), scol)
-        ts(b("dg"), b("idh"), scol, A.mult)
-        mm([(b("pd", 0, 128), b("one"), b("dg"), True, False), (b("pd", 0, 128), b("idh"), b("bigu"), False, True),
-            (b("pd", 128, 129), b("pmt"), b("sh", 0, 1), True, True)])
-        s2 = b("sc", 0, 1)
-        act(s2, b("pd", 128, 129))
-        lin(b("e2"), b("pd", 0, 128), -1.0, s2, AF.Sign)
-        lin(b("e3"), b("e2"), 1.0, 0.0, AF.Square, b("sc", 1, 2))
-        lin(b("sc", 2, 3), s2, 1.0, -(NL * t + 63.5), AF.Square)
-        ts(b("sc", 3, 4), b("sc", 2, 3), 4096.0, A.min, b("sc", 1, 2), A.add)
-        ts(b("sc", 4, 6), b("mk", 2, 4), b("sc", 3, 4), A.is_lt, -8192.0, A.mult)
-        act(b("cq"), ind(b("ec"), l2))
-        for a in range(2):
-            ts(b("rm", 16 * a, 16 * a + 16), key, base, A.add, b("sc", 4 + a, 5 + a), A.mult)
-        turn(b("rt"), b("rm"))
-        tt(b("qq", 32, 64), b("rt"), b("cq"), A.add)
-        ts(b("qq", 0, 32), b("qq", 32, 64), 4096.0, A.add)
-        ops[-1]["bias"] = KNOB["tables"]
-        ts(b("dh"), b("m2h"), scol, A.mult)
-        mm([(b("pb", 72, 80), b("dh"), b("bi"), True, True)])
-        tt(b("tgo", 0, 8), b("pb", 72, 80), b("dump"), A.subtract)
-
-        cp(b("f1", 0, 128), b("ld1", B1, B1 + 128))
-        tt(b("x1"), b("f1", 0, 64), b("f1", 64, 128), A.add)
-        tt(b("y1", 64, 96), b("x1", 32, 64), b("x1", 0, 32), A.subtract)
-        tt(b("f1", 224, 256), b("f1", 224, 256), b("y1", 64, 96), A.add)
-        cp(b("f1", 128, 224), b("ld1", B1 + 128, B1 + 224))
-        tt(b("y1", 0, 64), b("f1", 128, 192), b("f1", 192, 256), A.add)
-        compare(b("sd"), ("y1", 0), 32)
-        tt(b("mq"), ind(b("sd"), ldup), b("qq"), A.mult)
-        tt(b("v32"), b("mq", 0, 32), b("mq", 32, 64), A.subtract)
-        turn(b("t32"), b("v32"))
-        B2 = 16 * t
-        own = B2 + 8
-        red(b("ld2", own, own + 1), b("t32"), A.max, True)
-        after["V"] = last("V")
-        to_all(T.ld2[:, own:own + 1], [T.ld2[:, B2 + me:B2 + me + 1] for r in peers], [b("ld2", own, own + 1)], [b("ld2", B2, own)], HOP)
-        for k in lists:
-            ops[k]["ord"].append(last("G"))
-        win = b("ld2", B2, own + 8)
-        if t < NR - 1:
-            cp(ind(b("xm"), xoA), b("xs_", NL * t + NL, NL * t + 2 * NL))
-
-        mm([(top(b("pf_", 0, 64)), top(b("idh", 0, 16)), top(b("ph")), True, False)])
-        dec = b("ld2", own, own + 1)
-        ts(b("gmo"), b("m1"), dec, A.mult)
-        lin(b("gvo"), b("mr6"), dec, 0.0)
-        mm([(b("pb", 64, 72), b("gmo"), b("r1"), True, True)])
-        cp(b("lio", 0, 8), b("pb", 64, 72))
-        ts(b("tgo", 8, 16), b("pb", 64, 72), 8000.0, A.is_gt)
-        ts(b("lio", 8, 16), b("lio", 0, 8), 4095, A.bitwise_and)
-        tt(b("tgo", 16, 24), b("tgo", 8, 16), b("tgo", 0, 8), A.mult)
-        cp(b("sw", 8, 16), b("lio", 8, 16))
-        tt(b("tgo", 24, 32), b("tgo", 16, 24), b("dump"), A.add)
-        cp(b("sw", 16, 24), b("tgo", 24, 32))
-        mm([(b("pb", 256, 384), b("mr3"), b("iv", NL * t, NL * t + NL), True, False), (b("pb", 256, 384), b("gvo"), b("pm"), False, True)])
-        act(b("wvo"), b("pb", 256, 384))
-        tt(b("sro"), ind(b("tb"), b("sw", 8, 16)), b("wvo"), A.add)
-        cp(ind(b("ito"), b("sw", 16, 24)), b("sro"))
-        act(b("iao"), ind(b("ito"), b("sw", 24, 32)))
-        mm([(b("pg", 64, 128), b("iao"), b("zi", 72, 136), True, False), (b("pg", 64, 128), b("sro"), b("zi", 64, 128), False, True)])
-        act(b("eo"), b("pg", 64, 128))
-        cp(b("vo", 0, 9), b("eo", 32, 41))
-        ts(b("vo", 16, 25), b("vo", 0, 9), 12, A.arith_shift_right, 1, A.bitwise_and)
-        ts(b("sdo", 0, 8), b("eo", 48, 56), NL * t - 0.5, A.is_lt, 4.0, A.mult)
-        ts(b("sdo", 8, 9), b("eo", 40, 41), 8000.0, A.is_lt, 4.0, A.mult)
-        ts(b("sdo", 9, 10), b("eo", 48 + t, 49 + t), b("jt", t, t + 1), A.is_equal, 2.0, A.mult)
-        tt(b("sdo", 16, 25), b("vo", 16, 25), b("sdo", 0, 9), A.add)
-        lin(b("sdo", 16 + t, 17 + t), b("sdo", 16 + t, 17 + t), 1.0, b("sdo", 9, 10))
-        tt(b("sdo", 32, 40), b("eo", 48, 56), b("po", 0, 8), A.subtract)
-        tt(b("gd"), ind(b("sdo", 32, 48), ly), b("m3"), A.mult)
-        ops[-1]["bias"] = KNOB["own"]
-
-        for c in range(DIRECT[t], NV, 256):
-            act(b("pa0", c - 512, c - 256) if c >= 512 else b("pd", c - DIRECT[t], c - DIRECT[t] + 256), b("xs_", c, c + 256))
-        if t == 0:
-            for h in range(4):
-                act(b("xp", 256 * h, 256 * h + 256), ind(xv, b("pl0", 16 * h, 16 * h + 16)))
-            act(b("xps"), ind(b("xp"), so))
+        own_slot(b("x1", 2, 96, 3), b("sb1", B1 + 224, B1 + 256), b("pb", 0, 32))
+        aff("cc", b("cc", 0, 32), b("pb", 32, 64), -1.0, TOP)
+        aff("cc", b("cc", 32, 64), b("pb", 32, 64), 1.0, -TOP)
+        aff("sh", b("sh", 1, 2), scol)
+        ts(b("sh", 2, 3), scol, NL * t - 0.5, A.is_lt, 32768.0, A.mult)
+        ts(b("sh", 3, 4), scol, NL * t + NL - 0.5, A.is_gt, 32768.0, A.mult)
+        aff("dg", b("dg"), b("idh"), scol)
+        mm([(b("pc_", 128, 256), b("one"), b("dg"), True, False), (b("pc_", 128, 256), b("idh"), b("bigu"), False, True),
+            (b("pc_", 257, 259), b("pmt"), b("sh", 1, 3), True, False), (b("pc_", 258, 259), b("pmt"), b("sh", 3, 4), False, True)])
+        if "first" in ON_SCALAR:
+            lin(b("sc", 0, 1), b("pc_", 257, 258))
+            lin(b("e2"), b("pc_", 128, 256), -1.0, b("sc", 0, 1), AF.Sign)
+            lin(b("e3"), b("e2"), 1.0, 0.0, AF.Square, b("sc", 1, 2))
+            ts(b("sc", 4, 5), b("sc", 1, 2), 127.5, A.is_gt, b("pc_", 258, 259), A.mult)
         else:
-            act(b("xps"), ind(xv, b("pl%d" % t, 64, 72)))
-        if t < NR - 1:
-            pn = b("pnl", 16 * t, 16 * t + 8)
-            nx = NL * (t + 1)
-            pc = b("pc", 0, 8)
-            act(b("xpn", 0, NL), b("xs_", nx, nx + NL))
-            cp(pn, b("pl%d" % t, 8 * t + 8, 8 * t + 16))
-            act(b("xpn", NL, 2 * NL), ind(xv, pn))
-            cp(b("paf", 0, 8), pn)
-            act(b("pz"), ind(b("paf"), lpa))
-            mm([(b("pe", 64, 128), b("m2"), b("pz"), True, True)])
-            act(b("py"), b("pe", 64, 128))
-            act(b("pc"), ind(b("py"), lpo))
-
-        lv = b("pa1", 0, 8)
-        tt(b("gm"), ind(win, gl2), b("m1"), A.mult)
-        mm([(lv, b("gm"), b("r1"), True, True)])
-        cp(b("li", 0, 8), lv)
-        ts(b("tg", 8, 16), lv, 8000.0, A.is_gt)
-        ts(b("li", 8, 16), b("li", 0, 8), 4095, A.bitwise_and)
-        tt(b("tg", 16, 24), b("tg", 8, 16), b("tg", 0, 8), A.mult)
-        cp(b("cl"), b("li", 8, 16))
-        tt(b("tg", 24, 32), b("tg", 16, 24), b("dump"), A.add)
-        cp(b("tgt"), b("tg", 24, 32))
-        act(b("kcc"), ind(kc, b("cl")))
-        cp(ind(b("kt"), b("tgt")), b("kcc"))
-        act(b("gv"), ind(win, lv2))
-        mm([(b("pb", 128, 256), b("mr3"), b("iv", NL * t, NL * t + NL), True, False)])
-        mm([(b("pb", 128, 256), b("gv"), b("pm"), False, True)])
-        act(b("wv"), b("pb", 128, 256))
-        if t < NR - 1:
-            B3 = 128 * t
-            tt(b("pf"), ind(b("kt"), b("pnl", 16 * t, 16 * t + 16)), b("xpn"), A.mult)
-            mm([(b("pa1", 16 + 8 * w, 24 + 8 * w), b("pf", 128 * w, 128 * w + 128), b("bi"), True, True) for w in range(2)])
-            ts(b("sb3", 16 * t, 16 * t + 16), b("pa1", 16, 32), sgn, A.mult, OFF, A.add)
-            to_all(T.sb3[:, 16 * t:16 * t + 16], [T.ld3[:, B3 + 16 * i:B3 + 16 * i + 16] for i in range(n - 1)],
-                   [b("sb3", 16 * t, 16 * t + 16)], [b("ld3", B3, B3 + 112)], HOP)
-            after["V"] = last("V")
-        B9 = 72 * t
-        first = [True]
-
-        def sums(ys):
-            mm([(b("pc_", 0, 72), b("pr", 128 * y, 128 * y + 128), b("z9", 8 - y, 80 - y), first[0] and y == ys[0], y == 7) for y in ys])
-            first[0] = False
-        for c in (0, 4, 1, 2, 3):
-            if c == 4:
-                tt(b("pr", 1024, 1152), b("kcc"), b("xps"), A.mult)
-                sums([8])
-                continue
-            kj = ind(b("kt"), b("pl%d" % t, 16 * c, 16 * c + 16))
-            if 256 * c < DIRECT[t]:
-                tt(b("pr", 256 * c, 256 * c + 256), kj, b("xs_", 256 * c, 256 * c + 256), A.mult)
-            else:
-                act(b("kj", 256 * c, 256 * c + 256), kj)
-                tt(b("pr", 256 * c, 256 * c + 256), b("kj", 256 * c, 256 * c + 256),
-                   b("pa0", 256 * c - 512, 256 * c - 256) if c > 1 else b("pd", 256 * c - DIRECT[t], 256 * c + 256 - DIRECT[t]), A.mult)
-            sums([2 * c, 2 * c + 1])
-        ts(b("sb9", B9, B9 + 72), b("pc_", 0, 72), sgn, A.mult, OFF, A.add)
-        last_conv = last("V")
-        spread(lambda i: b("sb9", B9 + 9 * peers[i], B9 + 9 * peers[i] + 9), ("ld9", 64 * t), 9, False)
-        ops[-1]["bias"] = KNOB["sums"] if t < NR - 1 else 0.0
-
-        if t == NR - 1:
-            after["V"] = last_conv
-        tt(b("src"), ind(b("tb"), b("cl")), b("wv"), A.add)
-        if t < NR - 1:
-            cp(ind(b("it"), b("tgt")), b("src"))
-            act(b("ian"), ind(b("it"), pn))
-            mm([(b("pe", 0, 64), b("ian"), b("zi", 8, 72), True, False), (b("pe", 0, 64), b("it", nx, nx + NL), b("zi", 0, 64), False, True)])
-            act(b("ei"), b("pe", 0, 64))
-            own_slot("f3", 16, b("sb3", 16 * t, 16 * t + 16), b("ei", 0, 16))
-            cp(b("vi", 0, 16), b("ei", 32, 48))
-            ts(b("vi", 16, 32), b("vi", 0, 16), 12, A.arith_shift_right, 1, A.bitwise_and)
-            ts(b("sdf", 0, 16), b("ei", 48, 64), NL * t - 0.5, A.is_lt, 2.0, A.mult)
-            tt(b("sdf", 16, 32), b("vi", 16, 32), b("sdf", 0, 16), A.add)
-            tt(b("d1", 0, 24, 3), pc, b("ei", 48, 56), A.subtract)
-            tt(b("d1", 1, 24, 3), b("ei", 48, 56), b("ei", 56, 64), A.subtract)
-            act(b("d1", 2, 24, 3), b("ei", 56, 64))
-            if KNOB["pre"]:
-                after["V"] = last_conv
-            finish_sum("f3", "ld3", B3, 16, ("x3", 0), ("y3", 0), b("b3"))
-            for w in range(2):
-                tt(b("d0", 1 + w, 24, 3), b("b3", 8 * w, 8 * w + 8), b("sdf", 16 + 8 * w, 24 + 8 * w), A.not_equal)
-            scan(b("w3", 0, 24), b("d0"), b("d1"))
-            cp(b("ga"), ind(b("w3"), lso))
-            to_list("pa1", 32, "ga", "mz")
-            cp(b("so", 8 * t + 8, 8 * t + 16), b("pa1", 32, 40))
-            tt(b("tg", 0, 8), b("pa1", 32, 40), b("dump"), A.subtract)
-            swap_tables(t + 1, b("w3", 3 * me + 2, 3 * me + 3))
+            ts(b("e2"), b("pc_", 128, 256), b("pc_", 257, 258), A.subtract)
+            red(b("sc", 1, 2), b("e2"), A.min, True)
+            ts(b("sc", 4, 5), b("sc", 1, 2), 0.5, A.is_gt, b("pc_", 258, 259), A.mult)
+        lin(b("cq"), ind(b("ec"), l2), 1.0 / 2048)
+        turn(b("ct"), b("cq"))
+        tt(b("qq"), ind(b("ct"), lpq), b("qc"), A.add)
 
         k1 = len(ops)
-        mm([(b("pe", 128, 192), b("src"), b("zi", 8, 72), True, True)])
-        act(b("el"), b("pe", 128, 192))
-        ts(b("yw", 16, 24), b("el", 32, 40), 8000.0, A.is_gt)
-        lin(b("yw", 24, 32), b("el", 16, 24), 1.0, 1.0)
-        tt(b("yw", 0, 8), b("yw", 24, 32), b("yw", 16, 24), A.mult)
-        act(b("gy"), ind(b("yw", 0, 16), lyc))
-        to_list("pe", 256, "gy", "mzf")
-        lin(b("ycs", 8 * t, 8 * t + 8), b("pe", 256, 264), 1.0, -1.0)
+        two_step_sum("f1", "ld1", B1, 32, "x1", "y1", b("sd"))
+        if t > 0 and KNOB["listed"]:
+            ops[k1 + KNOB["listed"] - 1]["ord"].append(listed)
+        tt(b("td", 0, 16), b("sd", 0, 16), b("sd", 16, 32), A.subtract)
+        tt(b("v64"), ind(b("td"), ldup), b("cc"), A.mult)
+        turn(b("t64", 0, 64), b("v64"))
+        red(b("sc", 6, 7), b("t64", 0, 65), A.max)
+        ts(b("dd"), ind(b("t64", 0, 64), lpm), b("sc", 6, 7), A.is_equal, b("sc", 4, 5), A.mult)
+        B2 = 48 * t
+        own = B2 + 39
+        scan(b("ld2", B2 + 8, B2 + 40), b("dd"), b("qq"), cg(23), A.add, A.min)
+        to_all(T.ld2[:, own:own + 1], [T.ld2[:, B2 + me:B2 + me + 1] for r in peers], [b("ld2", own, own + 1)], [b("ld2", B2, B2 + 8)],
+               HOP + 0.15)
+        win = b("ld2", B2, B2 + 48)
+        mark = b("wb", 8 + t, 9 + t)
 
-        own_slot("f9", 9, b("sb9", B9 + 9 * me, B9 + 9 * me + 9), b("eo", 0, 9))
-        finish_sum("f9", "ld9", 64 * t, 9, ("x9", 0), ("x9", 40), b("w9", 0, 9))
-        tt(b("w9", 16, 25), b("w9", 0, 9), b("sdo", 16, 25), A.is_equal)
-        ts(b("rh2"), b("oh2", 128 * t, 128 * t + 128), b("w9", 24, 25), A.mult)
-        tt(b("g72"), ind(b("w9", 16, 32), ly), b("gd"), A.mult)
-        mm([(top(b("pg", 128, 192)), b("ohb", 16 * t, 16 * t + 16), b("rh2", 64, 128), True, True),
-            (top(b("pf_", 0, 64)), b("ohb", 16 * t, 16 * t + 16), b("rh2", 0, 64), False, False)])
-        act(top(b("sm")), top(b("pg", 128, 192)))
+        mm([(b("pf_", 0, 16), b("idh"), b("ph"), True, False)])
+
+        def vertex_tables():
+            lin(b("eo"), b("pg", 64, 128))
+            aff("sdo", b("sdo", 0, 9), b("pg", 96, 105) if "sdo" in ON_SCALAR else b("eo", 32, 41), 1.0, -8.0 * t)
+            tt(b("sdo", 16, 24), b("eo", 48, 56), b("po", 0, 8), A.subtract)
+            ts(b("sdo", 16 + t, 17 + t), b("eo", 48 + t, 49 + t), b("jt", t, t + 1), A.not_equal, b("sdo", 16 + t, 17 + t), A.mult)
         if t == NR - 1:
-            after["S"] = last("S")
-            dma("S", [(T.yc[:, :], T.ycs[:, :])], [b("ycs")], [])
-        mm([(top(b("pf_", 8 * t, 8 * t + 8)), mb, b("g72", 64, 72), False, False),
-            (top(b("pf_", 0, 64)), mb, b("g72", 0, 64), False, True)])
-        tt(top(b("pw")), top(b("pf_", 0, 64)), top(b("sm")), A.max)
-        dn = "dp%d" % (t + 1)
-        lo = top(b("pw"))
+            aff("dh", b("dh"), b("m2h"), scol)
+            mm([(b("pb", 80, 88), b("dh"), b("bi"), True, True)])
+            lin(b("tgo", 0, 8), b("pb", 80, 88))
+            aff("gmo", b("gmo"), b("m1"), b("ld2", own, own + 1))
+            mm([(b("pb", 64, 80), b("gmo"), b("r1"), True, True)])
+            decode("pb", 64, "lio", "tgo", b("sw", 8, 16), b("sw", 0, 8), b("sw", 16, 24))
+            lin(b("wvo"), ind(b("ws"), b("sw", 0, 8)), 1.0, mark)
+            tt(b("sro"), ind(b("tb"), b("sw", 8, 16)), b("wvo"), A.min)
+            tt(ind(b("ito"), b("sw", 16, 24)), b("sro"), b("lrow", NL * t, NL * t + NL), A.add)
+            lin(b("iao", 0, 128), ind(b("ito"), b("sw", 24, 32)))
+            mm([(b("pg", 64, 128), b("iao", 0, 128), b("zi", 72, 136), True, False), (b("pg", 64, 128), b("sro"), b("zi", 64, 128), False, True)])
+            vertex_tables()
+
+        pl = "pl%d" % t
+        lin(b("xps"), ind(xv, b("gpl")))
         if t < NR - 1:
-            lo = top(b("pu"))
-            cp(top(b("ph")), top(b("pw")))
-            cp(top(b("pu", 0, 64)), top(b("pw")))
-            grandparents(t + 1, b("w3", 3 * me + 2, 3 * me + 3))
-            own_parents()
-            late = [k for k in range(k1, len(ops)) if ops[k]["eng"] == "V" and KNOB["late"]]
-        dma("Y", [(T[dn][me], ap(lo))], [lo], [(dn, me, me + 1)])
-        to_all(T[dn][me], [T[dn][me] for r in peers], [(dn, me, me + 1)], [(dn, r, r + 1) for r in peers], HOPD)
-        ops[-1]["bias"] = KNOB["list"] if t < NR - 1 else 0.0
-        lists = [last("G")] if KNOB["behind"] else []
+            pn = b(pl, 8 * t + 8, 8 * t + 16)
+            nx = NL * (t + 1)
+            pc = b("pc", 0, 8)
+            lin(b("xpn"), ind(xv, pn))
+            lin(b("pe", 256, 384), b("xpn"))
+            cp(b("paf", 0, 8), pn)
+            lin(b("pz"), ind(b("paf"), lpa))
+            mm([(b("pe", 64, 128), b("m2"), b("pz"), True, True)])
+            lin(b("py"), b("pe", 64, 128))
+            lin(b("pc"), ind(b("py"), lpo))
+
+        tt(b("gm"), ind(win, gl2), b("m1"), A.mult)
+        mm([(b("pa0", 256, 272), b("gm"), b("r1"), True, True)])
+        ts(b("ck"), b("pa0", 256, 264), 2047.47, A.add, 2048.0, A.min)
+        decode("pa0", 256, "li", "tg", b("cl", 0, 8), b("cl", 8, 16), b("tgt"))
+        (cp if KNOB["kcc"] else lin)(b("kcc"), ind(b("kg"), b("ck")))
+        if KNOB["kcc"]:
+            for k in (-5, -4):
+                ops[k]["ord"].append(len(ops) - 1)
+        cp(ind(b("kt"), b("tgt")), b("kcc"))
         if t < NR - 1:
-            dma("Y", [(T["pl%d" % (t + 1)][:, :], T[dn][:])], [(dn, 0, 8)], [b("pl%d" % (t + 1))], DMAT + 0.3)
+            B3 = 128 * t
+            tt(b("pf", 128, 256), b("kt", nx, nx + NL), b("pe", 256, 384), A.mult)
+            tt(b("pf", 0, 128), ind(b("kt"), pn), b("xs_", nx, nx + NL), A.mult)
+            for w in (1, 0):
+                mm([(b("pa0", 272 + 8 * w, 280 + 8 * w), b("pf", 128 * w, 128 * w + 128), b("bi"), True, True)])
+            ts(b("sb3", 16 * t, 16 * t + 16), b("pa0", 272, 288), sgn, A.mult, OFF, A.add)
+            for (i0, i1) in ((0, 4), (4, 7)) if "f3" in KNOB["two"] else ((0, 7),):
+                to_all(T.sb3[:, 16 * t:16 * t + 16], [T.ld3[:, B3 + 16 * i:B3 + 16 * i + 16] for i in range(i0, i1)],
+                       [b("sb3", 16 * t, 16 * t + 16)], [b("ld3", B3 + 16 * i0, B3 + 16 * i1)], HOP - 0.1 + 0.07 * i0 + 0.15 * (i1 - i0 - 4 + (i0 > 0)),
+                       (16 * (i1 - i0), 32), peers[i0:i1])
+                if i0:
+                    ops[-2]["ord"].append(len(ops) - 4)
+        B9 = 72 * t
+        done = []
+        skip = t + 1 if t < NR - 1 else 9
+        w9 = 8 if t < NR - 1 else 9
+
+        def sums(y):
+            c = y - (y > skip)
+            mm([(b("pc_", 0, 72), b("pr", 128 * y, 128 * y + 128), b("z9", 8 - c, 80 - c), not done, len(done) == w9 - 1)])
+            done.append(y)
+
+        def by_scalar(y0, y1):
+            lin(b("kj", 128 * y0, 128 * y1), ind(b("kt"), b(pl, 8 * y0, 8 * y1)))
+            tt(b("pr", 128 * y0, 128 * y1), b("kj", 128 * y0, 128 * y1), b("px%d" % (y0 // 4), 128 * (y0 % 4), 128 * (y0 % 4 + y1 - y0)), A.mult)
+            for y in range(y0, y1):
+                sums(y)
+
+        def by_vector(y0, y1):
+            tt(b("pr", 128 * y0, 128 * y1), ind(b("kt"), b(pl, 8 * y0, 8 * y1)), b("xs_", 128 * y0, 128 * y1), A.mult)
+            for y in range(y0, y1):
+                sums(y)
+        tt(b("pr", 1024, 1152), ind(b("xps"), lpi), b("kcc"), A.mult)
+        sums(8)
+        for (e, y0, y1) in BLOCKS[t]:
+            (by_vector if e == "V" else by_scalar)(y0, y1)
+        ts(b("sb9", B9, B9 + 72), b("pc_", 0, 72), sgn, A.mult, OFF, A.add)
+        summed = last("V")
+        spread(lambda i: b("sb9", B9 + 9 * peers[i], B9 + 9 * peers[i] + w9), ("ld9", 64 * t), w9, t == NR - 1,
+               via=b("sb9", B9, B9 + 72) if t < NR - 1 else None)
+
+        lin(b("wv"), ind(b("ws"), b("cl", 8, 16)), 1.0, mark)
+        tt(b("src"), ind(b("tb"), b("cl", 0, 8)), b("wv"), A.min)
+        lin(b("ycr", 128 * t, 128 * t + 128), ind(b("src"), lpi))
+        dma("Y", [(T.yc[:, 8 * t:8 * t + 8], T.ycr[1:128:16, 128 * t:128 * t + 128])], [b("ycr", 128 * t, 128 * t + 128)], [])
+        if t < NR - 1:
+            tt(ind(b("it"), b("tgt")), b("src"), b("lrow", NL * t, NL * t + NL), A.add)
+            lin(b("ian"), ind(b("it"), pn))
+            mm([(b("pg", 72, 128, 16), b("src"), b("zo"), True, True)])
+            for (e, y0, y1) in BLOCKS[t]:
+                lin(b("iao", 128 * y0, 128 * y1), ind(b("it"), b(pl, 8 * y0, 8 * y1)))
+                for y in range(y0, y1):
+                    mm([(b("pg", 64 + y, 128, 16), b("iao", 128 * y, 128 * y + 128), b("zo"), True, True)])
+            vertex_tables()
+            mm([(b("pe", 0, 64), b("it", nx, nx + NL), b("zi", 0, 64), True, False), (b("pe", 0, 64), b("ian"), b("zi", 8, 72), False, True)])
+            own_slot(b("x3", 2, 48, 3), b("sb3", 16 * t, 16 * t + 16), b("pe", 0, 16))
+            ts(b("sdf"), b("pe", 32, 48), -8.0 * t, A.add)
+            cp(b("d1", 2, 24, 3), b("pe", 56, 64))
+            tt(b("d1", 0, 24, 3), pc, b("pe", 48, 56), A.subtract)
+            tt(b("d1", 1, 24, 3), b("pe", 48, 56), b("d1", 2, 24, 3), A.subtract)
+            k1 = len(ops)
+            two_step_sum("f3", "ld3", B3, 16, "x3", "y3", b("b3"))
+            if KNOB["summed"]:
+                ops[k1 + KNOB["summed"] - 1]["ord"].append(summed)
+            for w in range(2):
+                tt(b("d0", 1 + w, 24, 3), b("b3", 8 * w, 8 * w + 8), b("sdf", 8 * w, 8 * w + 8), A.not_equal)
+            scan(b("w3", 0, 24), b("d0"), b("d1"))
+            cp(b("ga"), ind(b("w3"), lso))
+            mm([(b("pa0", 288, 296, 1, 32 * (gr // 2), 32 * (gr // 2) + 32), b("mz", 16 - 16 * (gr % 2), 48 - 16 * (gr % 2)),
+                 b("ga", 8 * gr, 8 * gr + 8), gr % 2 == 0, gr % 2 == 1) for gr in range(8)])
+            cp(b("so", 8 * t + 8, 8 * t + 16), b("pa0", 288, 296))
+            aff("tg", b("tg", 0, 8), b("pa0", 288, 296))
+            swap_tables(t + 1, b("w3", 3 * me + 2, 3 * me + 3))
+            fill(b("x9", 48 + skip, 49 + skip), 1.0)
+            tt(b("sdo", 16 + skip, 17 + skip), b("w3", 3 * me + 2, 3 * me + 3), b("po", skip, skip + 1), A.subtract)
         else:
-            dma("Y", [(T.yp[:, :], T[dn][:])], [(dn, 0, 8)], [])
+            ts(b("sa", 0, 9), b("sdo", 0, 9), 0.0, A.is_equal)
+            ts(b("sa", 16, 25), b("sdo", 0, 9), 1.0, A.is_equal)
+            tt(b("sa", 16, 25), b("sa", 16, 25), b("sa", 0, 9), A.subtract)
+            for h in range(2):
+                tt(b("sa", 32 + 8 * h, 40 + 8 * h), b("sa", 16 * h, 16 * h + 8), b("sdo", 16, 24), A.mult)
+            tt(b("ox"), ind(b("sa", 32, 40), lx), b("mx"), A.mult)
+            tt(b("gd"), ind(b("sa", 40, 48), lx), b("mx"), A.mult)
+            aff("rhc", b("rh0"), b("rhc", 24 * t, 24 * t + 24), b("sa", 8, 9))
+            aff("rhc", b("rhc", 0, 24), b("rhc", 24 * t, 24 * t + 24), b("sa", 24, 25))
+            mm([(b("pf_", 0, 8), b("ox"), b("bi"), False, False), (b("pf_", 0, 16), b("ohm", 128 * t, 128 * t + 128), b("rh0", 0, 16), False, False),
+                (b("pf_", 0, 8), b("lt", 0, 128), b("rh0", 16, 24), False, False)])
 
-    m = len(ops)
-    succ = [[] for _ in range(m)]
-    for k in range(m):
-        for j in ops[k]["deps"]:
-            succ[j].append(k)
-    behind = [[] for _ in range(m)]
-    for k in range(m):
-        for j in ops[k]["ord"]:
-            behind[j].append(k)
-    left = [len(succ[k]) + len(behind[k]) for k in range(m)]
-    todo = [k for k in range(m) if left[k] == 0]
-    prio = [0.0] * m
+        parts = [(0, skip, 0), (skip + 1, 9, 1)] if t < NR - 1 else [(0, 9, 0)]
+        cp(b("f9", 7 * w9, 8 * w9) if t < NR - 1 else b("x9", 2, 27, 3), b("sb9", B9 + 9 * me, B9 + 9 * me + w9))
+        for (c0, c1, d) in parts:
+            o = b("f9", 7 * w9 + c0 - d, 7 * w9 + c1 - d) if t < NR - 1 else b("x9", 2, 27, 3)
+            tt(o, o, b("eo", c0, c1), A.subtract if me % 2 == 0 else A.add)
+        late = len(ops)
+        if t < NR - 1:
+            one_step_sum("f9", "ld9", 64 * t, w9, "x9", "w9", b("w9", 20, 20 + w9))
+            for (c0, c1, d) in parts:
+                tt(b("x9", 48 + c0, 48 + c1), b("w9", 20 + c0 - d, 20 + c1 - d), b("sdo", c0, c1), A.is_equal)
+            ts(b("rh2"), b("rhc", 24 * t, 24 * t + 24), b("x9", 56, 57), A.mult)
+            tt(b("gd", 0, 8), b("x9", 48, 56), b("sdo", 16, 24), A.mult)
+            tt(b("g72"), ind(b("gd", 0, 8), lx), b("mx"), A.mult)
+        else:
+            two_step_sum("f9", "ld9", 64 * t, w9, "x9", "w9", b("x9", 48, 57))
+            tt(b("g72"), ind(b("x9", 48, 64), lx), b("gd"), A.mult)
+            ts(b("rh2"), b("rhc", 0, 24), b("x9", 56, 57), A.mult)
+        ohm = b("ohm", 128 * t, 128 * t + 128)
+        mm([(b("pf_", 0, 16), ohm, b("rh2", 0, 16), False, False), (b("pf_", 0, 8), b("lt", NR - 1 - t, NR + 127 - t), b("rh2", 16, 24), False, False)])
+        mm([(b("pf_", 0, 8), b("g72"), b("bi"), False, True)])
+        cp(b("sm"), b("pf_", 0, 16))
+        dn = "dp%d" % (t + 1)
+        lo = b("pw", 0, 8)
+        if t < NR - 1:
+            tt(b("ph", 0, 8), b("sm", 0, 8), b("sm", 8, 16), A.max)
+        tt(lo, b("sm", 0, 8), b("sm", 8, 16), A.max)
+        if t < NR - 1:
+            cp(b("pu", 16 * t, 16 * t + 8), b("ph", 0, 8))
+            listed = last("V")
+            to_lists(b("pu", 16 * t, 16 * t + 8), dn, T["pl%d" % (t + 1)], [b("pl%d" % (t + 1))], HOPD + KNOB["list"])
+            grandparents(t + 1, b("w3", 3 * me + 2, 3 * me + 3))
+            own_parents(t + 1)
+        else:
+            to_lists(lo, dn, T.yp, [], HOPD, [b("sm", 0, 8), b("sm", 8, 16)])
 
-    def lag(j, k):
-        return 0.0 if ops[j]["eng"] == "P" and ops[k]["eng"] == "P" else ops[j]["lat"]
-    while todo:
-        k = todo.pop()
-        prio[k] = max([lag(k, j) + prio[j] for j in succ[k]] + [prio[j] for j in behind[k]] + [ops[k]["lat"]]) + ops[k]["cost"] + 1e-6 \
-            + ops[k]["bias"]
-        for j in ops[k]["deps"] + ops[k]["ord"]:
-            left[j] -= 1
-            if left[j] == 0:
-                todo.append(j)
-    assert max(left) == 0
-    rank = sorted(range(m), key=lambda k: (-prio[k], k))
-    wait = [[(j, ops[j]["cost"] + lag(j, k)) for j in ops[k]["deps"]] + [(j, ops[j]["cost"]) for j in ops[k]["ord"]] for k in range(m)]
-
-    def lay(more):
-        busy = {e: [] for e in "VSPGY"}
-        start = [0.0] * m
-        for k in rank:
-            s, c = 0.0, ops[k]["cost"]
-            for (j, d) in wait[k]:
-                if start[j] + d > s:
-                    s = start[j] + d
-            if ops[k]["eng"] == "X":
-                s += more.get(k, 0.0)
-            else:
-                sl_ = busy[ops[k]["eng"]]
-                lo, hi = 0, len(sl_)
-                while lo < hi:
-                    mid = (lo + hi) // 2
-                    if sl_[mid][1] <= s:
-                        lo = mid + 1
-                    else:
-                        hi = mid
-                while lo < len(sl_) and s + c > sl_[lo][0]:
-                    s = max(s, sl_[lo][1])
-                    lo += 1
-                sl_.insert(lo, (s, s + c))
-            start[k] = s
-        return start
-    shape = tuple((o["eng"], tuple(o["deps"]), tuple(o["ord"]), round(o["cost"], 4)) for o in ops)
+    if core in aids:
+        gone, h = 0, aids.index(core)
+        for (sem, cnt, calls) in relays:
+            if h < len(calls):
+                g.wait_ge(sem, cnt)
+                for tr in calls[h]:
+                    g.remote_dma_fused(tr, local_sem=T.sem.sent)
+                    gone += len(engs)
+        g.wait_ge(T.sem.sent, gone)
+        return
+    shape = tuple((o["eng"], tuple(o["deps"]), tuple(o["ord"])) for o in ops)
     if shape not in LAID:
-        more = {}
-        start = lay(more)
-        bound = max(start) + KNOB["give"]
-        for step in KNOB["steps"]:
-            for k in sorted((k for k in range(m) if ops[k]["eng"] == "X"), key=lambda k: start[k]):
-                more[k] = more.get(k, 0.0) + step
-                if max(lay(more)) > bound:
-                    more[k] -= step
-        LAID[shape] = lay(more)
-    start = LAID[shape]
-    order = sorted(range(m), key=lambda k: (start[k], -prio[k], k))
-    PLAN[me] = (ops, order, start)
+        LAID[shape] = plan(ops)
+    order = LAID[shape]
+    PLAN[me] = (ops, order)
+    succ = [[] for _ in ops]
+    for k, o in enumerate(ops):
+        for j in o["deps"]:
+            succ[j].append(k)
     queue = {"V": g.vector, "S": g.scalar, "P": g.tensor, "G": g, "Y": g.sync}
     count = {"V": 0, "S": 0, "P": 0, "G": 0}
     for k in order:
@@ -840,6 +845,198 @@ def rank_program(g, core, T, topo):
         o = ops[k]
         if o["kind"] in "da" and not any((q, k) in seen for q in queue):
             g.sync.wait_ge(o["sem"][0], o["sem"][1])
+
+
+def plan(ops):
+    m = len(ops)
+    succ = [[] for _ in range(m)]
+    behind = [[] for _ in range(m)]
+    for k in range(m):
+        for j in ops[k]["deps"]:
+            succ[j].append(k)
+        for j in ops[k]["ord"]:
+            behind[j].append(k)
+
+    def lag(j, k):
+        return 0.0 if ops[j]["eng"] == "P" and ops[k]["eng"] == "P" else ops[j]["lat"]
+    prio, rank, back = [0.0] * m, list(range(m)), []
+    left = [len(succ[k]) + len(behind[k]) for k in range(m)]
+    todo = [k for k in range(m) if left[k] == 0]
+    while todo:
+        k = todo.pop()
+        back.append(k)
+        for j in ops[k]["deps"] + ops[k]["ord"]:
+            left[j] -= 1
+            if left[j] == 0:
+                todo.append(j)
+    then = [[(j, lag(k, j) + ops[k]["cost"]) for j in succ[k]] + [(j, ops[k]["cost"]) for j in behind[k]] for k in range(m)]
+
+    def weigh(urge):
+        for k in back:
+            p, q = ops[k]["lat"] + ops[k]["cost"], 0.0
+            for (j, d) in then[k]:
+                if prio[j] + d > p:
+                    p = prio[j] + d
+                if prio[j] > q:
+                    q = prio[j]
+            prio[k] = max(p + urge.get(k, 0.0), q) + 1e-6
+        rank.sort(key=lambda k: (-prio[k], k))
+    wait = [[(j, ops[j]["cost"] + lag(j, k)) for j in ops[k]["deps"]] + [(j, ops[j]["cost"]) for j in ops[k]["ord"]] for k in range(m)]
+
+    def lay(more):
+        busy = {e: [] for e in "VSPGY"}
+        start = [0.0] * m
+        for k in rank:
+            s, c = 0.0, ops[k]["cost"]
+            for (j, d) in wait[k]:
+                if start[j] + d > s:
+                    s = start[j] + d
+            s += more.get(k, 0.0)
+            if ops[k]["eng"] != "X":
+                sl_ = busy[ops[k]["eng"]]
+                lo, hi = 0, len(sl_)
+                while lo < hi:
+                    mid = (lo + hi) // 2
+                    if sl_[mid][1] <= s:
+                        lo = mid + 1
+                    else:
+                        hi = mid
+                while lo < len(sl_) and s + c > sl_[lo][0]:
+                    s = max(s, sl_[lo][1])
+                    lo += 1
+                sl_.insert(lo, (s, s + c))
+            start[k] = s
+        return start
+
+    def laid(urge, more):
+        weigh(urge)
+        start = lay(more)
+        return sorted(range(m), key=lambda k: (start[k], -prio[k], k))
+    order = laid({}, {})
+
+    cases = []
+    for (fc, fw, row, fd, st) in KNOB["cases"]:
+        cost = [(o["cost"] - o.get("plus", 0.0)) * (fc if o["kind"] == "c" else 1.0) for o in ops]
+        lat = [o["lat"] * fw if o["kind"] == "c" else 0.2 * fw if o["kind"] == "a" else o["lat"] + fd for o in ops]
+        rows = [o["rows"][0] * (row + o["rows"][1] / 12e3) if "rows" in o else None for o in ops]
+        ons = {k: o["on"][1] * (row + o["on"][2] / 12e3) for k, o in enumerate(ops) if "on" in o}
+        cases.append((cost, lat, rows, ons, CALL + st, [[(j, cost[j] + (0.0 if ops[j]["eng"] == "P" and o["eng"] == "P" else lat[j])) for j in o["deps"]
+                                         if ops[j]["kind"] != "r"] for o in ops]))
+    eng = [o["eng"] for o in ops]
+    local = set(k for k in range(m) if ops[k]["kind"] == "d")
+
+    def run(order, case):
+        cost, lat, rows, ons, go, waits = case
+        free, prev = {}, {}
+        start, why, land = [0.0] * m, [None] * m, {}
+        end, tail, wire, aid, used = 0.0, 0, -1.0, -1.0, 0.0
+        for k in order:
+            e = eng[k]
+            s, w = 0.0, None
+            if e == "X":
+                s, w = land[ops[k]["by"]], (ops[k]["by"], False)
+            elif e in free:
+                s, w = free[e], (prev[e], True)
+            for (j, d) in waits[k]:
+                if start[j] + d > s:
+                    s, w = start[j] + d, (j, False)
+            if rows[k] is not None:
+                t0 = s + go + (FIRST + 0.5 if wire < 0 else 0.0)
+                if k in ons:
+                    if wire < 0:
+                        wire = t0 + rows[k]
+                    land[k] = t0 + rows[k] + 0.2 + go + (FIRST if aid < 0 else 0.0)
+                    aid = land[k] = max(land[k], aid) + ons[k]
+                else:
+                    used = max(t0, wire)
+                    wire = land[k] = used + rows[k]
+            start[k], why[k] = s, w
+            if k in local and used < s + cost[k] + lat[k] - 0.8 < wire:
+                free[e], prev[e] = s + cost[k], k
+                start[k] = wire + 0.8 - cost[k] - lat[k]
+                continue
+            free[e], prev[e] = s + cost[k], k
+            if s + cost[k] + lat[k] > end:
+                end, tail = s + cost[k] + lat[k], k
+        KNOB["start"] = start
+        return end, why, tail
+    base = [run(order, c)[0] for c in cases]
+
+    def score(order):
+        return sum(run(order, c)[0] / t0 for c, t0 in zip(cases, base))
+    needs = [set(o["deps"]) | set(o["ord"]) for o in ops]
+    urge, more, best = {}, {}, score(order)
+    for _ in range(KNOB["sweeps"]):
+        for k in range(m):
+            if eng[k] == "X" or ops[k]["cost"] >= KNOB["long"]:
+                for (d, step) in ((more, 0.3), (more, 1.0), (urge, 0.5), (urge, -0.5), (urge, 2.0), (more, -0.3)):
+                    old = d.get(k, 0.0)
+                    if d is urge or old + step >= 0:
+                        d[k] = old + step
+                        new = laid(urge, more)
+                        sc = score(new)
+                        if sc < best - 1e-4:
+                            order, best = new, sc
+                        else:
+                            d[k] = old
+
+    def moved(order, pos, a, c):
+        i, j = pos[a], pos[c]
+        go, stay = [a], []
+        mark = {a}
+        for k in order[i + 1:j + 1]:
+            if needs[k] & mark:
+                if k == c:
+                    return None
+                mark.add(k)
+                go.append(k)
+            else:
+                stay.append(k)
+        return order[:i] + stay + go + order[j + 1:]
+
+    def ahead(order, pos, a, c):
+        i, j = pos[a], pos[c]
+        go, stay = [c], []
+        want = set(needs[c])
+        for k in order[j - 1:i - 1 if i else None:-1]:
+            if k in want:
+                if k == a:
+                    return None
+                want |= needs[k]
+                go.append(k)
+            else:
+                stay.append(k)
+        return order[:i] + go[::-1] + stay[::-1] + order[j + 1:]
+    best = score(order)
+    for _ in range(KNOB["passes"]):
+        gain = False
+        for case in cases:
+            end, why, k = run(order, case)
+            pairs = []
+            while why[k] is not None:
+                j, same = why[k]
+                if same and j not in needs[k]:
+                    pairs.append((j, k))
+                k = j
+            for (a, c) in pairs:
+                pos = {k: i for i, k in enumerate(order)}
+                if pos[a] > pos[c]:
+                    continue
+                tries = [moved(order, pos, a, k) for k in order[pos[c]:pos[c] + KNOB["reach"]] if eng[k] == eng[c]]
+                before = [k for k in order[max(0, pos[c] - KNOB["reach"]):pos[c]] if eng[k] == eng[c]]
+                tries += [ahead(order, pos, k, c) for k in before[-1::-2]]
+                for new in tries:
+                    if new is not None:
+                        t0 = run(new, case)[0]
+                        if t0 < end - 1e-6:
+                            sc = score(new)
+                            if sc < best - 1e-6:
+                                order, best, gain, end = new, sc, True, t0
+                                break
+        if not gain:
+            break
+    KNOB["len"] = (max(prio), 0, base, [run(order, c)[0] for c in cases])
+    return order
 
 
 PLAN, LAID = {}, {}

from concourse.bass import DstId, RemoteDMATransfer
from concourse.mybir import AluOpType, AxisListType, ActivationFunctionType

NV, NC, NL, NR = 1024, 3584, 128, 3
BLK = 32
OFF = 32768.0
BIG = 4096.0
TOP = 2.0 ** 22
FAR = 2 ** 24 - 1
F32, BF, F16, I32, U16 = "float32", "bfloat16", "float16", "int32", "uint16"

_S = {
    "xs_": (NV, BF), "kcs": (NC, BF), "cds": (NV, I32), "cs": (128, F32), "ec": (128, F32), "rep": (128, F32), "pas": (64, I32), "pin": (8, I32), "tb": (NC, I32),
    "pl0": (64, U16), "pl1": (64, U16), "pl2": (64, U16),
    "ci": (16, I32), "cf": (16, F32), "cg": (32, F32), "iv": (144, F32), "rb": (128, F32), "tm": (128, F32),
    "lf": (96, F32), "lst": (128, U16), "la": (16, F32), "ws": (3, F32), "lrow": (384, F32), "wb": (16, F32),
    "m1": (128, F32), "r1": (16, F32), "m2": (128, F32), "bi": (8, F16), "b7": (8, F16), "m4": (128, F32),
    "pmt": (128, F16), "one": (128, F16), "idh": (128, F16), "bigu": (128, F16), "mz": (48, F16),
    "jt": (8, F32), "lnl": (8, F32), "z9": (80, F16), "z2": (72, F32), "zi": (136, F32),
    "m2h": (128, F16), "dh": (128, F16), "gmo": (128, F32),
    "lio": (32, I32), "tgo": (32, F32), "wvo": (128, F32), "sro": (128, F32), "ito": (1152, F32), "iao": (NV, F32), "zo": (4, F32), "kj": (1152, BF),
    "so": (24, U16), "cut": (128, U16), "xg": (128, BF), "xm": (2048, BF), "kg": (2064, BF),
    "sb1": (3 * 256, U16), "ld1": (3 * 256, U16), "f1": (256, F32), "x1": (96, F32), "x1s": (96, F32), "x1d": (96, F32), "y1": (64, F32),
    "sd": (32, F32), "td": (32, F32), "v64": (64, F32), "t64": (72, F32), "dd": (32, F32), "ld2": (144, F32),
    "sw": (40, U16), "su": (4, U16), "sh": (8, F16), "dg": (128, F16), "goff": (16, U16), "cq": (32, F32), "gg": (256, F32),
    "ct": (32, F32), "cc": (64, F32), "qc": (32, F32), "sc": (16, F32), "si": (8, I32),
    "pnl": (32, U16), "pc": (16, F32), "e2": (128, F32), "e3": (128, F32), "qq": (32, F32), "paf": (16, F32),
    "ux": (8, F32), "up": (16, F32), "pz": (64, F32), "py": (64, F32),
    "gm": (128, F32), "li": (32, I32), "cl": (16, U16), "ck": (8, U16), "tg": (32, F32), "tgt": (8, U16), "kcc": (128, BF), "kt": (1152, BF),
    "xpn": (128, BF), "pf": (256, F16), "sb3": (32, U16), "ld3": (256, U16), "f3": (128, F32), "x3": (64, F32), "y3": (32, F32),
    "b3": (16, F32), "d0": (24, F32), "d1": (24, F32), "w3": (32, F32), "ga": (64, F16), "wv": (128, F32), "src": (128, F32),
    "it": (1152, F32), "ian": (128, F32), "ei": (64, F32), "sdf": (16, F32), "ycr": (384, F32),
    "xps": (128, BF), "gpl": (8, U16), "pr": (1296, F16), "sb9": (3 * 72, U16), "ld9": (3 * 64, U16), "f9": (72, F32),
    "eo": (64, F32), "sdo": (32, F32), "x9": (64, F32), "w9": (32, F32), "po": (16, F32),
    "gd": (128, F32), "g72": (128, F16), "rh2": (24, F16), "rh0": (24, F16), "sa": (48, F32), "sm": (16, F32), "pu": (56, U16), "pw": (16, F32), "ph": (16, F16),
    "mx": (128, F32), "ox": (128, F16), "lt": (136, F16), "ohm": (384, F16), "oht": (128, F16), "ohu": (24, F32), "rhc": (72, F32),
}
PLACE = {}
_n = 0
for _k, (_w, _d) in _S.items():
    if _d == F32 and _w <= 96 and _k != "pw":
        PLACE[_k] = _n
        _n += (_w + 15) // 16 * 16
SCRATCH = {k: ("sbuf", [128, n], d) for k, (n, d) in _S.items() if k not in PLACE}
SCRATCH["small"] = ("sbuf", [128, _n], F32)
BANKS = ["pa0", "px0", "px1", "pb", "pc_", "pe", "pf_", "pg"]
for _b in BANKS:
    SCRATCH[_b] = ("psum", [128, 512], F32)
for _t in range(NR):
    SCRATCH["dg%d" % _t] = ("dram", [8, 128, 1], U16)
SCRATCH["dp1"] = ("dram", [8, 128, 8], U16)
SCRATCH["dp2"] = ("dram", [8, 128, 8], U16)
SCRATCH["dp3"] = ("dram", [8, 128, 8], F32)
SEMAPHORES = ["V", "S", "P", "G", "sent"] + ["d%d" % i for i in range(32)] + ["a%d" % i for i in range(32)] + ["h%d" % i for i in range(8)]
RELAYED = ("sb9",)

CYC, GAT, SCA, PEC, LAT, SLAT, SFIX = 0.0009, 1.56, 3.8, 0.00054, 0.175, 0.05, 0.1
HOPD, START = 1.9, 0.55
HOP, DMAT, CALL, FIRST, DISS = 1.4, 2.0, 0.28, 1.5, 0.12
KNOB = {"give": 0.1, "steps": (0.3,), "loads": (2.9, 4.3, 6.9, 4.0), "passes": 4, "reach": 40, "list": 0.5, "open": 0.3, "late": 1, "kcc": 1, "direct": 0, "two": ("f1", "f3", "f9"), "sweeps": 1, "long": 0.2, "listed": 1, "summed": 1,
        "cases": ((1.0, 1.0, 0.007, 0.0, 0.55), (0.95, 0.97, 0.003, 0.0, 0.4), (1.4, 1.0, 0.008, 0.0, 0.55), (1.02, 1.0, 0.035, 0.1, 0.85),
                  (1.1, 1.1, 0.02, 0.4, 0.9), (1.0, 1.0, 0.04, 0.2, 0.7))}
ON_SCALAR = ["rhc", "up", "first", "dh", "dg", "sh", "sdo", "cc"]
TBV = 2304
PIECES = [[("V", 128), ("S", 192), ("V", 256), ("S", 256), ("V", 320), ("S", 320), ("V", 320), ("S", 256)],
          [("S", 384), ("V", 192), ("S", 256), ("V", 256), ("S", 256), ("V", 256), ("S", 192), ("V", 256)]]
BLOCKS = [[("S", 0, 1), ("S", 2, 4), ("S", 4, 6), ("S", 6, 8)], [("S", 0, 2), ("S", 3, 4), ("S", 4, 6), ("S", 6, 8)],
          [("V", 0, 2), ("S", 4, 6), ("V", 2, 3), ("S", 6, 8), ("S", 3, 4)]]


def bits(engines):
    return sum(1 << e for e in engines)


def rank_program(g, core, T, topo):
    def helpers(c):
        return [x for x in topo.cores_of(c) if x not in T.cores and topo.die(x) == topo.die(c)][:2]
    me = T.rank_of(core)
    if me is None:
        mine = [r for r, c in enumerate(T.cores) if core in helpers(c)]
        if not mine:
            return
        me = mine[0]
    home = T.cores[me]
    aids = helpers(home)
    n = len(T.cores)
    A, AX, AF = AluOpType, AxisListType.X, ActivationFunctionType
    sgn = 1.0 if me % 2 == 0 else -1.0
    ops = []
    hist = {}
    after = {}

    def last(eng):
        return max(k for k in range(len(ops)) if ops[k]["eng"] == eng)

    def b(name, c0=0, c1=None, step=1, p0=0, p1=128):
        if c1 is None:
            c1 = _S[name][0]
        if name in PLACE:
            return ("small", c0 + PLACE[name], c1 + PLACE[name], step, p0, p1)
        return (name, c0, c1, step, p0, p1)

    def ind(win, off):
        return ("#", win, off)

    def ap(x):
        if x[0] == "#":
            return ap(x[1]).indirect(ap(x[2]))
        if x[3] == 1:
            return T[x[0]][x[4]:x[5], x[1]:x[2]]
        return T[x[0]][x[4]:x[5], x[1]:x[2]:x[3]]

    def val(x):
        return ap(x) if isinstance(x, tuple) else x

    def width(x):
        if x[0] == "#":
            return 16 * (x[2][2] - x[2][1])
        return (x[2] - x[1] + x[3] - 1) // x[3]

    def add(eng, fn, reads, writes, cost, lat=None, kind="c", extra=None):
        k = len(ops)
        lat = LAT + (SLAT if eng == "S" else 0.0) if lat is None else lat
        deps, ords = {}, {}
        rl, wl = [], []
        for x in reads:
            if isinstance(x, tuple):
                rl += [x[1], x[2]] if x[0] == "#" else [x]
        for x in writes:
            if x[0] == "#":
                wl.append(x[1])
                rl.append(x[2])
            else:
                wl.append(x)
        for x, wr in [(x, False) for x in rl] + [(x, True) for x in wl]:
            h = hist.setdefault(x[0], [])
            st = x[3] if len(x) > 3 else 1
            for (j, c0, c1, s2, w2) in h:
                if j == k:
                    continue
                meet = (wr or w2) and c0 < x[2] and x[1] < c1 and not (s2 == st and (c0 - x[1]) % st)
                if x[0] in BANKS and (ops[j]["eng"] != eng or eng == "P"):
                    deps[j] = True
                elif meet:
                    deps[j] = True
            h.append((k, x[1], x[2], st, wr))
        if extra is not None:
            deps[extra] = True
        if eng in after:
            ords[after[eng]] = True
        ops.append({"eng": eng, "fn": fn, "deps": sorted(deps), "cost": cost, "lat": lat, "kind": kind, "tag": writes[0][:2] if writes else "",
                    "ord": sorted(j for j in ords if j not in deps)})
        return k

    def short(x):
        return x[0] != "#" and SCRATCH[x[0]][2] in (BF, F16, U16)

    def vcost(out, x, per=1.0, fix=0.05):
        m = width(out)
        if out[0] == "#":
            return fix + m * SCA * CYC
        if x[0] == "#":
            return fix + m * max(GAT, per) * CYC
        return max(m * per, 64) * CYC + (SFIX if fix > 0.05 else 0.0)

    def cp(out, x):
        add("V", lambda: g.vector.tensor_copy(ap(out), ap(x)), [x], [out], vcost(out, x, 0.5 if short(out) and short(x) else 1.0))

    def tt(out, x, y, op):
        two = x[0] not in BANKS and y[0] not in BANKS
        add("V", lambda: g.vector.tensor_tensor(ap(out), ap(x), ap(y), op), [x, y], [out], vcost(out, x, 2.0 if two else 1.0))

    def ts(out, x, s1, op0, s2=None, op1=None):
        if op1 is None:
            fn = lambda: g.vector.tensor_scalar(ap(out), ap(x), val(s1), None, op0)
        else:
            fn = lambda: g.vector.tensor_scalar(ap(out), ap(x), val(s1), val(s2), op0, op1)
        add("V", fn, [x, s1, s2], [out], vcost(out, x, 0.5 if short(out) and short(x) else 1.0))

    def red(out, x, op, ab=False):
        more = {"apply_absolute_value": True} if ab else {}
        add("V", lambda: g.vector.tensor_reduce(ap(out), ap(x), AX, op, **more), [x], [out], vcost(x, x))

    def scan(out, d0, d1, init=0.0, op0=A.mult, op1=A.add):
        add("V", lambda: g.vector.tensor_tensor_scan(ap(out), ap(d0), ap(d1), val(init), op0, op1), [d0, d1, init], [out], vcost(out, d0))

    def turn(out, x):
        add("V", lambda: g.vector.transpose(ap(out), ap(x)), [x], [out], vcost(out, x))

    def fill(out, c):
        add("V", lambda: g.vector.memset(ap(out), c), [], [out], vcost(out, out, 0.5 if short(out) else 1.0))

    def lin(out, x, scale=1.0, bias=0.0, func=AF.Identity, total=None):
        more = {} if total is None else {"accum_out": ap(total)}
        add("S", lambda: g.scalar.activation(ap(out), ap(x), func, bias=val(bias), scale=val(scale), **more),
            [x, scale, bias], [out] + ([total] if more else []), vcost(out, x, 1.0, 0.065) + (0.02 if more else 0.0))

    def aff(tag, out, x, scale=1.0, bias=0.0):
        if tag in ON_SCALAR:
            lin(out, x, scale, bias)
        else:
            ts(out, x, scale, A.mult, bias, A.add)

    def mm(items):
        def fn():
            r = None
            for (o, l, rr, st, sp) in items:
                r = g.tensor.matmul(ap(o), ap(l), ap(rr), st, sp)
            return r
        cost = 0.0
        for (o, l, rr, st, sp) in items:
            cost += max(min(64, width(l)), width(rr)) * (4 if SCRATCH[l[0]][2] == F32 else 1) * PEC
        add("P", fn, [x for it in items for x in it[1:3]], [it[0] for it in items], cost)

    def iota(out, pat, base, cm):
        if SCRATCH[out[0]][2] == I32:
            fn = lambda: g.iota(ap(out), pat, base, cm)
        else:
            fn = lambda: g.iota(ap(out), pat, base, cm, allow_small_or_imprecise_dtypes=True)
        add("G", fn, [], [out], 0.13 + width(out) * 2 * CYC)

    nd = [0]

    def dma(eng, pairs, reads, writes, lat=DMAT):
        sem = T.sem["d%d" % nd[0]]
        nd[0] += 1
        q = g.sync if eng == "Y" else g.scalar

        def fn():
            for (o, i) in pairs:
                q.dma_start(o, i).then_inc(sem, 16)
        k = add(eng, fn, reads, writes, DISS * len(pairs), lat, "d")
        ops[k]["sem"] = (sem, 16 * len(pairs))

    peers = [(me + i) % n for i in range(1, n)]
    engs = topo.engines(home, T.cores[peers[0]])
    for r in peers:
        engs = [e for e in engs if all(e in topo.engines(c, T.cores[r]) for c in [home] + aids)]
    near = [e for e in topo.engines(home, aids[0]) if e in topo.engines(home, aids[1])]
    spare = [e for e in near if e not in engs]

    def address(to, by):
        rid, pid = topo.addr(to, by)
        return DstId(rid=rid, pnc=pid)
    dst = {r: address(T.cores[r], home) for r in peers}
    far = [{r: address(T.cores[r], c) for r in peers} for c in aids]
    na = [0]
    sent = [0]
    relays = []

    def hand_on(src, mid, calls, use, rows):
        sem = T.sem["h%d" % len(relays)]
        per = len(use) // len(calls)
        relays.append((sem, per, calls))
        srcs = src if isinstance(src, list) else [src]
        tr = [RemoteDMATransfer(dst_ids=[address(aids[h], home)], dma_engine_mask=bits(use[h * per:h * per + per]), remote_sem=sem,
                                srcs=[ap(x) for x in srcs], dsts=[mid], alu_op=2 * (len(srcs) - 1)) for h in range(len(calls))]
        sent[0] += len(use)
        k = add("G", lambda: g.remote_dma_fused(tr, local_sem=T.sem.sent), srcs, [], CALL, 0.0, "r")
        ops[k]["rows"], ops[k]["on"] = (128 // per, 32), (len(calls),) + rows
        ops[k]["ord"] += [j for j in range(k) if "on" in ops[j]]
        return k

    def arrive(k, lands, lat, cnt):
        sem = T.sem["a%d" % na[0]]
        na[0] += 1
        k2 = add("X", None, [], lands, 0.0, lat, "a", extra=k)
        ops[k2]["sem"], ops[k2]["by"] = (sem, cnt), k

    def spread(src, land, w, early, more=(), via=None):
        sems = [T.sem["a%d" % na[0]], T.sem["a%d" % (na[0] + (1 if early else 0))]]
        calls, i0 = [], 0
        for many in (4, 2, 1):
            per = len(engs) // many
            calls.append([RemoteDMATransfer(dst_ids=[(far[min(i0, 1)] if via else dst)[peers[i]]], dma_engine_mask=bits(engs[(i - i0) * per:(i - i0 + 1) * per]),
                                            remote_sem=sems[min(i0, 1)], src=ap(src(i)),
                                            dst=ap(b(land[0], land[1] + i * w, land[1] + (i + 1) * w))) for i in range(i0, i0 + many)])
            i0 += many
        if via:
            k = hand_on(via, ap(via), [calls[:1], calls[1:]], spare, (64, 2 * w))
            arrive(k, [b(land[0], land[1], land[1] + 7 * w)], HOP + 1.0, 3 * len(engs))
            return
        sent[0] += 3 * len(engs)
        k1 = add("G", lambda: g.remote_dma_fused(calls[0], local_sem=T.sem.sent), [src(i) for i in range(4)] + list(more), [], CALL, 0.0, "r")

        def fn():
            for tr_ in calls[1:]:
                g.remote_dma_fused(tr_, local_sem=T.sem.sent)
        k2 = add("G", fn, [src(i) for i in range(4, 7)], [], 2 * CALL, 0.0, "r")
        ops[k2]["ord"].append(k1)
        ops[k1]["rows"], ops[k2]["rows"] = (64, 2 * w), (48, 2 * w)
        if early:
            arrive(k1, [b(land[0], land[1], land[1] + 4 * w)], HOP - 0.1, len(engs))
            arrive(k2, [b(land[0], land[1] + 4 * w, land[1] + 7 * w)], HOP + 0.2, 2 * len(engs))
        else:
            arrive(k2, [b(land[0], land[1], land[1] + 7 * w)], HOP - 0.1, 3 * len(engs))

    def to_all(src, dsts, reads, lands, lat, rows=(112, 24), to=peers):
        tr = [RemoteDMATransfer(dst_ids=[dst[r] for r in to], dma_engine_mask=bits(engs), remote_sem=T.sem["a%d" % na[0]],
                                srcs=[src], dsts=dsts)]
        sent[0] += len(engs)
        k = add("G", lambda: g.remote_dma_fused(tr, local_sem=T.sem.sent), reads, [], CALL, 0.0, "r")
        ops[k]["rows"] = rows
        arrive(k, lands, lat, len(to) * len(engs))

    def own_slot(o, own, thr):
        cp(o, own)
        tt(o, o, thr, A.subtract if me % 2 == 0 else A.add)

    def compare(out, y, w):
        ev_, od_ = b(y[0], y[1], y[1] + w), b(y[0], y[1] + w, y[1] + 2 * w)
        if me % 2 == 0:
            tt(out, od_, ev_, A.is_gt)
        else:
            tt(out, ev_, od_, A.is_gt)

    def one_step_sum(f, land, base, w, x, y, out):
        cp(b(f, 0, 7 * w), b(land, base, base + 7 * w))
        tt(b(x, 0, 4 * w), b(f, 0, 4 * w), b(f, 4 * w, 8 * w), A.add)
        tt(b(y, 0, 2 * w), b(x, 0, 2 * w), b(x, 2 * w, 4 * w), A.add)
        compare(out, (y, 0), w)

    def to_lists(lo, dn, to, lands, lat, fold=None):
        share = [peers[:4], peers[4:]] if dn == "dg0" else [peers]
        on = [[[RemoteDMATransfer(dst_ids=[far[h][r] for r in to_], dma_engine_mask=bits(engs), remote_sem=T.sem["a%d" % na[0]],
                                  srcs=[T[dn][me]], dsts=[T[dn][me] for r in to_])]] for h, to_ in enumerate(share)]
        if dn == "dp3" and KNOB["direct"]:
            to_all(ap(lo), [T[dn][me] for r in peers], [lo], [(dn, r, r + 1) for r in peers], HOP + 0.3, (112, 32))
        else:
            k = hand_on(fold or lo, T[dn][me], on, near if dn in ("dg0", "dp3") else spare, (7, 512))
            arrive(k, [(dn, r, r + 1) for r in peers], lat, (n - 1) * len(engs))
        dma("S" if dn == "dg0" else "Y", [(to[16 * me:16 * me + 16, :], ap(lo))], [lo], lands)
        cuts = ((0, me), (me + 1, n)) if 0 < me < n - 1 else ((1, 4), (4, n)) if me == 0 else ((0, 4), (4, me))
        rest = [(to[16 * r0:16 * r1, :], T[dn][r0:r1]) for (r0, r1) in cuts]
        if lands:
            dma("Y", rest, [(dn, 0, 8)], lands, DMAT + 0.2)
        else:
            for e, pair in zip("YS", rest):
                dma(e, [pair], [(dn, 0, 8)], [])

    def two_step_sum(f, land, base, w, x, y, out):
        if f not in KNOB["two"]:
            cp(b(f, 7 * w, 8 * w), b(x, 2, 3 * w, 3))
            return one_step_sum(f, land, base, w, "x1s", y, out)
        cp(b(f, 0, 4 * w), b(land, base, base + 4 * w))
        for h in range(2):
            tt(b(x, h, 3 * w, 3), b(f, h * w, h * w + w), b(f, 2 * w + h * w, 3 * w + h * w), A.add)
        scan(b("x1s", 0, 3 * w), b("x1d", 0, 3 * w), b(x, 0, 3 * w))
        cp(b(f, 4 * w, 7 * w), b(land, base + 4 * w, base + 7 * w))
        ops[-1]["ord"].append(len(ops) - 2)
        tt(b(y, 0, w), b(f, 4 * w, 5 * w), b(f, 6 * w, 7 * w), A.add)
        tt(b(y, w, 2 * w), b(f, 5 * w, 6 * w), b("x1s", 2, 3 * w, 3), A.add)
        compare(out, (y, 0), w)

    dma("Y", [(T.pas[:, :], T.pa[:, :])], [], [b("pas")], 2.0)
    after["Y"] = last("Y")
    dma("S", [(T["xs_"][:, :], T.xv[:, :])], [], [b("xs_")], KNOB["loads"][0])
    dma("S", [(T.pin[:, :], T.pa[16 * me:16 * me + 16, :])], [], [b("pin")], 2.0)
    dma("Y", [(T.cds[:, :], T.cd[:, :])], [], [b("cds")], KNOB["loads"][1])
    after["Y"] = last("Y")
    dma("Y", [(T.kcs[:, :], T.kc[:, :])], [], [b("kcs")], KNOB["loads"][2])
    after["Y"] = last("Y")
    iota(b("ci", 0, 1), [[0, 1]], 0, 1)
    fill(b("xm", 0, NV), 0.0)
    lin(b("xm", NV, 2 * NV), b("xs_"), 0.0)

    def lane_features(t, lat, behind=()):
        dma("Y", [(T.xm[16 * r:16 * r + 16, 256 * ((r - me - 1) % n):256 * ((r - me - 1) % n) + NL],
                   T.xv[16 * r:16 * r + 16, NL * t:NL * t + NL]) for r in range(n)], list(behind), [b("xm")], lat)
    for c in range(0, TBV, 384):
        fill(b("tb", c, c + 384), FAR)
    iota(b("iv"), [[1, 144]], 0, 0)
    iota(b("rb"), [[0, 8], [1, 16]], 0, 0)
    iota(b("tm"), [[1, 16], [128, 8]], 0, 0)
    iota(b("tb", TBV, NC), [[0, NC - TBV]], FAR, 0)
    ops[-1]["ord"] += [k for k in range(len(ops) - 1) if ops[k]["eng"] == "G"]
    rows = [(T.tb[8 * i + 4:8 * i + 5, :], (T.bt, T.co)[i % 2][me:me + 1, :]) for i in range(16)]
    rows += [(T.tb[0:128:16, :], T.bt[:, :]), (T.tb[1:128:16, :], T.co[:, :])]
    dma("Y", rows, [], [b("tb")], KNOB["loads"][3])
    after.pop("Y")
    for c in range(0, 1152, 288):
        lin(b("kt", c, c + 288), b("xs_", 0, 288))

    def cg(i):
        return b("cg", i, i + 1)
    p_ = b("ci", 0, 1)
    ts(b("ci", 1, 2), p_, 15, A.bitwise_and)
    ts(b("ci", 2, 3), p_, 4, A.arith_shift_right)
    ts(b("ci", 3, 4), p_, 7, A.bitwise_and)
    ts(b("ci", 4, 5), p_, 4, A.arith_shift_right, 1, A.bitwise_and)
    ts(b("ci", 5, 6), p_, 3, A.arith_shift_right, 1, A.bitwise_and)
    ts(b("ci", 6, 7), p_, 1, A.bitwise_and)
    ts(b("ci", 7, 8), p_, 1, A.arith_shift_right, 7, A.bitwise_and)
    ts(b("ci", 8, 9), p_, 3, A.arith_shift_right)
    ts(b("ci", 9, 10), p_, 3, A.bitwise_and)
    cp(b("cf", 0, 10), b("ci", 0, 10))
    cP, cB, cG, cP7, cA, cB3, cB0, cB1, cP3, cR3 = [b("cf", i, i + 1) for i in range(10)]
    iota(b("jt"), [[128, 8]], 0, 1)
    iota(b("mx"), [[1, 16], [0, 8]], 0, 0)
    i2, i4, i8, i128, rb128 = b("iv", 0, 2), b("iv", 0, 4), b("iv", 0, 8), b("iv", 0, 128), b("rb")
    xoA, xoB, lpm, lpq, lx = b("lst", 0, 8), b("lst", 8, 16), b("lst", 16, 18), b("lst", 18, 20), b("lst", 24, 32)
    l8, gl2, lpi = b("lst", 32, 40), b("lst", 40, 48), b("lst", 48, 56)
    lso, lpa, ldup, lpo = b("lst", 64, 68), b("lst", 68, 72), b("lst", 76, 80), b("lst", 80, 81)
    lin(cg(0), cB, 8.0, cG)
    lin(cg(1), cB0, 8.0, cG)
    ts(cg(4), cG, float(me) + 0.5, A.is_lt, 8.0, A.mult)
    ts(cg(14), cG, cg(4), A.add, -me - 0.5, A.add)
    lin(cg(2), cg(14), 256.0)
    ts(b("lnl"), i8, 16.0, A.mult, cB, A.add)
    ts(xoB, b("lnl"), cg(2), A.add)
    ts(xoA, b("lnl"), cg(2), A.add, -128.0, A.add)
    l1, l2 = b("lst", 20, 21), b("lst", 22, 24)
    cp(l1, cP)
    ts(l2, i2, 0.0, A.mult, cg(0), A.add)
    lin(cg(25), cP, 1.0, float(-16 * me))
    ts(b("rep"), rb128, cg(25), A.is_equal)
    ts(b("zo"), i4, cg(25), A.is_equal)
    add("V", lambda: g.vector.memset(ap(b("pg", 64, 128)), 0.0), [], [b("pg", 64, 128)], 64 * CYC)
    ts(b("la", 0, 8), i8, float(me), A.is_equal, float(39 - me), A.mult)
    tt(b("la", 0, 8), b("la", 0, 8), i8, A.add)
    cp(gl2, b("la", 0, 8))
    cp(l8, i8)
    ts(cg(10), cP7, cG, A.is_equal)
    ts(b("la", 8, 12), i4, 2.0, A.mult, cB3, A.add)
    lin(b("lf", 80, 84), b("la", 8, 12), 3.0, -22.0)
    ts(lso, b("lf", 80, 84), cg(10), A.mult, 24.0, A.add)
    lin(cg(12), cP7, 1.0, -8.0)
    ts(b("lf", 88, 92), b("la", 8, 12), cG, A.is_equal, cg(12), A.mult)
    ts(lpa, b("lf", 88, 92), 8.0, A.add)
    ts(b("la", 12, 14), i2, cA, A.not_equal, 16.0, A.mult)
    for h in range(2):
        ts(b("lst", 76 + 2 * h, 78 + 2 * h), b("la", 12, 14), cB, A.add)
    ts(lx, i8, 0.0, A.mult, cP7, A.add)
    lin(cg(5), cP7, 16.0, cB3)
    ts(lpi, i8, 2.0, A.mult, cg(5), A.add)
    ts(lpo, cP7, 8.0, A.mult, cG, A.add)
    ts(b("m1"), rb128, cg(1), A.is_equal)
    ts(b("r1", 8, 16), i8, cB1, A.is_equal, 2048.0, A.mult)
    ts(b("r1", 0, 8), i8, cB1, A.is_equal, -0.25, A.mult)
    ts(b("m2"), rb128, cB, A.is_equal)
    ts(b("m2h"), rb128, cB, A.is_equal)
    ts(b("m4"), rb128, cP3, A.is_equal)
    ts(b("bi"), i8, cG, A.is_equal)
    ts(b("b7"), i8, cP7, A.is_equal)
    ts(b("idh"), i128, cP, A.is_equal)
    fill(b("one"), 1.0)
    ts(b("bigu"), i128, cg(0), A.is_ge, BIG, A.mult)
    lin(cg(8), cG, 9.0, 8.0)
    ts(b("z9"), b("iv", 0, 80), cg(8), A.is_equal)
    lin(cg(13), cB, 16.0, cG)
    ts(b("zi"), b("iv", 0, 136), -8.0, A.add, cg(13), A.is_equal)
    ts(b("mz"), b("iv", 0, 48), -16.0, A.add, cB, A.is_equal)
    ts(b("mx"), b("mx"), cB, A.is_equal)
    lin(cg(15), cB, 8.0, float(NR - 1))
    ts(b("lt"), b("iv", 0, 136), cg(15), A.is_equal)
    lin(cg(16), cP7, 16.0, cP3)
    ts(b("pmt"), i128, cg(16), A.is_equal)
    lin(cg(9), cG, 2.0, -15.0)
    lin(cg(17), cB, 4.0, cg(9))
    ts(cg(18), cP7, 4.0, A.is_equal)
    ts(b("z2", 0, 65), b("iv", 0, 65), cg(17), A.is_equal, cg(18), A.mult)
    lin(b("e2", 0, 49), b("z2", 0, 49))
    tt(b("z2", 16, 65), b("z2", 16, 65), b("e2", 0, 49), A.add)
    lin(cg(3), cA, 16.0, 15.0)
    ts(cg(19), cg(3), cB1, A.subtract)
    ts(lpq, i2, -8.0, A.mult, cg(19), A.add)
    lin(cg(20), cB0, -32.0, 32.0)
    ts(cg(21), cg(20), cg(19), A.add)
    ts(lpm, i2, -8.0, A.mult, cg(21), A.add)
    lin(cg(22), cg(0), -64.0, 2032.0 * 4)
    ts(b("qc"), b("iv", 0, 32), 2.0, A.mult, cg(22), A.add)
    lin(cg(23), cg(0), -4.0, -4096.0)
    ts(b("wb", 0, 4), i4, cR3, A.is_equal)
    ts(b("ws", 0, 1), cR3, 1.5, A.is_lt, float(FAR), A.mult)
    ts(b("ws", 1, 2), b("ws", 0, 1), b("wb", 2, 3), A.add)
    ts(cg(24), b("wb", 2, 3), 4.0, A.mult, b("wb", 1, 2), A.subtract)
    ts(b("ws", 2, 3), b("wb", 0, 1), float(FAR), A.mult, cg(24), A.add)
    ts(b("wb", 8, 12), i4, b("wb", 2, 3), A.mult, 8.0, A.mult)
    for t in range(NR):
        ts(b("lrow", NL * t, NL * t + NL), i128, float(NL * t), A.add, b("wb", 3, 4), A.mult)
    for h in range(3):
        fill(b("x1d", h, 96, 3), (0.0, -1.0, 1.0)[h])
    fill(b("t64", 64, 72), 0.5)
    fill(b("td", 16, 32), 0.0)
    fill(b("kg", 2048, 2064), 0.0)
    for name in ("ito", "it"):
        for c in range(0, 1152, 288):
            iota(b(name, c, c + 288), [[0, 288]], -1, 0)
    for name in ("ld2", "d0", "w3", "x9", "sdo", "paf", "pw", "po"):
        fill(b(name), 0.0)
    cp(b("so", 0, 8), b("pas", 0, 8))
    cp(b("tg", 0, 8), b("pas", 0, 8))
    cp(b("pl0"), b("pas"))
    xv, kc = b("xs_"), b("kcs")
    for c in range(0, NV, 256):
        lin(b("px%d" % (c // 512), c % 512, c % 512 + 256), b("xs_", c, c + 256))

    def own_parents(t):
        if t == NR - 1:
            mm([(b("pe", 128, 136), b("pmt"), b("ph", 0, 8), True, True)])
            cp(b("sw", 24, 32), b("pe", 128, 136))
        tt(b("ox"), ind(b("pw"), l8), b("m4"), A.mult)
        mm([(b("pe", 136, 144), b("ox"), b("b7"), True, True)])
        lin(b("po", 0, 8), b("pe", 136, 144))

    def swap_tables(t, scol):
        cp(b("si", 0, 1), scol)
        ts(b("si", 1, 2), b("si", 0, 1), 128 * 7 + 15, A.bitwise_and)
        ts(b("si", 2, 3), b("si", 0, 1), 16 * 7, A.bitwise_and)
        cp(b("sc", 8, 10), b("si", 1, 3))
        ts(b("ohm", 128 * t, 128 * t + 128), b("tm"), b("sc", 8, 9), A.is_equal)
        ts(b("ohu", 8 * t, 8 * t + 8), b("iv", 0, 128, 16), b("sc", 9, 10), A.is_equal)
        mm([(b("pb", 128, 256), b("ohm", 128 * t, 128 * t + 128), b("idh"), True, True)])
        lin(b("oht"), b("pb", 128, 256))
        aff("rhc", b("rhc", 24 * t, 24 * t + 8), b("ohu", 8 * t, 8 * t + 8), -2048.0)
        aff("rhc", b("rhc", 24 * t + 8, 24 * t + 16), b("ohu", 8 * t, 8 * t + 8), b("jt", t, t + 1))

    def grandparents(t, scol):
        mm([(b("pg", 448, 456), b("oht"), b("ph", 0, 8), True, True)])
        tt(b("ux"), b("pg", 448, 456), b("ohu", 8 * t, 8 * t + 8), A.mult)
        red(b("up", 0, 1), b("ux"), A.add)
        cp(b("pu", 32 + 8 * t, 33 + 8 * t), b("up", 0, 1))
        to_lists(b("pu", 32 + 8 * t, 33 + 8 * t), "dg%d" % t, T.gpl, [b("gpl")], HOPD)
        aff("up", b("up", 1, 2), scol, -1.0, b("up", 0, 1))
        aff("up", b("rhc", 24 * t + 16, 24 * t + 24), b("bi"), b("up", 1, 2))

    def decode(bank, c0, li, tg, cut, state, tgt):
        tt(b(tg, 8, 16), b(bank, c0, c0 + 8), b(tg, 0, 8), A.max)
        cp(b(li, 0, 8), b(bank, c0 + 8, c0 + 16))
        cp(tgt, b(tg, 8, 16))
        ts(b(li, 8, 16), b(li, 0, 8), 4095, A.bitwise_and)
        ts(b(li, 16, 24), b(li, 0, 8), 12, A.arith_shift_right, 2 ** 19 + 1, A.bitwise_and)
        cp(cut, b(li, 8, 16))
        ts(state, b(li, 16, 24), 2.0, A.min)
    fill(b("ph", 8, 16), 0.0)
    cp(b("ph", 0, 8), b("pin"))
    cp(b("pw", 0, 8), b("pin"))
    own_parents(0)
    swap_tables(0, b("po", 0, 1))
    grandparents(0, b("po", 0, 1))
    opening = last("G")
    ops[opening]["plus"] = FIRST + KNOB["open"]
    ops[opening]["cost"] += ops[opening]["plus"]

    nb = 128 // BLK
    cp(ind(b("xm"), xoA), b("xs_", 0, NL))
    for t in range(NR):
        so = b("so", 8 * t, 8 * t + 8)
        scol = b("po", 0, 1) if t == 0 else b("w3", 3 * me + 2, 3 * me + 3)
        cp(b("cut"), ind(b("cds"), so))
        lin(b("xg"), ind(xv, so))
        cp(ind(b("xm"), xoB), b("xg"))
        c0 = 0
        for (e, w) in PIECES[min(t, 1)]:
            (lin if e == "S" else cp)(b("kg", c0, c0 + w), ind(kc, b("cut", c0 // 16, (c0 + w) // 16)))
            its = []
            for m in range(c0 // BLK, (c0 + w) // BLK):
                q, blk = m // nb, m % nb
                its.append((b("pa0", q, 256, 16, blk * BLK, blk * BLK + BLK), b("kg", m * BLK, m * BLK + BLK),
                            b("xm", 2 * m + 1, 2048, 128), True, True))
                its.append((b("pa0", q, 256, 16, blk * BLK, blk * BLK + 16), b("kg", m * BLK, m * BLK + 16),
                            b("xm", 2 * m, 2048, 128), True, True))
            mm(its)
            c0 += w
        B1 = 256 * t
        if t > 0 and KNOB["late"] == 1:
            ops[late]["ord"].append(last("V"))
        for h in range(2):
            ts(b("sb1", B1 + 128 * h, B1 + 128 * h + 128), b("pa0", 128 * h, 128 * h + 128), sgn, A.mult, OFF, A.add)
        if t > 0 and KNOB["late"] == 2:
            ops[late]["ord"].append(last("V"))
        spread(lambda i: b("sb1", B1 + 32 * i, B1 + 32 * i + 32), ("ld1", B1), 32, True, [b("ld2")] if t == 0 else [])
        if t == 0:
            ops[last("G") - 1]["ord"].append(opening)
        if t < NR - 1:
            lane_features(t + 1, 2.0, [b("ld1", B1, B1 + 224)])

        cp(b("cs"), b("cut"))
        mm([(b("pb", 384, 512), b("rep"), b("cs"), True, True)])
        lin(b("ec"), b("pb", 384, 512))
        cp(b("goff"), ind(b("ec"), l1))
        cp(b("gg"), ind(b("tb"), b("goff")))
        mm([(b("pb", 0, 64), b("gg", 128 * h, 128 * h + 128), b("z2", 1 - h, 65 - h), h == 0, h == 1) for h in range(2)])
        own_slot(b("x1", 2, 96, 3), b("sb1", B1 + 224, B1 + 256), b("pb", 0, 32))
        aff("cc", b("cc", 0, 32), b("pb", 32, 64), -1.0, TOP)
        aff("cc", b("cc", 32, 64), b("pb", 32, 64), 1.0, -TOP)
        aff("sh", b("sh", 1, 2), scol)
        ts(b("sh", 2, 3), scol, NL * t - 0.5, A.is_lt, 32768.0, A.mult)
        ts(b("sh", 3, 4), scol, NL * t + NL - 0.5, A.is_gt, 32768.0, A.mult)
        aff("dg", b("dg"), b("idh"), scol)
        mm([(b("pc_", 128, 256), b("one"), b("dg"), True, False), (b("pc_", 128, 256), b("idh"), b("bigu"), False, True),
            (b("pc_", 257, 259), b("pmt"), b("sh", 1, 3), True, False), (b("pc_", 258, 259), b("pmt"), b("sh", 3, 4), False, True)])
        if "first" in ON_SCALAR:
            lin(b("sc", 0, 1), b("pc_", 257, 258))
            lin(b("e2"), b("pc_", 128, 256), -1.0, b("sc", 0, 1), AF.Sign)
            lin(b("e3"), b("e2"), 1.0, 0.0, AF.Square, b("sc", 1, 2))
            ts(b("sc", 4, 5), b("sc", 1, 2), 127.5, A.is_gt, b("pc_", 258, 259), A.mult)
        else:
            ts(b("e2"), b("pc_", 128, 256), b("pc_", 257, 258), A.subtract)
            red(b("sc", 1, 2), b("e2"), A.min, True)
            ts(b("sc", 4, 5), b("sc", 1, 2), 0.5, A.is_gt, b("pc_", 258, 259), A.mult)
        lin(b("cq"), ind(b("ec"), l2), 1.0 / 2048)
        turn(b("ct"), b("cq"))
        tt(b("qq"), ind(b("ct"), lpq), b("qc"), A.add)

        k1 = len(ops)
        two_step_sum("f1", "ld1", B1, 32, "x1", "y1", b("sd"))
        if t > 0 and KNOB["listed"]:
            ops[k1 + KNOB["listed"] - 1]["ord"].append(listed)
        tt(b("td", 0, 16), b("sd", 0, 16), b("sd", 16, 32), A.subtract)
        tt(b("v64"), ind(b("td"), ldup), b("cc"), A.mult)
        turn(b("t64", 0, 64), b("v64"))
        red(b("sc", 6, 7), b("t64", 0, 65), A.max)
        ts(b("dd"), ind(b("t64", 0, 64), lpm), b("sc", 6, 7), A.is_equal, b("sc", 4, 5), A.mult)
        B2 = 48 * t
        own = B2 + 39
        scan(b("ld2", B2 + 8, B2 + 40), b("dd"), b("qq"), cg(23), A.add, A.min)
        to_all(T.ld2[:, own:own + 1], [T.ld2[:, B2 + me:B2 + me + 1] for r in peers], [b("ld2", own, own + 1)], [b("ld2", B2, B2 + 8)],
               HOP + 0.15)
        win = b("ld2", B2, B2 + 48)
        mark = b("wb", 8 + t, 9 + t)

        mm([(b("pf_", 0, 16), b("idh"), b("ph"), True, False)])

        def vertex_tables():
            lin(b("eo"), b("pg", 64, 128))
            aff("sdo", b("sdo", 0, 9), b("pg", 96, 105) if "sdo" in ON_SCALAR else b("eo", 32, 41), 1.0, -8.0 * t)
            tt(b("sdo", 16, 24), b("eo", 48, 56), b("po", 0, 8), A.subtract)
            ts(b("sdo", 16 + t, 17 + t), b("eo", 48 + t, 49 + t), b("jt", t, t + 1), A.not_equal, b("sdo", 16 + t, 17 + t), A.mult)
        if t == NR - 1:
            aff("dh", b("dh"), b("m2h"), scol)
            mm([(b("pb", 80, 88), b("dh"), b("bi"), True, True)])
            lin(b("tgo", 0, 8), b("pb", 80, 88))
            aff("gmo", b("gmo"), b("m1"), b("ld2", own, own + 1))
            mm([(b("pb", 64, 80), b("gmo"), b("r1"), True, True)])
            decode("pb", 64, "lio", "tgo", b("sw", 8, 16), b("sw", 0, 8), b("sw", 16, 24))
            lin(b("wvo"), ind(b("ws"), b("sw", 0, 8)), 1.0, mark)
            tt(b("sro"), ind(b("tb"), b("sw", 8, 16)), b("wvo"), A.min)
            tt(ind(b("ito"), b("sw", 16, 24)), b("sro"), b("lrow", NL * t, NL * t + NL), A.add)
            lin(b("iao", 0, 128), ind(b("ito"), b("sw", 24, 32)))
            mm([(b("pg", 64, 128), b("iao", 0, 128), b("zi", 72, 136), True, False), (b("pg", 64, 128), b("sro"), b("zi", 64, 128), False, True)])
            vertex_tables()

        pl = "pl%d" % t
        lin(b("xps"), ind(xv, b("gpl")))
        if t < NR - 1:
            pn = b(pl, 8 * t + 8, 8 * t + 16)
            nx = NL * (t + 1)
            pc = b("pc", 0, 8)
            lin(b("xpn"), ind(xv, pn))
            lin(b("pe", 256, 384), b("xpn"))
            cp(b("paf", 0, 8), pn)
            lin(b("pz"), ind(b("paf"), lpa))
            mm([(b("pe", 64, 128), b("m2"), b("pz"), True, True)])
            lin(b("py"), b("pe", 64, 128))
            lin(b("pc"), ind(b("py"), lpo))

        tt(b("gm"), ind(win, gl2), b("m1"), A.mult)
        mm([(b("pa0", 256, 272), b("gm"), b("r1"), True, True)])
        ts(b("ck"), b("pa0", 256, 264), 2047.47, A.add, 2048.0, A.min)
        decode("pa0", 256, "li", "tg", b("cl", 0, 8), b("cl", 8, 16), b("tgt"))
        (cp if KNOB["kcc"] else lin)(b("kcc"), ind(b("kg"), b("ck")))
        if KNOB["kcc"]:
            for k in (-5, -4):
                ops[k]["ord"].append(len(ops) - 1)
        cp(ind(b("kt"), b("tgt")), b("kcc"))
        if t < NR - 1:
            B3 = 128 * t
            tt(b("pf", 128, 256), b("kt", nx, nx + NL), b("pe", 256, 384), A.mult)
            tt(b("pf", 0, 128), ind(b("kt"), pn), b("xs_", nx, nx + NL), A.mult)
            for w in (1, 0):
                mm([(b("pa0", 272 + 8 * w, 280 + 8 * w), b("pf", 128 * w, 128 * w + 128), b("bi"), True, True)])
            ts(b("sb3", 16 * t, 16 * t + 16), b("pa0", 272, 288), sgn, A.mult, OFF, A.add)
            for (i0, i1) in ((0, 4), (4, 7)) if "f3" in KNOB["two"] else ((0, 7),):
                to_all(T.sb3[:, 16 * t:16 * t + 16], [T.ld3[:, B3 + 16 * i:B3 + 16 * i + 16] for i in range(i0, i1)],
                       [b("sb3", 16 * t, 16 * t + 16)], [b("ld3", B3 + 16 * i0, B3 + 16 * i1)], HOP - 0.1 + 0.07 * i0 + 0.15 * (i1 - i0 - 4 + (i0 > 0)),
                       (16 * (i1 - i0), 32), peers[i0:i1])
                if i0:
                    ops[-2]["ord"].append(len(ops) - 4)
        B9 = 72 * t
        done = []
        skip = t + 1 if t < NR - 1 else 9
        w9 = 8 if t < NR - 1 else 9

        def sums(y):
            c = y - (y > skip)
            mm([(b("pc_", 0, 72), b("pr", 128 * y, 128 * y + 128), b("z9", 8 - c, 80 - c), not done, len(done) == w9 - 1)])
            done.append(y)

        def by_scalar(y0, y1):
            lin(b("kj", 128 * y0, 128 * y1), ind(b("kt"), b(pl, 8 * y0, 8 * y1)))
            tt(b("pr", 128 * y0, 128 * y1), b("kj", 128 * y0, 128 * y1), b("px%d" % (y0 // 4), 128 * (y0 % 4), 128 * (y0 % 4 + y1 - y0)), A.mult)
            for y in range(y0, y1):
                sums(y)

        def by_vector(y0, y1):
            tt(b("pr", 128 * y0, 128 * y1), ind(b("kt"), b(pl, 8 * y0, 8 * y1)), b("xs_", 128 * y0, 128 * y1), A.mult)
            for y in range(y0, y1):
                sums(y)
        tt(b("pr", 1024, 1152), ind(b("xps"), lpi), b("kcc"), A.mult)
        sums(8)
        for (e, y0, y1) in BLOCKS[t]:
            (by_vector if e == "V" else by_scalar)(y0, y1)
        ts(b("sb9", B9, B9 + 72), b("pc_", 0, 72), sgn, A.mult, OFF, A.add)
        summed = last("V")
        spread(lambda i: b("sb9", B9 + 9 * peers[i], B9 + 9 * peers[i] + w9), ("ld9", 64 * t), w9, t == NR - 1,
               via=b("sb9", B9, B9 + 72) if t < NR - 1 else None)

        lin(b("wv"), ind(b("ws"), b("cl", 8, 16)), 1.0, mark)
        tt(b("src"), ind(b("tb"), b("cl", 0, 8)), b("wv"), A.min)
        lin(b("ycr", 128 * t, 128 * t + 128), ind(b("src"), lpi))
        dma("Y", [(T.yc[:, 8 * t:8 * t + 8], T.ycr[1:128:16, 128 * t:128 * t + 128])], [b("ycr", 128 * t, 128 * t + 128)], [])
        if t < NR - 1:
            tt(ind(b("it"), b("tgt")), b("src"), b("lrow", NL * t, NL * t + NL), A.add)
            lin(b("ian"), ind(b("it"), pn))
            mm([(b("pg", 72, 128, 16), b("src"), b("zo"), True, True)])
            for (e, y0, y1) in BLOCKS[t]:
                lin(b("iao", 128 * y0, 128 * y1), ind(b("it"), b(pl, 8 * y0, 8 * y1)))
                for y in range(y0, y1):
                    mm([(b("pg", 64 + y, 128, 16), b("iao", 128 * y, 128 * y + 128), b("zo"), True, True)])
            vertex_tables()
            mm([(b("pe", 0, 64), b("it", nx, nx + NL), b("zi", 0, 64), True, False), (b("pe", 0, 64), b("ian"), b("zi", 8, 72), False, True)])
            own_slot(b("x3", 2, 48, 3), b("sb3", 16 * t, 16 * t + 16), b("pe", 0, 16))
            ts(b("sdf"), b("pe", 32, 48), -8.0 * t, A.add)
            cp(b("d1", 2, 24, 3), b("pe", 56, 64))
            tt(b("d1", 0, 24, 3), pc, b("pe", 48, 56), A.subtract)
            tt(b("d1", 1, 24, 3), b("pe", 48, 56), b("d1", 2, 24, 3), A.subtract)
            k1 = len(ops)
            two_step_sum("f3", "ld3", B3, 16, "x3", "y3", b("b3"))
            if KNOB["summed"]:
                ops[k1 + KNOB["summed"] - 1]["ord"].append(summed)
            for w in range(2):
                tt(b("d0", 1 + w, 24, 3), b("b3", 8 * w, 8 * w + 8), b("sdf", 8 * w, 8 * w + 8), A.not_equal)
            scan(b("w3", 0, 24), b("d0"), b("d1"))
            cp(b("ga"), ind(b("w3"), lso))
            mm([(b("pa0", 288, 296, 1, 32 * (gr // 2), 32 * (gr // 2) + 32), b("mz", 16 - 16 * (gr % 2), 48 - 16 * (gr % 2)),
                 b("ga", 8 * gr, 8 * gr + 8), gr % 2 == 0, gr % 2 == 1) for gr in range(8)])
            cp(b("so", 8 * t + 8, 8 * t + 16), b("pa0", 288, 296))
            aff("tg", b("tg", 0, 8), b("pa0", 288, 296))
            swap_tables(t + 1, b("w3", 3 * me + 2, 3 * me + 3))
            fill(b("x9", 48 + skip, 49 + skip), 1.0)
            tt(b("sdo", 16 + skip, 17 + skip), b("w3", 3 * me + 2, 3 * me + 3), b("po", skip, skip + 1), A.subtract)
        else:
            ts(b("sa", 0, 9), b("sdo", 0, 9), 0.0, A.is_equal)
            ts(b("sa", 16, 25), b("sdo", 0, 9), 1.0, A.is_equal)
            tt(b("sa", 16, 25), b("sa", 16, 25), b("sa", 0, 9), A.subtract)
            for h in range(2):
                tt(b("sa", 32 + 8 * h, 40 + 8 * h), b("sa", 16 * h, 16 * h + 8), b("sdo", 16, 24), A.mult)
            tt(b("ox"), ind(b("sa", 32, 40), lx), b("mx"), A.mult)
            tt(b("gd"), ind(b("sa", 40, 48), lx), b("mx"), A.mult)
            aff("rhc", b("rh0"), b("rhc", 24 * t, 24 * t + 24), b("sa", 8, 9))
            aff("rhc", b("rhc", 0, 24), b("rhc", 24 * t, 24 * t + 24), b("sa", 24, 25))
            mm([(b("pf_", 0, 8), b("ox"), b("bi"), False, False), (b("pf_", 0, 16), b("ohm", 128 * t, 128 * t + 128), b("rh0", 0, 16), False, False),
                (b("pf_", 0, 8), b("lt", 0, 128), b("rh0", 16, 24), False, False)])

        parts = [(0, skip, 0), (skip + 1, 9, 1)] if t < NR - 1 else [(0, 9, 0)]
        cp(b("f9", 7 * w9, 8 * w9) if t < NR - 1 else b("x9", 2, 27, 3), b("sb9", B9 + 9 * me, B9 + 9 * me + w9))
        for (c0, c1, d) in parts:
            o = b("f9", 7 * w9 + c0 - d, 7 * w9 + c1 - d) if t < NR - 1 else b("x9", 2, 27, 3)
            tt(o, o, b("eo", c0, c1), A.subtract if me % 2 == 0 else A.add)
        late = len(ops)
        if t < NR - 1:
            one_step_sum("f9", "ld9", 64 * t, w9, "x9", "w9", b("w9", 20, 20 + w9))
            for (c0, c1, d) in parts:
                tt(b("x9", 48 + c0, 48 + c1), b("w9", 20 + c0 - d, 20 + c1 - d), b("sdo", c0, c1), A.is_equal)
            ts(b("rh2"), b("rhc", 24 * t, 24 * t + 24), b("x9", 56, 57), A.mult)
            tt(b("gd", 0, 8), b("x9", 48, 56), b("sdo", 16, 24), A.mult)
            tt(b("g72"), ind(b("gd", 0, 8), lx), b("mx"), A.mult)
        else:
            two_step_sum("f9", "ld9", 64 * t, w9, "x9", "w9", b("x9", 48, 57))
            tt(b("g72"), ind(b("x9", 48, 64), lx), b("gd"), A.mult)
            ts(b("rh2"), b("rhc", 0, 24), b("x9", 56, 57), A.mult)
        ohm = b("ohm", 128 * t, 128 * t + 128)
        mm([(b("pf_", 0, 16), ohm, b("rh2", 0, 16), False, False), (b("pf_", 0, 8), b("lt", NR - 1 - t, NR + 127 - t), b("rh2", 16, 24), False, False)])
        mm([(b("pf_", 0, 8), b("g72"), b("bi"), False, True)])
        cp(b("sm"), b("pf_", 0, 16))
        dn = "dp%d" % (t + 1)
        lo = b("pw", 0, 8)
        if t < NR - 1:
            tt(b("ph", 0, 8), b("sm", 0, 8), b("sm", 8, 16), A.max)
        tt(lo, b("sm", 0, 8), b("sm", 8, 16), A.max)
        if t < NR - 1:
            cp(b("pu", 16 * t, 16 * t + 8), b("ph", 0, 8))
            listed = last("V")
            to_lists(b("pu", 16 * t, 16 * t + 8), dn, T["pl%d" % (t + 1)], [b("pl%d" % (t + 1))], HOPD + KNOB["list"])
            grandparents(t + 1, b("w3", 3 * me + 2, 3 * me + 3))
            own_parents(t + 1)
        else:
            to_lists(lo, dn, T.yp, [], HOPD, [b("sm", 0, 8), b("sm", 8, 16)])

    if core in aids:
        gone, h = 0, aids.index(core)
        for (sem, cnt, calls) in relays:
            if h < len(calls):
                g.wait_ge(sem, cnt)
                for tr in calls[h]:
                    g.remote_dma_fused(tr, local_sem=T.sem.sent)
                    gone += len(engs)
        g.wait_ge(T.sem.sent, gone)
        return
    shape = tuple((o["eng"], tuple(o["deps"]), tuple(o["ord"])) for o in ops)
    if shape not in LAID:
        LAID[shape] = plan(ops)
    order = LAID[shape]
    PLAN[me] = (ops, order)
    succ = [[] for _ in ops]
    for k, o in enumerate(ops):
        for j in o["deps"]:
            succ[j].append(k)
    queue = {"V": g.vector, "S": g.scalar, "P": g.tensor, "G": g, "Y": g.sync}
    count = {"V": 0, "S": 0, "P": 0, "G": 0}
    for k in order:
        o = ops[k]
        if o["kind"] == "c" and any(not (o["eng"] == "P" and ops[j]["eng"] == "P") for j in succ[k]):
            count[o["eng"]] += 1
            o["sem"] = (T.sem[o["eng"]], count[o["eng"]])
            o["key"] = o["eng"]
        elif o["kind"] in "da":
            o["key"] = k
    seen = {}
    for k in order:
        o = ops[k]
        e = o["eng"]
        if e == "X":
            continue
        need = {}
        for j in o["deps"]:
            d = ops[j]
            if d["kind"] == "r" or (e == "P" and d["eng"] == "P"):
                continue
            if d["sem"][1] > need.get(d["key"], (None, 0))[1]:
                need[d["key"]] = d["sem"]
        for key in need:
            if need[key][1] > seen.get((e, key), 0):
                queue[e].wait_ge(need[key][0], need[key][1])
                seen[(e, key)] = need[key][1]
        r = o["fn"]()
        if o["kind"] == "c" and "sem" in o:
            r.then_inc(o["sem"][0], 1)
    for e in count:
        if count[e] > max([seen.get((q, e), 0) for q in queue]):
            g.wait_ge(T.sem[e], count[e])
    g.wait_ge(T.sem.sent, sent[0])
    for k in order:
        o = ops[k]
        if o["kind"] in "da" and not any((q, k) in seen for q in queue):
            g.sync.wait_ge(o["sem"][0], o["sem"][1])


def plan(ops):
    m = len(ops)
    succ = [[] for _ in range(m)]
    behind = [[] for _ in range(m)]
    for k in range(m):
        for j in ops[k]["deps"]:
            succ[j].append(k)
        for j in ops[k]["ord"]:
            behind[j].append(k)

    def lag(j, k):
        return 0.0 if ops[j]["eng"] == "P" and ops[k]["eng"] == "P" else ops[j]["lat"]
    prio, rank, back = [0.0] * m, list(range(m)), []
    left = [len(succ[k]) + len(behind[k]) for k in range(m)]
    todo = [k for k in range(m) if left[k] == 0]
    while todo:
        k = todo.pop()
        back.append(k)
        for j in ops[k]["deps"] + ops[k]["ord"]:
            left[j] -= 1
            if left[j] == 0:
                todo.append(j)
    then = [[(j, lag(k, j) + ops[k]["cost"]) for j in succ[k]] + [(j, ops[k]["cost"]) for j in behind[k]] for k in range(m)]

    def weigh(urge):
        for k in back:
            p, q = ops[k]["lat"] + ops[k]["cost"], 0.0
            for (j, d) in then[k]:
                if prio[j] + d > p:
                    p = prio[j] + d
                if prio[j] > q:
                    q = prio[j]
            prio[k] = max(p + urge.get(k, 0.0), q) + 1e-6
        rank.sort(key=lambda k: (-prio[k], k))
    wait = [[(j, ops[j]["cost"] + lag(j, k)) for j in ops[k]["deps"]] + [(j, ops[j]["cost"]) for j in ops[k]["ord"]] for k in range(m)]

    def lay(more):
        busy = {e: [] for e in "VSPGY"}
        start = [0.0] * m
        for k in rank:
            s, c = 0.0, ops[k]["cost"]
            for (j, d) in wait[k]:
                if start[j] + d > s:
                    s = start[j] + d
            s += more.get(k, 0.0)
            if ops[k]["eng"] != "X":
                sl_ = busy[ops[k]["eng"]]
                lo, hi = 0, len(sl_)
                while lo < hi:
                    mid = (lo + hi) // 2
                    if sl_[mid][1] <= s:
                        lo = mid + 1
                    else:
                        hi = mid
                while lo < len(sl_) and s + c > sl_[lo][0]:
                    s = max(s, sl_[lo][1])
                    lo += 1
                sl_.insert(lo, (s, s + c))
            start[k] = s
        return start

    def laid(urge, more):
        weigh(urge)
        start = lay(more)
        return sorted(range(m), key=lambda k: (start[k], -prio[k], k))
    order = laid({}, {})

    cases = []
    for (fc, fw, row, fd, st) in KNOB["cases"]:
        cost = [(o["cost"] - o.get("plus", 0.0)) * (fc if o["kind"] == "c" else 1.0) for o in ops]
        lat = [o["lat"] * fw if o["kind"] == "c" else 0.2 * fw if o["kind"] == "a" else o["lat"] + fd for o in ops]
        rows = [o["rows"][0] * (row + o["rows"][1] / 12e3) if "rows" in o else None for o in ops]
        ons = {k: o["on"][1] * (row + o["on"][2] / 12e3) for k, o in enumerate(ops) if "on" in o}
        cases.append((cost, lat, rows, ons, CALL + st, [[(j, cost[j] + (0.0 if ops[j]["eng"] == "P" and o["eng"] == "P" else lat[j])) for j in o["deps"]
                                         if ops[j]["kind"] != "r"] for o in ops]))
    eng = [o["eng"] for o in ops]
    local = set(k for k in range(m) if ops[k]["kind"] == "d")

    def run(order, case):
        cost, lat, rows, ons, go, waits = case
        free, prev = {}, {}
        start, why, land = [0.0] * m, [None] * m, {}
        end, tail, wire, aid, used = 0.0, 0, -1.0, -1.0, 0.0
        for k in order:
            e = eng[k]
            s, w = 0.0, None
            if e == "X":
                s, w = land[ops[k]["by"]], (ops[k]["by"], False)
            elif e in free:
                s, w = free[e], (prev[e], True)
            for (j, d) in waits[k]:
                if start[j] + d > s:
                    s, w = start[j] + d, (j, False)
            if rows[k] is not None:
                t0 = s + go + (FIRST + 0.5 if wire < 0 else 0.0)
                if k in ons:
                    if wire < 0:
                        wire = t0 + rows[k]
                    land[k] = t0 + rows[k] + 0.2 + go + (FIRST if aid < 0 else 0.0)
                    aid = land[k] = max(land[k], aid) + ons[k]
                else:
                    used = max(t0, wire)
                    wire = land[k] = used + rows[k]
            start[k], why[k] = s, w
            if k in local and used < s + cost[k] + lat[k] - 0.8 < wire:
                free[e], prev[e] = s + cost[k], k
                start[k] = wire + 0.8 - cost[k] - lat[k]
                continue
            free[e], prev[e] = s + cost[k], k
            if s + cost[k] + lat[k] > end:
                end, tail = s + cost[k] + lat[k], k
        KNOB["start"] = start
        return end, why, tail
    base = [run(order, c)[0] for c in cases]

    def score(order):
        return sum(run(order, c)[0] / t0 for c, t0 in zip(cases, base))
    needs = [set(o["deps"]) | set(o["ord"]) for o in ops]
    urge, more, best = {}, {}, score(order)
    for _ in range(KNOB["sweeps"]):
        for k in range(m):
            if eng[k] == "X" or ops[k]["cost"] >= KNOB["long"]:
                for (d, step) in ((more, 0.3), (more, 1.0), (urge, 0.5), (urge, -0.5), (urge, 2.0), (more, -0.3)):
                    old = d.get(k, 0.0)
                    if d is urge or old + step >= 0:
                        d[k] = old + step
                        new = laid(urge, more)
                        sc = score(new)
                        if sc < best - 1e-4:
                            order, best = new, sc
                        else:
                            d[k] = old

    def moved(order, pos, a, c):
        i, j = pos[a], pos[c]
        go, stay = [a], []
        mark = {a}
        for k in order[i + 1:j + 1]:
            if needs[k] & mark:
                if k == c:
                    return None
                mark.add(k)
                go.append(k)
            else:
                stay.append(k)
        return order[:i] + stay + go + order[j + 1:]

    def ahead(order, pos, a, c):
        i, j = pos[a], pos[c]
        go, stay = [c], []
        want = set(needs[c])
        for k in order[j - 1:i - 1 if i else None:-1]:
            if k in want:
                if k == a:
                    return None
                want |= needs[k]
                go.append(k)
            else:
                stay.append(k)
        return order[:i] + go[::-1] + stay[::-1] + order[j + 1:]
    best = score(order)
    for _ in range(KNOB["passes"]):
        gain = False
        for case in cases:
            end, why, k = run(order, case)
            pairs = []
            while why[k] is not None:
                j, same = why[k]
                if same and j not in needs[k]:
                    pairs.append((j, k))
                k = j
            for (a, c) in pairs:
                pos = {k: i for i, k in enumerate(order)}
                if pos[a] > pos[c]:
                    continue
                tries = [moved(order, pos, a, k) for k in order[pos[c]:pos[c] + KNOB["reach"]] if eng[k] == eng[c]]
                before = [k for k in order[max(0, pos[c] - KNOB["reach"]):pos[c]] if eng[k] == eng[c]]
                tries += [ahead(order, pos, k, c) for k in before[-1::-2]]
                for new in tries:
                    if new is not None:
                        t0 = run(new, case)[0]
                        if t0 < end - 1e-6:
                            sc = score(new)
                            if sc < best - 1e-6:
                                order, best, gain, end = new, sc, True, t0
                                break
        if not gain:
            break
    KNOB["len"] = (max(prio), 0, base, [run(order, c)[0] for c in cases])
    return order


PLAN, LAID = {}, {}
